import numpy as np
import ml_dtypes


def mxq(x, axis, fmt="e4m3"):
    dtype, down = {"e4m3": (ml_dtypes.float8_e4m3fn, 7), "e5m2": (ml_dtypes.float8_e5m2, 14)}[fmt]
    v = np.moveaxis(np.asarray(x, np.float32).astype(ml_dtypes.bfloat16).astype(np.float64), axis, -1)
    blocks = v.reshape(v.shape[:-1] + (-1, 32))
    amax = np.abs(blocks).max(-1, keepdims=True)
    byte = np.maximum(np.where(amax > 0, np.frexp(amax)[1] - 1 + 127, 0) - down, 1)
    scale = np.exp2(byte - 127.0)
    codes = (blocks / scale).astype(np.float32).astype(dtype).astype(np.float64)
    return np.moveaxis((codes * scale).reshape(v.shape), -1, axis)


WIDE = False


def mx_kscale(k):
    if not WIDE:
        return np.ones(k)
    levels = np.array([10, -10, 5, -5, 0])
    if k % 512:
        return np.exp2(np.random.permutation(np.resize(levels, k // 32))).repeat(32)
    a = np.empty((k // 512, 16))
    for p in range(k // 512):
        a[p, :8] = np.random.permutation(np.resize(levels, 8))
        for g in range(8):
            far = levels[np.abs(levels - a[p, g]) >= 10]
            a[p, g + 8] = far[np.random.randint(len(far))]
    return np.exp2(a.ravel()).repeat(32)


def f64(x):
    return np.asarray(x).astype(np.float64)


def striped(idx):
    return np.tile(idx.reshape(-1, 16).T, (8, 1)).astype(np.uint16)


def unstriped(offs):
    return offs[:16].T.reshape(-1).astype(np.int64)


E2M1 = np.array([0.0, 0.5, 1.0, 1.5, 2.0, 3.0, 4.0, 6.0, -0.0, -0.5, -1.0, -1.5, -2.0, -3.0, -4.0, -6.0])


def pack_weight(w, fmt):
    k, n = w.shape
    w = f64(np.asarray(w, np.float32).astype(ml_dtypes.bfloat16)).reshape(k // 32, 32, n)
    amax = np.abs(w).max(1)
    if fmt == "e4m3":
        byte = np.frexp(amax)[1] - 1 + 127 - 7
    else:
        mant, ex = np.frexp(amax / 6.0)
        byte = np.where(mant > 0.5, ex, ex - 1) + 127
    byte = np.clip(np.where(amax > 0, byte, 1), 1, 254)
    scaled = (w * np.exp2(127.0 - byte)[:, None, :]).reshape(k, n).astype(np.float32)
    by_word = np.ascontiguousarray(scaled.reshape(k // 512, 128, 4, n).transpose(0, 1, 3, 2))
    if fmt == "e4m3":
        words = by_word.astype(ml_dtypes.float8_e4m3fn).view(np.uint8)
    else:
        c = by_word.astype(ml_dtypes.float4_e2m1fn).view(np.uint8) & 0xF
        words = (c[..., 0::2] | (c[..., 1::2] << 4)).reshape(k // 512, 128, 2 * n)
    return np.ascontiguousarray(words), np.ascontiguousarray(byte.astype(np.uint8).reshape(k // 512, 16, n))


def unpack_weight(words, scales, fmt):
    g, _, n = scales.shape
    words = np.ascontiguousarray(words).reshape(g, 128, n, -1)
    if fmt == "e4m3":
        vals = words.view(ml_dtypes.float8_e4m3fn).astype(np.float64)
    else:
        nib = np.empty((g, 128, n, 4), np.uint8)
        nib[..., 0::2] = words & 0xF
        nib[..., 1::2] = words >> 4
        vals = E2M1[nib]
    vals = vals * np.repeat(np.exp2(scales.astype(np.float64) - 127.0), 8, axis=1)[..., None]
    return vals.transpose(0, 1, 3, 2).reshape(g * 512, n)


def relu2(v):
    return np.maximum(v, 0.0) ** 2


K, T, E, C, N = 1024, 1536, 8, 128, 512


def by_expert(wq, xq):
    return np.concatenate([wq[e].T @ xq[:, e * C:(e + 1) * C] for e in range(E)], axis=1)


def setup_inputs():
    n = np.random.standard_normal
    s = mx_kscale(K)[:, None]
    w = [pack_weight(m, "e2m1") for m in n((E, K, N)) / np.sqrt(K) / s[None]]
    return {
        "xT": (n((K, T)) * s).astype(np.float32),
        "w_words": np.stack([m[0] for m in w]),
        "w_scales": np.stack([m[1] for m in w]),
        "b": (0.3 * n((N, E))).astype(np.float32),
        "gate": np.tile(np.random.uniform(0.2, 1.0, E * C), (N, 1)).astype(np.float32),
        "offs": striped(np.random.permutation(T)[:E * C]),
        "dst": striped(np.random.permutation(T)[:E * C]),
    }


def reference(xT, w_words, w_scales, b, gate, offs, dst):
    idx = unstriped(offs)
    w = np.stack([unpack_weight(w_words[e], w_scales[e], "e2m1") for e in range(E)])
    xq = mxq(f64(xT)[:, idx], 0, "e4m3")
    y = by_expert(w, xq)
    y = relu2(y + np.repeat(f64(b), C, axis=1))
    out = np.zeros((N, T))
    out[:, unstriped(dst)] = f64(gate) * y
    return out

@@ -1,0 +1,179 @@
+from contextlib import ExitStack
+
+import concourse.mybir as mybir
+
+K, T, E, C, N = 1024, 1536, 8, 128, 512
+S = E * C
+P = 128
+PACK = 4
+PASSES = K // (P * PACK)
+N_TILES = N // P
+CHUNKS = (((0, 768), (768, 1280), (1280, 1536)), ((0, 512), (512, 1024), (1024, 1280), (1280, 1536)))
+
+FLOPS = 2 * K * S * N
+BYTES = 4 * K * T + E * PASSES * (P * 2 * N + 16 * N) + 4 * N * E + 4 * S + 2 * 2 * P * (S // 16) + 4 * N * T
+
+F32 = mybir.dt.float32
+BF16 = mybir.dt.bfloat16
+I32 = mybir.dt.int32
+U32 = mybir.dt.uint32
+U16 = mybir.dt.uint16
+U8 = mybir.dt.uint8
+E4M3X4 = mybir.dt.float8_e4m3fn_x4
+E2M1X4 = mybir.dt.float4_e2m1fn_x4
+ACT = mybir.ActivationFunctionType
+MULT = mybir.AluOpType.mult
+
+SCALAR_COLS = ((352, 256, 96), (512, 512, 256, 96))
+HALF = 4 * C
+
+
+def tile_moe_two_lin_relu2_kernel(tc, xT, w_words, w_scales, b, gate, offs, dst, out):
+    nc = tc.nc
+    with ExitStack() as ctx:
+        keep = ctx.enter_context(tc.tile_pool(name="keep", bufs=1))
+        work = ctx.enter_context(tc.tile_pool(name="work", bufs=4))
+        psum = ctx.enter_context(tc.psum_pool(name="psum", bufs=8))
+
+        offs_sb = keep.tile([P, S // 16], U16, name="offs_sb")
+        dst_sb = keep.tile([P, S // 16], U16, name="dst_sb")
+        b_sb = keep.tile([P, N_TILES, E], F32, name="b_sb")
+        gate_sb = keep.tile([P, S], F32, name="gate_sb")
+        w_sb = [keep.tile([P, 2 * PASSES, 2 * N], U8, name=f"w_sb{g}", align_bytes=64) for g in range(E // 2)]
+        ws_sb = keep.tile([P, E * PASSES, N], U8, name="ws_sb", align_bytes=64)
+        codes = [keep.tile([P, T], U32, name=f"codes{a}", tag=f"codes{a}", align_bytes=64) for a in range(PASSES)]
+        bytes_ = [keep.tile([P, T], U8, name=f"scale_bytes{a}", tag=f"scale_bytes{a}", align_bytes=64) for a in range(PASSES)]
+        outs = [keep.tile([P, T], F32, name=f"out_sb{t}") for t in range(2)]
+
+        raw = {}
+        for a in range(PASSES):
+            rows = xT[a * 512 : (a + 1) * 512, :].rearrange("(p d) t -> p d t", d=PACK)
+            for c, (t0, t1) in enumerate(CHUNKS[a]):
+                r = keep.tile([P, PACK, t1 - t0], F32, name=f"raw{a}_{c}")
+                nc.sync.dma_start(out=r[:], in_=rows[:, :, t0:t1])
+                raw[a, c] = r
+                if (a, c) == (0, 1):
+                    nc.sync.dma_start(offs_sb[:], offs)
+
+        nc.gpsimd.memset(bytes_[0][:].bitcast(I32), 0)
+        nc.vector.memset(outs[0][:], 0.0)
+        nc.vector.memset(outs[1][:], 0.0)
+        nc.gpsimd.memset(bytes_[1][:].bitcast(I32), 0)
+        nc.gpsimd.memset(ws_sb[:].rearrange("p g n -> p (g n)").bitcast(I32), 0)
+        warm = keep.tile([P, 1], F32, name="warm")
+        nc.gpsimd.memset(warm[:], 0.0)
+        nc.scalar.activation(warm[:], warm[:], ACT.Square)
+
+        def load_w(g):
+            nc.sync.dma_start(
+                out=w_sb[g][:].bitcast(I32), in_=w_words[2 * g : 2 * g + 2].rearrange("e a p c -> p (e a) c").bitcast(I32)
+            )
+
+        def load_ws(e0, e1):
+            for r in range(4):
+                nc.sync.dma_start(
+                    out=ws_sb[r : P : 32, 2 * e0 : 2 * e1, :].bitcast(I32),
+                    in_=w_scales[e0:e1, :, r : 16 : 4, :].rearrange("e a q n -> q (e a) n").bitcast(I32),
+                )
+
+        load_ws(0, 4)
+        load_w(0)
+        nc.sync.dma_start(out=b_sb[:], in_=b.rearrange("(t p) e -> p t e", p=P))
+        nc.sync.dma_start(dst_sb[:], dst)
+        nc.sync.dma_start(gate_sb[:, 0:HALF], gate[0:P, 0:HALF])
+        load_w(1)
+        load_ws(4, 8)
+        load_w(2)
+        load_w(3)
+        nc.sync.dma_start(gate_sb[:, HALF:S], gate[0:P, HALF:S])
+
+        def prepare(a, c):
+            t0, t1 = CHUNKS[a][c]
+            width = t1 - t0
+            split = SCALAR_COLS[a][c]
+            g = work.tile([P, width, PACK], BF16, name="grouped", align_bytes=64)
+            src = raw[a, c]
+
+            def four(lo, hi):
+                return (
+                    g[:, lo:hi, :].rearrange("p (c i) d -> p c d i", i=4),
+                    src[:, :, lo:hi].rearrange("p d (c i) -> p c d i", i=4),
+                )
+
+            if split:
+                nc.scalar.copy(*four(0, split))
+            if split < width:
+                nc.vector.tensor_copy(*four(split, width))
+            for lo in range(0, width, 512):
+                hi = min(lo + 512, width)
+                cols = slice(t0 + lo, t0 + hi)
+                nc.vector.quantize_mx(
+                    out=codes[a][:, cols].bitcast(E4M3X4),
+                    scales=bytes_[a][:, cols],
+                    in_=g[:, lo:hi, :].rearrange("p t d -> p (t d)"),
+                )
+
+        for c in range(3):
+            prepare(0, c)
+        gw0 = keep.tile([P, S], U32, name="gw0", align_bytes=64)
+        gs0 = keep.tile([P, S], U8, name="gs0", align_bytes=64)
+        nc.vector.tensor_copy(gw0[:], codes[0][:].indirect(offs_sb[:]))
+        nc.vector.tensor_copy(gs0[:], bytes_[0][:].indirect(offs_sb[:]))
+        for c in range(4):
+            prepare(1, c)
+
+        gw1 = keep.tile([P, S], U32, name="gw1", align_bytes=64)
+        gs1 = keep.tile([P, S], U8, name="gs1", align_bytes=64)
+        for s0, s1 in ((0, 512), (512, 1024)):
+            cols = offs_sb[:, s0 // 16 : s1 // 16]
+            nc.vector.tensor_copy(gw1[:, s0:s1], codes[1][:].indirect(cols))
+            nc.vector.tensor_copy(gs1[:, s0:s1], bytes_[1][:].indirect(cols))
+
+        for t, tag in ((2, "codes1"), (3, "scale_bytes1")):
+            o = keep.tile([P, T], F32, name=f"out_sb{t}", tag=tag, align_bytes=64)
+            nc.gpsimd.memset(o[:], 0.0)
+            outs.append(o)
+
+        squares = [keep.tile([P, S], F32, name=f"squares{t}") for t in range(N_TILES)]
+        words = (gw0, gw1)
+        scales = (gs0, gs1)
+
+        def produce(t, s0, s1):
+            acc = psum.tile([P, s1 - s0], F32, name="acc")
+            u = work.tile([P, s1 - s0], F32, name="u")
+            n_cols = slice(t * P, (t + 1) * P)
+            for e in range(s0 // C, s1 // C):
+                slots = slice(e * C, (e + 1) * C)
+                local = slice(e * C - s0, (e + 1) * C - s0)
+                for a in range(PASSES):
+                    nc.tensor.matmul_mx(
+                        out=acc[:, local],
+                        lhsT=w_sb[e // 2][:, PASSES * (e % 2) + a, t * 2 * P : (t + 1) * 2 * P].bitcast(E2M1X4),
+                        lhsT_scale=ws_sb[:, PASSES * e + a, n_cols],
+                        rhs=words[a][:, slots].bitcast(E4M3X4),
+                        rhs_scale=scales[a][:, slots],
+                        start=(a == 0),
+                        stop=(a == PASSES - 1),
+                    )
+                nc.scalar.activation(u[:, local], acc[:, local], ACT.Relu, bias=b_sb[:, t, e : e + 1])
+            nc.scalar.activation(squares[t][:, s0:s1], u[:], ACT.Square)
+
+        def scatter(t, s0, s1):
+            nc.vector.tensor_tensor(
+                outs[t][:].indirect(dst_sb[:, s0 // 16 : s1 // 16]), squares[t][:, s0:s1], gate_sb[:, s0:s1], MULT
+            )
+
+        def store(t):
+            nc.sync.dma_start(out=out[t * P : (t + 1) * P, :], in_=outs[t][:])
+
+        for s0, s1 in ((0, 256), (256, 512), (512, 1024)):
+            for t in (0, 1):
+                produce(t, s0, s1)
+                scatter(t, s0, s1)
+                if s1 == S:
+                    store(t)
+        for t in (2, 3):
+            produce(t, 0, 512)
+            produce(t, 512, 1024)
+            scatter(t, 0, S)
+            store(t)

@@ -8,7 +8,7 @@ P = 128
 PACK = 4
 PASSES = K // (P * PACK)
 N_TILES = N // P
-CHUNKS = (((0, 768), (768, 1280), (1280, 1536)), ((0, 512), (512, 1024), (1024, 1280), (1280, 1536)))
+CHUNKS = (((0, 1024), (1024, 1536)), ((0, 512), (512, 1024), (1024, 1280), (1280, 1536)))
 
 FLOPS = 2 * K * S * N
 BYTES = 4 * K * T + E * PASSES * (P * 2 * N + 16 * N) + 4 * N * E + 4 * S + 2 * 2 * P * (S // 16) + 4 * N * T
@@ -24,7 +24,10 @@ E2M1X4 = mybir.dt.float4_e2m1fn_x4
 ACT = mybir.ActivationFunctionType
 MULT = mybir.AluOpType.mult
 
-SCALAR_COLS = ((352, 256, 96), (512, 512, 256, 96))
+SCALAR_COLS = ((512, 288), (448, 448, 160, 128))
+PLANE_ROW = (4, 0)
+FIRST = 2 * C
+SHIFTED = 112
 HALF = 4 * C
 
 
@@ -42,8 +45,9 @@ def tile_moe_two_lin_relu2_kernel(tc, xT, w_words, w_scales, b, gate, offs, dst,
         w_sb = [keep.tile([P, 2 * PASSES, 2 * N], U8, name=f"w_sb{g}", align_bytes=64) for g in range(E // 2)]
         ws_sb = keep.tile([P, E * PASSES, N], U8, name="ws_sb", align_bytes=64)
         codes = [keep.tile([P, T], U32, name=f"codes{a}", tag=f"codes{a}", align_bytes=64) for a in range(PASSES)]
-        bytes_ = [keep.tile([P, T], U8, name=f"scale_bytes{a}", tag=f"scale_bytes{a}", align_bytes=64) for a in range(PASSES)]
-        outs = [keep.tile([P, T], F32, name=f"out_sb{t}") for t in range(2)]
+        bytes_ = keep.tile([P, T], U8, name="scale_bytes", tag="scale_bytes", align_bytes=64)
+        gs0 = keep.tile([P, S], U8, name="gs0", align_bytes=64)
+        outs = [keep.tile([P, T], F32, name=f"out_sb{t}") for t in range(N_TILES)]
 
         raw = {}
         for a in range(PASSES):
@@ -55,10 +59,10 @@ def tile_moe_two_lin_relu2_kernel(tc, xT, w_words, w_scales, b, gate, offs, dst,
                 if (a, c) == (0, 1):
                     nc.sync.dma_start(offs_sb[:], offs)
 
-        nc.gpsimd.memset(bytes_[0][:].bitcast(I32), 0)
-        nc.vector.memset(outs[0][:], 0.0)
-        nc.vector.memset(outs[1][:], 0.0)
-        nc.gpsimd.memset(bytes_[1][:].bitcast(I32), 0)
+        nc.gpsimd.memset(bytes_[:].bitcast(I32), 0)
+        for t in range(N_TILES):
+            nc.vector.memset(outs[t][:], 0.0)
+        nc.gpsimd.memset(gs0[:].bitcast(I32), 0)
         nc.gpsimd.memset(ws_sb[:].rearrange("p g n -> p (g n)").bitcast(I32), 0)
         warm = keep.tile([P, 1], F32, name="warm")
         nc.gpsimd.memset(warm[:], 0.0)
@@ -78,14 +82,6 @@ def tile_moe_two_lin_relu2_kernel(tc, xT, w_words, w_scales, b, gate, offs, dst,
 
         load_ws(0, 4)
         load_w(0)
-        nc.sync.dma_start(out=b_sb[:], in_=b.rearrange("(t p) e -> p t e", p=P))
-        nc.sync.dma_start(dst_sb[:], dst)
-        nc.sync.dma_start(gate_sb[:, 0:HALF], gate[0:P, 0:HALF])
-        load_w(1)
-        load_ws(4, 8)
-        load_w(2)
-        load_w(3)
-        nc.sync.dma_start(gate_sb[:, HALF:S], gate[0:P, HALF:S])
 
         def prepare(a, c):
             t0, t1 = CHUNKS[a][c]
@@ -109,30 +105,39 @@ def tile_moe_two_lin_relu2_kernel(tc, xT, w_words, w_scales, b, gate, offs, dst,
                 cols = slice(t0 + lo, t0 + hi)
                 nc.vector.quantize_mx(
                     out=codes[a][:, cols].bitcast(E4M3X4),
-                    scales=bytes_[a][:, cols],
+                    scales=bytes_[PLANE_ROW[a] : P, cols],
                     in_=g[:, lo:hi, :].rearrange("p t d -> p (t d)"),
                 )
 
-        for c in range(3):
+        for c in range(2):
             prepare(0, c)
         gw0 = keep.tile([P, S], U32, name="gw0", align_bytes=64)
-        gs0 = keep.tile([P, S], U8, name="gs0", align_bytes=64)
+        early = keep.tile([P, FIRST], U8, name="early", align_bytes=64)
+
+        def shift(queue, src, s0, s1):
+            queue.dma_start(out=gs0[0:SHIFTED, s0:s1].bitcast(I32), in_=src.bitcast(I32))
+
+        nc.vector.tensor_copy(early[:], bytes_[:].indirect(offs_sb[:, 0 : FIRST // 16]))
         nc.vector.tensor_copy(gw0[:], codes[0][:].indirect(offs_sb[:]))
-        nc.vector.tensor_copy(gs0[:], bytes_[0][:].indirect(offs_sb[:]))
+        shift(nc.sync, early[4 : 4 + SHIFTED, :], 0, FIRST)
+        nc.sync.dma_start(out=b_sb[:], in_=b.rearrange("(t p) e -> p t e", p=P))
+        nc.sync.dma_start(dst_sb[:], dst)
+        nc.sync.dma_start(gate_sb[:, 0:HALF], gate[0:P, 0:HALF])
+        load_w(1)
         for c in range(4):
             prepare(1, c)
 
         gw1 = keep.tile([P, S], U32, name="gw1", align_bytes=64)
         gs1 = keep.tile([P, S], U8, name="gs1", align_bytes=64)
-        for s0, s1 in ((0, 512), (512, 1024)):
+        for s0, s1 in ((0, FIRST), (FIRST, S)):
             cols = offs_sb[:, s0 // 16 : s1 // 16]
+            nc.vector.tensor_copy(gs1[:, s0:s1], bytes_[:].indirect(cols))
             nc.vector.tensor_copy(gw1[:, s0:s1], codes[1][:].indirect(cols))
-            nc.vector.tensor_copy(gs1[:, s0:s1], bytes_[1][:].indirect(cols))
-
-        for t, tag in ((2, "codes1"), (3, "scale_bytes1")):
-            o = keep.tile([P, T], F32, name=f"out_sb{t}", tag=tag, align_bytes=64)
-            nc.gpsimd.memset(o[:], 0.0)
-            outs.append(o)
+        shift(nc.gpsimd, gs1[4 : 4 + SHIFTED, FIRST:S], FIRST, S)
+        load_ws(4, 8)
+        load_w(2)
+        load_w(3)
+        nc.sync.dma_start(gate_sb[:, HALF:S], gate[0:P, HALF:S])
 
         squares = [keep.tile([P, S], F32, name=f"squares{t}") for t in range(N_TILES)]
         words = (gw0, gw1)
@@ -166,14 +171,15 @@ def tile_moe_two_lin_relu2_kernel(tc, xT, w_words, w_scales, b, gate, offs, dst,
         def store(t):
             nc.sync.dma_start(out=out[t * P : (t + 1) * P, :], in_=outs[t][:])
 
-        for s0, s1 in ((0, 256), (256, 512), (512, 1024)):
-            for t in (0, 1):
-                produce(t, s0, s1)
-                scatter(t, s0, s1)
-                if s1 == S:
-                    store(t)
-        for t in (2, 3):
-            produce(t, 0, 512)
-            produce(t, 512, 1024)
-            scatter(t, 0, S)
+        for t in range(N_TILES):
+            produce(t, 0, FIRST)
+            scatter(t, 0, FIRST)
+        for t in (0, 1):
+            produce(t, FIRST, HALF)
+            scatter(t, FIRST, HALF)
+        for t in range(N_TILES):
+            if t >= 2:
+                produce(t, FIRST, HALF)
+            produce(t, HALF, S)
+            scatter(t, HALF if t < 2 else FIRST, S)
             store(t)

@@ -133,7 +133,7 @@ def tile_moe_two_lin_relu2_kernel(tc, xT, w_words, w_scales, b, gate, offs, dst,
             cols = offs_sb[:, s0 // 16 : s1 // 16]
             nc.vector.tensor_copy(gs1[:, s0:s1], bytes_[:].indirect(cols))
             nc.vector.tensor_copy(gw1[:, s0:s1], codes[1][:].indirect(cols))
-        shift(nc.gpsimd, gs1[4 : 4 + SHIFTED, FIRST:S], FIRST, S)
+        shift(nc.sync, gs1[4 : 4 + SHIFTED, FIRST:S], FIRST, S)
         load_ws(4, 8)
         load_w(2)
         load_w(3)

@@ -8,7 +8,7 @@ P = 128
 PACK = 4
 PASSES = K // (P * PACK)
 N_TILES = N // P
-CHUNKS = (((0, 1024), (1024, 1536)), ((0, 512), (512, 1024), (1024, 1280), (1280, 1536)))
+CHUNKS = (((0, 768), (768, 1536)), ((0, 512), (512, 1024), (1024, 1280), (1280, 1536)))
 
 FLOPS = 2 * K * S * N
 BYTES = 4 * K * T + E * PASSES * (P * 2 * N + 16 * N) + 4 * N * E + 4 * S + 2 * 2 * P * (S // 16) + 4 * N * T
@@ -24,7 +24,7 @@ E2M1X4 = mybir.dt.float4_e2m1fn_x4
 ACT = mybir.ActivationFunctionType
 MULT = mybir.AluOpType.mult
 
-SCALAR_COLS = ((512, 288), (448, 448, 160, 128))
+SCALAR_COLS = ((416, 352), (448, 448, 160, 128))
 PLANE_ROW = (4, 0)
 FIRST = 2 * C
 SHIFTED = 112
@@ -50,14 +50,19 @@ def tile_moe_two_lin_relu2_kernel(tc, xT, w_words, w_scales, b, gate, offs, dst,
         outs = [keep.tile([P, T], F32, name=f"out_sb{t}") for t in range(N_TILES)]
 
         raw = {}
-        for a in range(PASSES):
-            rows = xT[a * 512 : (a + 1) * 512, :].rearrange("(p d) t -> p d t", d=PACK)
-            for c, (t0, t1) in enumerate(CHUNKS[a]):
-                r = keep.tile([P, PACK, t1 - t0], F32, name=f"raw{a}_{c}")
-                nc.sync.dma_start(out=r[:], in_=rows[:, :, t0:t1])
-                raw[a, c] = r
-                if (a, c) == (0, 1):
-                    nc.sync.dma_start(offs_sb[:], offs)
+        half = T // 2
+        raw0 = keep.tile([P, 11, half], F32, name="raw0")
+        pairs = xT[0:512, :].rearrange("(p h e) t -> p h (e t)", h=2, e=2)
+        nc.sync.dma_start(out=raw0[:, 0:6, :].rearrange("p (h j) t -> p h (j t)", h=2), in_=pairs[:, :, 0 : 3 * half])
+        nc.sync.dma_start(out=raw0[:, 6:10:3, :], in_=pairs[:, :, 3 * half : 4 * half])
+        nc.sync.dma_start(offs_sb[:], offs)
+        raw[0, 0] = raw0[:, 0:6, :].rearrange("p (h j) t -> p h j t", h=2)[:, :, 0:3:2, :]
+        raw[0, 1] = raw0[:, 1:11, :].rearrange("p (e j) t -> p j e t", e=2)[:, 0:4:3, :, :]
+        rows = xT[512:1024, :].rearrange("(p d) t -> p d t", d=PACK)
+        for c, (t0, t1) in enumerate(CHUNKS[1]):
+            r = keep.tile([P, PACK, t1 - t0], F32, name=f"raw1_{c}")
+            nc.sync.dma_start(out=r[:], in_=rows[:, :, t0:t1])
+            raw[1, c] = r[:].rearrange("p (h e) t -> p h e t", h=2)
 
         nc.gpsimd.memset(bytes_[:].bitcast(I32), 0)
         for t in range(N_TILES):
@@ -92,8 +97,8 @@ def tile_moe_two_lin_relu2_kernel(tc, xT, w_words, w_scales, b, gate, offs, dst,
 
             def four(lo, hi):
                 return (
-                    g[:, lo:hi, :].rearrange("p (c i) d -> p c d i", i=4),
-                    src[:, :, lo:hi].rearrange("p d (c i) -> p c d i", i=4),
+                    g[:, lo:hi, :].rearrange("p (c i) (h e) -> p c h e i", i=4, h=2),
+                    src[:, :, :, lo:hi].rearrange("p h e (c i) -> p c h e i", i=4),
                 )
 
             if split:

@@ -6,9 +6,10 @@ K, T, E, C, N = 1024, 1536, 8, 128, 512
 S = E * C
 P = 128
 PACK = 4
-PASSES = K // (P * PACK)
+K_PASS = P * PACK
+PASSES = K // K_PASS
 N_TILES = N // P
-CHUNKS = (((0, 768), (768, 1536)), ((0, 512), (512, 1024), (1024, 1280), (1280, 1536)))
+LIST = 16
 
 FLOPS = 2 * K * S * N
 BYTES = 4 * K * T + E * PASSES * (P * 2 * N + 16 * N) + 4 * N * E + 4 * S + 2 * 2 * P * (S // 16) + 4 * N * T
@@ -24,11 +25,16 @@ E2M1X4 = mybir.dt.float4_e2m1fn_x4
 ACT = mybir.ActivationFunctionType
 MULT = mybir.AluOpType.mult
 
-SCALAR_COLS = ((416, 352), (448, 448, 160, 128))
-PLANE_ROW = (4, 0)
+T_HALF = T // 2
+PASS1_CHUNKS = (512, 512, 256, 256)
+QUANT_TOKENS = 512
+VECTOR_TOKENS_WHILE_GATHERING = 64
+
+SCALE_ROW = (4, 0)
+MOVED_ROWS = 112
+
 FIRST = 2 * C
-SHIFTED = 112
-HALF = 4 * C
+HALF = S // 2
 
 
 def tile_moe_two_lin_relu2_kernel(tc, xT, w_words, w_scales, b, gate, offs, dst, out):
@@ -38,153 +44,150 @@ def tile_moe_two_lin_relu2_kernel(tc, xT, w_words, w_scales, b, gate, offs, dst,
         work = ctx.enter_context(tc.tile_pool(name="work", bufs=4))
         psum = ctx.enter_context(tc.psum_pool(name="psum", bufs=8))
 
-        offs_sb = keep.tile([P, S // 16], U16, name="offs_sb")
-        dst_sb = keep.tile([P, S // 16], U16, name="dst_sb")
+        offs_sb = keep.tile([P, S // LIST], U16, name="offs_sb")
+        dst_sb = keep.tile([P, S // LIST], U16, name="dst_sb")
         b_sb = keep.tile([P, N_TILES, E], F32, name="b_sb")
         gate_sb = keep.tile([P, S], F32, name="gate_sb")
-        w_sb = [keep.tile([P, 2 * PASSES, 2 * N], U8, name=f"w_sb{g}", align_bytes=64) for g in range(E // 2)]
-        ws_sb = keep.tile([P, E * PASSES, N], U8, name="ws_sb", align_bytes=64)
-        codes = [keep.tile([P, T], U32, name=f"codes{a}", tag=f"codes{a}", align_bytes=64) for a in range(PASSES)]
-        bytes_ = keep.tile([P, T], U8, name="scale_bytes", tag="scale_bytes", align_bytes=64)
-        gs0 = keep.tile([P, S], U8, name="gs0", align_bytes=64)
-        outs = [keep.tile([P, T], F32, name=f"out_sb{t}") for t in range(N_TILES)]
+        w_sb = [keep.tile([P, 2 * PASSES, 2 * N], U8, name=f"w_sb{pair}", align_bytes=64) for pair in range(E // 2)]
+        w_scale_sb = keep.tile([P, E * PASSES, N], U8, name="w_scale_sb", align_bytes=64)
+        token_words = [keep.tile([P, T], U32, name=f"token_words{a}", align_bytes=64) for a in range(PASSES)]
+        token_scales = keep.tile([P, T], U8, name="token_scales", align_bytes=64)
+        slot_scales0 = keep.tile([P, S], U8, name="slot_scales0", align_bytes=64)
+        out_sb = [keep.tile([P, T], F32, name=f"out_sb{t}") for t in range(N_TILES)]
 
-        raw = {}
-        half = T // 2
-        raw0 = keep.tile([P, 11, half], F32, name="raw0")
-        pairs = xT[0:512, :].rearrange("(p h e) t -> p h (e t)", h=2, e=2)
-        nc.sync.dma_start(out=raw0[:, 0:6, :].rearrange("p (h j) t -> p h (j t)", h=2), in_=pairs[:, :, 0 : 3 * half])
-        nc.sync.dma_start(out=raw0[:, 6:10:3, :], in_=pairs[:, :, 3 * half : 4 * half])
+        x0 = keep.tile([P, 11, T_HALF], F32, name="x0")
+        row_pairs = xT[0:K_PASS, :].rearrange("(p h e) t -> p h (e t)", h=2, e=2)
+        nc.sync.dma_start(out=x0[:, 0:6, :].rearrange("p (h u) t -> p h (u t)", h=2), in_=row_pairs[:, :, 0 : 3 * T_HALF])
+        nc.sync.dma_start(out=x0[:, 6:10:3, :], in_=row_pairs[:, :, 3 * T_HALF : 4 * T_HALF])
         nc.sync.dma_start(offs_sb[:], offs)
-        raw[0, 0] = raw0[:, 0:6, :].rearrange("p (h j) t -> p h j t", h=2)[:, :, 0:3:2, :]
-        raw[0, 1] = raw0[:, 1:11, :].rearrange("p (e j) t -> p j e t", e=2)[:, 0:4:3, :, :]
-        rows = xT[512:1024, :].rearrange("(p d) t -> p d t", d=PACK)
-        for c, (t0, t1) in enumerate(CHUNKS[1]):
-            r = keep.tile([P, PACK, t1 - t0], F32, name=f"raw1_{c}")
-            nc.sync.dma_start(out=r[:], in_=rows[:, :, t0:t1])
-            raw[1, c] = r[:].rearrange("p (h e) t -> p h e t", h=2)
+        x0_chunks = (
+            x0[:, 0:6, :].rearrange("p (h u) t -> p h u t", h=2)[:, :, 0:3:2, :],
+            x0[:, 1:11, :].rearrange("p (e u) t -> p u e t", e=2)[:, 0:4:3, :, :],
+        )
 
-        nc.gpsimd.memset(bytes_[:].bitcast(I32), 0)
-        for t in range(N_TILES):
-            nc.vector.memset(outs[t][:], 0.0)
-        nc.gpsimd.memset(gs0[:].bitcast(I32), 0)
-        nc.gpsimd.memset(ws_sb[:].rearrange("p g n -> p (g n)").bitcast(I32), 0)
-        warm = keep.tile([P, 1], F32, name="warm")
-        nc.gpsimd.memset(warm[:], 0.0)
-        nc.scalar.activation(warm[:], warm[:], ACT.Square)
+        x1_rows = xT[K_PASS:K, :].rearrange("(p d) t -> p d t", d=PACK)
+        x1_starts = [sum(PASS1_CHUNKS[:c]) for c in range(len(PASS1_CHUNKS))]
+        x1_chunks = []
+        for t0, width in zip(x1_starts, PASS1_CHUNKS):
+            x1 = keep.tile([P, PACK, width], F32, name=f"x1_{t0}")
+            nc.sync.dma_start(out=x1[:], in_=x1_rows[:, :, t0 : t0 + width])
+            x1_chunks.append(x1[:].rearrange("p (h e) t -> p h e t", h=2))
 
-        def load_w(g):
-            nc.sync.dma_start(
-                out=w_sb[g][:].bitcast(I32), in_=w_words[2 * g : 2 * g + 2].rearrange("e a p c -> p (e a) c").bitcast(I32)
-            )
+        nc.gpsimd.memset(token_scales[:].bitcast(I32), 0)
+        for t in range(N_TILES - 1):
+            nc.vector.memset(out_sb[t][:], 0.0)
+        nc.gpsimd.memset(slot_scales0[:].bitcast(I32), 0)
+        nc.gpsimd.memset(w_scale_sb[:].rearrange("p g n -> p (g n)").bitcast(I32), 0)
+        nc.scalar.activation(out_sb[N_TILES - 1][:], out_sb[0][:], ACT.Square)
 
-        def load_ws(e0, e1):
+        def load_weights(pair):
+            words = w_words[2 * pair : 2 * pair + 2].rearrange("e a p c -> p (e a) c")
+            nc.sync.dma_start(out=w_sb[pair][:].bitcast(I32), in_=words.bitcast(I32))
+
+        def load_weight_scales(e0, e1):
             for r in range(4):
                 nc.sync.dma_start(
-                    out=ws_sb[r : P : 32, 2 * e0 : 2 * e1, :].bitcast(I32),
-                    in_=w_scales[e0:e1, :, r : 16 : 4, :].rearrange("e a q n -> q (e a) n").bitcast(I32),
+                    out=w_scale_sb[r:P:32, PASSES * e0 : PASSES * e1, :].bitcast(I32),
+                    in_=w_scales[e0:e1, :, r:16:4, :].rearrange("e a q n -> q (e a) n").bitcast(I32),
                 )
 
-        load_ws(0, 4)
-        load_w(0)
+        def load_gate(s0, s1):
+            nc.sync.dma_start(gate_sb[:, s0:s1], gate[0:P, s0:s1])
 
-        def prepare(a, c):
-            t0, t1 = CHUNKS[a][c]
-            width = t1 - t0
-            split = SCALAR_COLS[a][c]
-            g = work.tile([P, width, PACK], BF16, name="grouped", align_bytes=64)
-            src = raw[a, c]
+        load_weight_scales(0, E // 2)
+        load_weights(0)
 
-            def four(lo, hi):
+        def quantise(a, x, t0, width, scalar_tokens):
+            grouped = work.tile([P, width, PACK], BF16, name="grouped", align_bytes=64)
+
+            def by_fours(lo, hi):
                 return (
-                    g[:, lo:hi, :].rearrange("p (c i) (h e) -> p c h e i", i=4, h=2),
-                    src[:, :, :, lo:hi].rearrange("p h e (c i) -> p c h e i", i=4),
+                    grouped[:, lo:hi, :].rearrange("p (c i) (h e) -> p c h e i", i=4, h=2),
+                    x[:, :, :, lo:hi].rearrange("p h e (c i) -> p c h e i", i=4),
                 )
 
-            if split:
-                nc.scalar.copy(*four(0, split))
-            if split < width:
-                nc.vector.tensor_copy(*four(split, width))
-            for lo in range(0, width, 512):
-                hi = min(lo + 512, width)
-                cols = slice(t0 + lo, t0 + hi)
+            nc.scalar.copy(*by_fours(0, scalar_tokens))
+            nc.vector.tensor_copy(*by_fours(scalar_tokens, width))
+            for lo in range(0, width, QUANT_TOKENS):
+                hi = min(lo + QUANT_TOKENS, width)
+                tokens = slice(t0 + lo, t0 + hi)
                 nc.vector.quantize_mx(
-                    out=codes[a][:, cols].bitcast(E4M3X4),
-                    scales=bytes_[PLANE_ROW[a] : P, cols],
-                    in_=g[:, lo:hi, :].rearrange("p t d -> p (t d)"),
+                    out=token_words[a][:, tokens].bitcast(E4M3X4),
+                    scales=token_scales[SCALE_ROW[a] : P, tokens],
+                    in_=grouped[:, lo:hi, :].rearrange("p t d -> p (t d)"),
                 )
 
-        for c in range(2):
-            prepare(0, c)
-        gw0 = keep.tile([P, S], U32, name="gw0", align_bytes=64)
-        early = keep.tile([P, FIRST], U8, name="early", align_bytes=64)
+        def gather(slot_values, token_values, s0, s1):
+            nc.vector.tensor_copy(slot_values, token_values[:].indirect(offs_sb[:, s0 // LIST : s1 // LIST]))
 
-        def shift(queue, src, s0, s1):
-            queue.dma_start(out=gs0[0:SHIFTED, s0:s1].bitcast(I32), in_=src.bitcast(I32))
+        def move_pass0_scales(gathered, s0, s1):
+            rows = slice(SCALE_ROW[0], SCALE_ROW[0] + MOVED_ROWS)
+            nc.sync.dma_start(out=slot_scales0[0:MOVED_ROWS, s0:s1].bitcast(I32), in_=gathered[rows, :].bitcast(I32))
 
-        nc.vector.tensor_copy(early[:], bytes_[:].indirect(offs_sb[:, 0 : FIRST // 16]))
-        nc.vector.tensor_copy(gw0[:], codes[0][:].indirect(offs_sb[:]))
-        shift(nc.sync, early[4 : 4 + SHIFTED, :], 0, FIRST)
+        for c, x in enumerate(x0_chunks):
+            quantise(0, x, c * T_HALF, T_HALF, T_HALF // 2)
+        slot_words0 = keep.tile([P, S], U32, name="slot_words0", align_bytes=64)
+        first_scales0 = keep.tile([P, FIRST], U8, name="first_scales0", align_bytes=64)
+        gather(first_scales0[:], token_scales, 0, FIRST)
+        gather(slot_words0[:], token_words[0], 0, S)
+        move_pass0_scales(first_scales0[:], 0, FIRST)
         nc.sync.dma_start(out=b_sb[:], in_=b.rearrange("(t p) e -> p t e", p=P))
         nc.sync.dma_start(dst_sb[:], dst)
-        nc.sync.dma_start(gate_sb[:, 0:HALF], gate[0:P, 0:HALF])
-        load_w(1)
-        for c in range(4):
-            prepare(1, c)
+        load_gate(0, HALF)
+        load_weights(1)
 
-        gw1 = keep.tile([P, S], U32, name="gw1", align_bytes=64)
-        gs1 = keep.tile([P, S], U8, name="gs1", align_bytes=64)
+        for x, t0, width in zip(x1_chunks, x1_starts, PASS1_CHUNKS):
+            wide = width == max(PASS1_CHUNKS)
+            quantise(1, x, t0, width, width - VECTOR_TOKENS_WHILE_GATHERING if wide else width // 2)
+        slot_words1 = keep.tile([P, S], U32, name="slot_words1", align_bytes=64)
+        slot_scales1 = keep.tile([P, S], U8, name="slot_scales1", align_bytes=64)
         for s0, s1 in ((0, FIRST), (FIRST, S)):
-            cols = offs_sb[:, s0 // 16 : s1 // 16]
-            nc.vector.tensor_copy(gs1[:, s0:s1], bytes_[:].indirect(cols))
-            nc.vector.tensor_copy(gw1[:, s0:s1], codes[1][:].indirect(cols))
-        shift(nc.sync, gs1[4 : 4 + SHIFTED, FIRST:S], FIRST, S)
-        load_ws(4, 8)
-        load_w(2)
-        load_w(3)
-        nc.sync.dma_start(gate_sb[:, HALF:S], gate[0:P, HALF:S])
+            gather(slot_scales1[:, s0:s1], token_scales, s0, s1)
+            gather(slot_words1[:, s0:s1], token_words[1], s0, s1)
+        move_pass0_scales(slot_scales1[:, FIRST:S], FIRST, S)
+        load_weight_scales(E // 2, E)
+        load_weights(2)
+        load_weights(3)
+        load_gate(HALF, S)
 
-        squares = [keep.tile([P, S], F32, name=f"squares{t}") for t in range(N_TILES)]
-        words = (gw0, gw1)
-        scales = (gs0, gs1)
+        slot_words = (slot_words0, slot_words1)
+        slot_scales = (slot_scales0, slot_scales1)
+        y_sb = [keep.tile([P, S], F32, name=f"y_sb{t}") for t in range(N_TILES)]
 
-        def produce(t, s0, s1):
+        def experts(t, s0, s1):
             acc = psum.tile([P, s1 - s0], F32, name="acc")
-            u = work.tile([P, s1 - s0], F32, name="u")
-            n_cols = slice(t * P, (t + 1) * P)
-            for e in range(s0 // C, s1 // C):
+            relu = work.tile([P, s1 - s0], F32, name="relu")
+            columns = {e: slice(e * C - s0, (e + 1) * C - s0) for e in range(s0 // C, s1 // C)}
+            for e, local in columns.items():
                 slots = slice(e * C, (e + 1) * C)
-                local = slice(e * C - s0, (e + 1) * C - s0)
                 for a in range(PASSES):
                     nc.tensor.matmul_mx(
                         out=acc[:, local],
-                        lhsT=w_sb[e // 2][:, PASSES * (e % 2) + a, t * 2 * P : (t + 1) * 2 * P].bitcast(E2M1X4),
-                        lhsT_scale=ws_sb[:, PASSES * e + a, n_cols],
-                        rhs=words[a][:, slots].bitcast(E4M3X4),
-                        rhs_scale=scales[a][:, slots],
+                        lhsT=w_sb[e // 2][:, PASSES * (e % 2) + a, 2 * t * P : 2 * (t + 1) * P].bitcast(E2M1X4),
+                        lhsT_scale=w_scale_sb[:, PASSES * e + a, t * P : (t + 1) * P],
+                        rhs=slot_words[a][:, slots].bitcast(E4M3X4),
+                        rhs_scale=slot_scales[a][:, slots],
                         start=(a == 0),
                         stop=(a == PASSES - 1),
                     )
-                nc.scalar.activation(u[:, local], acc[:, local], ACT.Relu, bias=b_sb[:, t, e : e + 1])
-            nc.scalar.activation(squares[t][:, s0:s1], u[:], ACT.Square)
+            for e, local in columns.items():
+                nc.scalar.activation(relu[:, local], acc[:, local], ACT.Relu, bias=b_sb[:, t, e : e + 1])
+            nc.scalar.activation(y_sb[t][:, s0:s1], relu[:], ACT.Square)
 
         def scatter(t, s0, s1):
-            nc.vector.tensor_tensor(
-                outs[t][:].indirect(dst_sb[:, s0 // 16 : s1 // 16]), squares[t][:, s0:s1], gate_sb[:, s0:s1], MULT
-            )
+            window = out_sb[t][:].indirect(dst_sb[:, s0 // LIST : s1 // LIST])
+            nc.vector.tensor_tensor(window, y_sb[t][:, s0:s1], gate_sb[:, s0:s1], MULT)
 
-        def store(t):
-            nc.sync.dma_start(out=out[t * P : (t + 1) * P, :], in_=outs[t][:])
-
+        early_tiles = range(N_TILES // 2)
         for t in range(N_TILES):
-            produce(t, 0, FIRST)
+            experts(t, 0, FIRST)
             scatter(t, 0, FIRST)
-        for t in (0, 1):
-            produce(t, FIRST, HALF)
+        for t in early_tiles:
+            experts(t, FIRST, HALF)
             scatter(t, FIRST, HALF)
         for t in range(N_TILES):
-            if t >= 2:
-                produce(t, FIRST, HALF)
-            produce(t, HALF, S)
-            scatter(t, HALF if t < 2 else FIRST, S)
-            store(t)
+            if t not in early_tiles:
+                experts(t, FIRST, HALF)
+            experts(t, HALF, S)
+            scatter(t, HALF if t in early_tiles else FIRST, S)
+            nc.sync.dma_start(out=out[t * P : (t + 1) * P, :], in_=out_sb[t][:])

@@ -28,7 +28,8 @@ MULT = mybir.AluOpType.mult
 T_HALF = T // 2
 PASS1_CHUNKS = (512, 512, 256, 256)
 QUANT_TOKENS = 512
-VECTOR_TOKENS_WHILE_GATHERING = 64
+PASS0_SCALAR_TOKENS = (448, 384)
+PASS1_SCALAR_TOKENS = (512, 448, 160, 128)
 
 SCALE_ROW = (4, 0)
 MOVED_ROWS = 112
@@ -107,7 +108,8 @@ def tile_moe_two_lin_relu2_kernel(tc, xT, w_words, w_scales, b, gate, offs, dst,
                 )
 
             nc.scalar.copy(*by_fours(0, scalar_tokens))
-            nc.vector.tensor_copy(*by_fours(scalar_tokens, width))
+            if scalar_tokens < width:
+                nc.vector.tensor_copy(*by_fours(scalar_tokens, width))
             for lo in range(0, width, QUANT_TOKENS):
                 hi = min(lo + QUANT_TOKENS, width)
                 tokens = slice(t0 + lo, t0 + hi)
@@ -125,7 +127,7 @@ def tile_moe_two_lin_relu2_kernel(tc, xT, w_words, w_scales, b, gate, offs, dst,
             nc.sync.dma_start(out=slot_scales0[0:MOVED_ROWS, s0:s1].bitcast(I32), in_=gathered[rows, :].bitcast(I32))
 
         for c, x in enumerate(x0_chunks):
-            quantise(0, x, c * T_HALF, T_HALF, T_HALF // 2)
+            quantise(0, x, c * T_HALF, T_HALF, PASS0_SCALAR_TOKENS[c])
         slot_words0 = keep.tile([P, S], U32, name="slot_words0", align_bytes=64)
         first_scales0 = keep.tile([P, FIRST], U8, name="first_scales0", align_bytes=64)
         gather(first_scales0[:], token_scales, 0, FIRST)
@@ -136,9 +138,8 @@ def tile_moe_two_lin_relu2_kernel(tc, xT, w_words, w_scales, b, gate, offs, dst,
         load_gate(0, HALF)
         load_weights(1)
 
-        for x, t0, width in zip(x1_chunks, x1_starts, PASS1_CHUNKS):
-            wide = width == max(PASS1_CHUNKS)
-            quantise(1, x, t0, width, width - VECTOR_TOKENS_WHILE_GATHERING if wide else width // 2)
+        for x, t0, width, scalar_tokens in zip(x1_chunks, x1_starts, PASS1_CHUNKS, PASS1_SCALAR_TOKENS):
+            quantise(1, x, t0, width, scalar_tokens)
         slot_words1 = keep.tile([P, S], U32, name="slot_words1", align_bytes=64)
         slot_scales1 = keep.tile([P, S], U8, name="slot_scales1", align_bytes=64)
         for s0, s1 in ((0, FIRST), (FIRST, S)):

@@ -25,17 +25,10 @@ E2M1X4 = mybir.dt.float4_e2m1fn_x4
 ACT = mybir.ActivationFunctionType
 MULT = mybir.AluOpType.mult
 
-T_HALF = T // 2
-PASS1_CHUNKS = (512, 512, 256, 256)
-QUANT_TOKENS = 512
-PASS0_SCALAR_TOKENS = (448, 384)
-PASS1_SCALAR_TOKENS = (512, 448, 160, 128)
-
-SCALE_ROW = (4, 0)
-MOVED_ROWS = 112
-
-FIRST = 2 * C
-HALF = S // 2
+G = 2 * C
+GROUPS = ((0, G), (G, 2 * G), (2 * G, S))
+T_FIRST = 768
+SCALAR_TOKENS = ((0, 384), (768, 128), (768, 128))
 
 
 def tile_moe_two_lin_relu2_kernel(tc, xT, w_words, w_scales, b, gate, offs, dst, out):
@@ -51,39 +44,37 @@ def tile_moe_two_lin_relu2_kernel(tc, xT, w_words, w_scales, b, gate, offs, dst,
         gate_sb = keep.tile([P, S], F32, name="gate_sb")
         w_sb = [keep.tile([P, 2 * PASSES, 2 * N], U8, name=f"w_sb{pair}", align_bytes=64) for pair in range(E // 2)]
         w_scale_sb = keep.tile([P, E * PASSES, N], U8, name="w_scale_sb", align_bytes=64)
-        token_words = [keep.tile([P, T], U32, name=f"token_words{a}", align_bytes=64) for a in range(PASSES)]
-        token_scales = keep.tile([P, T], U8, name="token_scales", align_bytes=64)
-        slot_scales0 = keep.tile([P, S], U8, name="slot_scales0", align_bytes=64)
         out_sb = [keep.tile([P, T], F32, name=f"out_sb{t}") for t in range(N_TILES)]
 
-        x0 = keep.tile([P, 11, T_HALF], F32, name="x0")
-        row_pairs = xT[0:K_PASS, :].rearrange("(p h e) t -> p h (e t)", h=2, e=2)
-        nc.sync.dma_start(out=x0[:, 0:6, :].rearrange("p (h u) t -> p h (u t)", h=2), in_=row_pairs[:, :, 0 : 3 * T_HALF])
-        nc.sync.dma_start(out=x0[:, 6:10:3, :], in_=row_pairs[:, :, 3 * T_HALF : 4 * T_HALF])
-        nc.sync.dma_start(offs_sb[:], offs)
-        x0_chunks = (
-            x0[:, 0:6, :].rearrange("p (h u) t -> p h u t", h=2)[:, :, 0:3:2, :],
-            x0[:, 1:11, :].rearrange("p (e u) t -> p u e t", e=2)[:, 0:4:3, :, :],
-        )
+        def rows(a):
+            return xT[a * K_PASS : (a + 1) * K_PASS, :].rearrange("(p d) t -> p (d t)", d=PACK)
 
-        x1_rows = xT[K_PASS:K, :].rearrange("(p d) t -> p d t", d=PACK)
-        x1_starts = [sum(PASS1_CHUNKS[:c]) for c in range(len(PASS1_CHUNKS))]
-        x1_chunks = []
-        for t0, width in zip(x1_starts, PASS1_CHUNKS):
-            x1 = keep.tile([P, PACK, width], F32, name=f"x1_{t0}")
-            nc.sync.dma_start(out=x1[:], in_=x1_rows[:, :, t0 : t0 + width])
-            x1_chunks.append(x1[:].rearrange("p (h e) t -> p h e t", h=2))
+        x_pair = []
+        for u in range(3):
+            a, h = divmod(u, 2)
+            x = keep.tile([P, 2 * T], F32, name=f"x_pair{u}", align_bytes=64)
+            run = rows(a)[:, 2 * h * T : 2 * (h + 1) * T]
+            nc.sync.dma_start(out=x[:, 0 : T + T_FIRST], in_=run[:, 0 : T + T_FIRST])
+            nc.sync.dma_start(out=x[:, T + T_FIRST : 2 * T], in_=run[:, T + T_FIRST : 2 * T])
+            if u == 0:
+                nc.sync.dma_start(offs_sb[:], offs)
+            x_pair.append(x[:].rearrange("p (e t) -> p t e", e=2))
+            last_pair = x
+        x_row = []
+        for d in (2, 3):
+            x = keep.tile([P, T], F32, name=f"x_row{d}")
+            nc.sync.dma_start(out=x[:], in_=rows(1)[:, d * T : (d + 1) * T])
+            x_row.append(x)
 
-        nc.gpsimd.memset(token_scales[:].bitcast(I32), 0)
-        for t in range(N_TILES - 1):
-            nc.vector.memset(out_sb[t][:], 0.0)
-        nc.gpsimd.memset(slot_scales0[:].bitcast(I32), 0)
         nc.gpsimd.memset(w_scale_sb[:].rearrange("p g n -> p (g n)").bitcast(I32), 0)
-        nc.scalar.activation(out_sb[N_TILES - 1][:], out_sb[0][:], ACT.Square)
+        for t in range(N_TILES // 2):
+            nc.vector.memset(out_sb[t][:], 0.0)
+        for t in range(N_TILES // 2, N_TILES):
+            nc.scalar.activation(out_sb[t][:], out_sb[0][:], ACT.Square)
 
-        def load_weights(pair):
-            words = w_words[2 * pair : 2 * pair + 2].rearrange("e a p c -> p (e a) c")
-            nc.sync.dma_start(out=w_sb[pair][:].bitcast(I32), in_=words.bitcast(I32))
+        def load_weights(g):
+            words = w_words[2 * g : 2 * g + 2].rearrange("e a p c -> p (e a) c")
+            nc.sync.dma_start(out=w_sb[g][:].bitcast(I32), in_=words.bitcast(I32))
 
         def load_weight_scales(e0, e1):
             for r in range(4):
@@ -95,69 +86,98 @@ def tile_moe_two_lin_relu2_kernel(tc, xT, w_words, w_scales, b, gate, offs, dst,
         def load_gate(s0, s1):
             nc.sync.dma_start(gate_sb[:, s0:s1], gate[0:P, s0:s1])
 
-        load_weight_scales(0, E // 2)
+        load_weight_scales(0, 2)
         load_weights(0)
-
-        def quantise(a, x, t0, width, scalar_tokens):
-            grouped = work.tile([P, width, PACK], BF16, name="grouped", align_bytes=64)
-
-            def by_fours(lo, hi):
-                return (
-                    grouped[:, lo:hi, :].rearrange("p (c i) (h e) -> p c h e i", i=4, h=2),
-                    x[:, :, :, lo:hi].rearrange("p h e (c i) -> p c h e i", i=4),
-                )
-
-            nc.scalar.copy(*by_fours(0, scalar_tokens))
-            if scalar_tokens < width:
-                nc.vector.tensor_copy(*by_fours(scalar_tokens, width))
-            for lo in range(0, width, QUANT_TOKENS):
-                hi = min(lo + QUANT_TOKENS, width)
-                tokens = slice(t0 + lo, t0 + hi)
-                nc.vector.quantize_mx(
-                    out=token_words[a][:, tokens].bitcast(E4M3X4),
-                    scales=token_scales[SCALE_ROW[a] : P, tokens],
-                    in_=grouped[:, lo:hi, :].rearrange("p t d -> p (t d)"),
-                )
-
-        def gather(slot_values, token_values, s0, s1):
-            nc.vector.tensor_copy(slot_values, token_values[:].indirect(offs_sb[:, s0 // LIST : s1 // LIST]))
-
-        def move_pass0_scales(gathered, s0, s1):
-            rows = slice(SCALE_ROW[0], SCALE_ROW[0] + MOVED_ROWS)
-            nc.sync.dma_start(out=slot_scales0[0:MOVED_ROWS, s0:s1].bitcast(I32), in_=gathered[rows, :].bitcast(I32))
-
-        for c, x in enumerate(x0_chunks):
-            quantise(0, x, c * T_HALF, T_HALF, PASS0_SCALAR_TOKENS[c])
-        slot_words0 = keep.tile([P, S], U32, name="slot_words0", align_bytes=64)
-        first_scales0 = keep.tile([P, FIRST], U8, name="first_scales0", align_bytes=64)
-        gather(first_scales0[:], token_scales, 0, FIRST)
-        gather(slot_words0[:], token_words[0], 0, S)
-        move_pass0_scales(first_scales0[:], 0, FIRST)
         nc.sync.dma_start(out=b_sb[:], in_=b.rearrange("(t p) e -> p t e", p=P))
         nc.sync.dma_start(dst_sb[:], dst)
-        load_gate(0, HALF)
+        load_gate(0, G)
+        load_weight_scales(2, E)
         load_weights(1)
-
-        for x, t0, width, scalar_tokens in zip(x1_chunks, x1_starts, PASS1_CHUNKS, PASS1_SCALAR_TOKENS):
-            quantise(1, x, t0, width, scalar_tokens)
-        slot_words1 = keep.tile([P, S], U32, name="slot_words1", align_bytes=64)
-        slot_scales1 = keep.tile([P, S], U8, name="slot_scales1", align_bytes=64)
-        for s0, s1 in ((0, FIRST), (FIRST, S)):
-            gather(slot_scales1[:, s0:s1], token_scales, s0, s1)
-            gather(slot_words1[:, s0:s1], token_words[1], s0, s1)
-        move_pass0_scales(slot_scales1[:, FIRST:S], FIRST, S)
-        load_weight_scales(E // 2, E)
+        load_gate(G, S)
         load_weights(2)
         load_weights(3)
-        load_gate(HALF, S)
 
-        slot_words = (slot_words0, slot_words1)
-        slot_scales = (slot_scales0, slot_scales1)
+        pair_words = [keep.tile([P, T], U32, name=f"pair_words{u}") for u in range(3)]
+
+        def round_pair(u):
+            rounded = pair_words[u][:].bitcast(BF16).rearrange("p (t e) -> p t e", e=2)
+            for (t0, t1), scalar_tokens in zip(((0, T_FIRST), (T_FIRST, T)), SCALAR_TOKENS[u]):
+                cut = t0 + scalar_tokens
+                if t0 < cut:
+                    nc.scalar.copy(rounded[:, t0:cut, :], x_pair[u][:, t0:cut, :])
+                if cut < t1:
+                    nc.vector.tensor_copy(rounded[:, cut:t1, :], x_pair[u][:, cut:t1, :])
+
+        def entries(s0, s1):
+            return offs_sb[:, s0 // LIST : s1 // LIST]
+
+        codes = [keep.tile([P, S], U32, name=f"codes{a}", align_bytes=64) for a in range(PASSES)]
+        scales = [keep.tile([P, S], U8, name=f"scales{a}", align_bytes=64) for a in range(PASSES)]
+
+        def quantise(a, s0, s1, woven):
+            nc.vector.quantize_mx(
+                out=codes[a][:, s0:s1].bitcast(E4M3X4),
+                scales=scales[a][:, s0:s1],
+                in_=woven.bitcast(BF16),
+            )
+
+        halves0 = keep.tile([P, 2, S], U32, name="halves0")
+        for u in range(2):
+            round_pair(u)
+            nc.vector.tensor_copy(halves0[:, u, :], pair_words[u][:].indirect(entries(0, S)))
+        round_pair(2)
+        woven0_late = keep.tile([P, S], U32, name="woven0_late", align_bytes=64)
+        woven0 = {
+            0: last_pair[:, 0 : 2 * G].bitcast(U32),
+            G: last_pair[:, T : T + 2 * G].bitcast(U32),
+            2 * G: woven0_late[:, 0 : 2 * G],
+            3 * G: woven0_late[:, 2 * G : 4 * G],
+        }
+
+        def weave0(s0, s1):
+            woven = woven0[s0].rearrange("p (s h) -> p s h", h=2)
+            nc.scalar.copy(woven, halves0[:, :, s0:s1].rearrange("p h s -> p s h"))
+
+        for s0, s1 in GROUPS[:2]:
+            weave0(s0, s1)
+
+        LATE = S - G
+        halves1 = keep.tile([P, 2 * LATE], U32, name="halves1", align_bytes=64)
+        first = halves1[:, 0 : 2 * G]
+        first_values = first.bitcast(BF16).rearrange("p (s d) -> p s d", d=PACK)
+        nc.vector.tensor_copy(first.rearrange("p (s h) -> p s h", h=2)[:, :, 0], pair_words[2][:].indirect(entries(0, G)))
+        nc.vector.tensor_copy(first_values[:, :, 2], x_row[0][:].indirect(entries(0, G)))
+        quantise(0, 0, G, woven0[0])
+        nc.vector.tensor_copy(first_values[:, :, 3], x_row[1][:].indirect(entries(0, G)))
+        quantise(1, 0, G, first)
+
+        rounded_row = [keep.tile([P, T], BF16, name=f"rounded_row{e}") for e in range(2)]
+        for e in range(2):
+            nc.scalar.copy(rounded_row[e][:], x_row[e][:])
+
+        woven1 = keep.tile([P, 2 * LATE], U32, name="woven1", align_bytes=64)
+
+        def half(h, s0, s1):
+            return halves1[:, h * LATE + s0 - G : h * LATE + s1 - G]
+
+        def gather_low(s0, s1):
+            nc.vector.tensor_copy(half(0, s0, s1), pair_words[2][:].indirect(entries(s0, s1)))
+
+        def gather_high(s0, s1):
+            high = half(1, s0, s1).bitcast(BF16).rearrange("p (s e) -> p s e", e=2)
+            for e in range(2):
+                nc.scalar.activation(high[:, :, e], rounded_row[e][:].indirect(entries(s0, s1)), ACT.Copy)
+            both = halves1[:].rearrange("p (h s) -> p s h", h=2)
+            woven = woven1[:, 2 * (s0 - G) : 2 * (s1 - G)].rearrange("p (s h) -> p s h", h=2)
+            nc.scalar.copy(woven, both[:, s0 - G : s1 - G, :])
+
         y_sb = [keep.tile([P, S], F32, name=f"y_sb{t}") for t in range(N_TILES)]
 
-        def experts(t, s0, s1):
+        def experts(t, s0, s1, relu=None):
             acc = psum.tile([P, s1 - s0], F32, name="acc")
-            relu = work.tile([P, s1 - s0], F32, name="relu")
+            if relu is None:
+                relu_tile = work.tile([P, s1 - s0], F32, name="relu_tile")
+                relu = relu_tile[:]
             columns = {e: slice(e * C - s0, (e + 1) * C - s0) for e in range(s0 // C, s1 // C)}
             for e, local in columns.items():
                 slots = slice(e * C, (e + 1) * C)
@@ -166,29 +186,56 @@ def tile_moe_two_lin_relu2_kernel(tc, xT, w_words, w_scales, b, gate, offs, dst,
                         out=acc[:, local],
                         lhsT=w_sb[e // 2][:, PASSES * (e % 2) + a, 2 * t * P : 2 * (t + 1) * P].bitcast(E2M1X4),
                         lhsT_scale=w_scale_sb[:, PASSES * e + a, t * P : (t + 1) * P],
-                        rhs=slot_words[a][:, slots].bitcast(E4M3X4),
-                        rhs_scale=slot_scales[a][:, slots],
+                        rhs=codes[a][:, slots].bitcast(E4M3X4),
+                        rhs_scale=scales[a][:, slots],
                         start=(a == 0),
                         stop=(a == PASSES - 1),
                     )
             for e, local in columns.items():
                 nc.scalar.activation(relu[:, local], acc[:, local], ACT.Relu, bias=b_sb[:, t, e : e + 1])
-            nc.scalar.activation(y_sb[t][:, s0:s1], relu[:], ACT.Square)
+            nc.scalar.activation(y_sb[t][:, s0:s1], relu, ACT.Square)
 
         def scatter(t, s0, s1):
             window = out_sb[t][:].indirect(dst_sb[:, s0 // LIST : s1 // LIST])
             nc.vector.tensor_tensor(window, y_sb[t][:, s0:s1], gate_sb[:, s0:s1], MULT)
 
-        early_tiles = range(N_TILES // 2)
+        gather_low(G, 2 * G)
+        gather_low(2 * G, S)
+        quantise(0, G, 2 * G, woven0[G])
+
+        experts(0, 0, C)
+        experts(0, C, G)
+        experts(1, 0, G, half(1, G, 2 * G).bitcast(F32))
+        gather_high(G, 2 * G)
+        experts(2, 0, G)
+        experts(3, 0, G, woven0[2 * G][:, 0:G].bitcast(F32))
+        weave0(2 * G, 3 * G)
         for t in range(N_TILES):
-            experts(t, 0, FIRST)
-            scatter(t, 0, FIRST)
-        for t in early_tiles:
-            experts(t, FIRST, HALF)
-            scatter(t, FIRST, HALF)
+            scatter(t, 0, G)
+            if t == 1:
+                quantise(1, G, 2 * G, woven1[:, 0 : 2 * G])
+        experts(0, G, 2 * G)
+        experts(1, G, 2 * G, half(1, 2 * G, 3 * G).bitcast(F32))
+        gather_high(2 * G, 3 * G)
+        experts(2, G, 2 * G)
+        experts(3, G, 2 * G, woven0[3 * G][:, 0:G].bitcast(F32))
+        weave0(3 * G, S)
+        quantise(0, 2 * G, 3 * G, woven0[2 * G])
         for t in range(N_TILES):
-            if t not in early_tiles:
-                experts(t, FIRST, HALF)
-            experts(t, HALF, S)
-            scatter(t, HALF if t in early_tiles else FIRST, S)
+            scatter(t, G, 2 * G)
+            if t == 1:
+                quantise(1, 2 * G, 3 * G, woven1[:, 2 * G : 4 * G])
+        experts(0, 2 * G, 3 * G, half(1, 3 * G, S).bitcast(F32))
+        gather_high(3 * G, S)
+        quantise(0, 3 * G, S, woven0[3 * G])
+        for t in range(N_TILES - 1):
+            if t > 0:
+                experts(t, 2 * G, 3 * G)
+            scatter(t, 2 * G, 3 * G)
+            if t == 0:
+                quantise(1, 3 * G, S, woven1[:, 4 * G : 6 * G])
+        for t in range(N_TILES):
+            s0 = 3 * G if t < N_TILES - 1 else 2 * G
+            experts(t, s0, S)
+            scatter(t, s0, S)
             nc.sync.dma_start(out=out[t * P : (t + 1) * P, :], in_=out_sb[t][:])

@@ -28,7 +28,7 @@ MULT = mybir.AluOpType.mult
 G = 2 * C
 GROUPS = ((0, G), (G, 2 * G), (2 * G, S))
 T_FIRST = 768
-SCALAR_TOKENS = ((0, 384), (768, 128), (768, 128))
+SCALAR_TOKENS = ((256, 256), (640, 128), (768, 128))
 
 
 def tile_moe_two_lin_relu2_kernel(tc, xT, w_words, w_scales, b, gate, offs, dst, out):
@@ -42,9 +42,9 @@ def tile_moe_two_lin_relu2_kernel(tc, xT, w_words, w_scales, b, gate, offs, dst,
         dst_sb = keep.tile([P, S // LIST], U16, name="dst_sb")
         b_sb = keep.tile([P, N_TILES, E], F32, name="b_sb")
         gate_sb = keep.tile([P, S], F32, name="gate_sb")
-        w_sb = [keep.tile([P, 2 * PASSES, 2 * N], U8, name=f"w_sb{pair}", align_bytes=64) for pair in range(E // 2)]
+        w_sb = {pair: keep.tile([P, 2 * PASSES, 2 * N], U8, name=f"w_sb{pair}", align_bytes=64) for pair in range(1, E // 2)}
         w_scale_sb = keep.tile([P, E * PASSES, N], U8, name="w_scale_sb", align_bytes=64)
-        out_sb = [keep.tile([P, T], F32, name=f"out_sb{t}") for t in range(N_TILES)]
+        out_sb = {t: keep.tile([P, T], F32, name=f"out_sb{t}") for t in (0, 1, 3)}
 
         def rows(a):
             return xT[a * K_PASS : (a + 1) * K_PASS, :].rearrange("(p d) t -> p (d t)", d=PACK)
@@ -67,10 +67,9 @@ def tile_moe_two_lin_relu2_kernel(tc, xT, w_words, w_scales, b, gate, offs, dst,
             x_row.append(x)
 
         nc.gpsimd.memset(w_scale_sb[:].rearrange("p g n -> p (g n)").bitcast(I32), 0)
-        for t in range(N_TILES // 2):
+        for t in (0, 3):
             nc.vector.memset(out_sb[t][:], 0.0)
-        for t in range(N_TILES // 2, N_TILES):
-            nc.scalar.activation(out_sb[t][:], out_sb[0][:], ACT.Square)
+        nc.scalar.activation(out_sb[1][:], out_sb[0][:], ACT.Square)
 
         def load_weights(g):
             words = w_words[2 * g : 2 * g + 2].rearrange("e a p c -> p (e a) c")
@@ -86,11 +85,19 @@ def tile_moe_two_lin_relu2_kernel(tc, xT, w_words, w_scales, b, gate, offs, dst,
         def load_gate(s0, s1):
             nc.sync.dma_start(gate_sb[:, s0:s1], gate[0:P, s0:s1])
 
+        def load_first_weights(t0, t1):
+            words = w_words[0:2, :, :, 2 * t0 * P : 2 * t1 * P].rearrange("e a p c -> p (e a) c")
+            tile = keep.tile([P, 2 * PASSES, 2 * (t1 - t0) * P], U8, name=f"w_first{t0}", align_bytes=64)
+            nc.sync.dma_start(out=tile[:].bitcast(I32), in_=words.bitcast(I32))
+            return [tile[:, :, 2 * (t - t0) * P : 2 * (t - t0 + 1) * P] for t in range(t0, t1)]
+
         load_weight_scales(0, 2)
-        load_weights(0)
+        w_first = load_first_weights(0, 1)
         nc.sync.dma_start(out=b_sb[:], in_=b.rearrange("(t p) e -> p t e", p=P))
+        w_first = w_first + load_first_weights(1, 2)
         nc.sync.dma_start(dst_sb[:], dst)
         load_gate(0, G)
+        w_first = w_first + load_first_weights(2, N_TILES)
         load_weight_scales(2, E)
         load_weights(1)
         load_gate(G, S)
@@ -125,6 +132,9 @@ def tile_moe_two_lin_relu2_kernel(tc, xT, w_words, w_scales, b, gate, offs, dst,
         for u in range(2):
             round_pair(u)
             nc.vector.tensor_copy(halves0[:, u, :], pair_words[u][:].indirect(entries(0, S)))
+            if u == 0:
+                out_sb[2] = keep.tile([P, T], F32, name="x_pair0", align_bytes=64)
+                nc.scalar.activation(out_sb[2][:], out_sb[0][:], ACT.Square)
         round_pair(2)
         woven0_late = keep.tile([P, S], U32, name="woven0_late", align_bytes=64)
         woven0 = {
@@ -181,10 +191,11 @@ def tile_moe_two_lin_relu2_kernel(tc, xT, w_words, w_scales, b, gate, offs, dst,
             columns = {e: slice(e * C - s0, (e + 1) * C - s0) for e in range(s0 // C, s1 // C)}
             for e, local in columns.items():
                 slots = slice(e * C, (e + 1) * C)
+                words = w_first[t] if e < 2 else w_sb[e // 2][:, :, 2 * t * P : 2 * (t + 1) * P]
                 for a in range(PASSES):
                     nc.tensor.matmul_mx(
                         out=acc[:, local],
-                        lhsT=w_sb[e // 2][:, PASSES * (e % 2) + a, 2 * t * P : 2 * (t + 1) * P].bitcast(E2M1X4),
+                        lhsT=words[:, PASSES * (e % 2) + a, :].bitcast(E2M1X4),
                         lhsT_scale=w_scale_sb[:, PASSES * e + a, t * P : (t + 1) * P],
                         rhs=codes[a][:, slots].bitcast(E4M3X4),
                         rhs_scale=scales[a][:, slots],
@@ -205,34 +216,27 @@ def tile_moe_two_lin_relu2_kernel(tc, xT, w_words, w_scales, b, gate, offs, dst,
 
         experts(0, 0, C)
         experts(0, C, G)
-        experts(1, 0, G, half(1, G, 2 * G).bitcast(F32))
-        gather_high(G, 2 * G)
-        experts(2, 0, G)
-        experts(3, 0, G, woven0[2 * G][:, 0:G].bitcast(F32))
-        weave0(2 * G, 3 * G)
-        for t in range(N_TILES):
-            scatter(t, 0, G)
-            if t == 1:
-                quantise(1, G, 2 * G, woven1[:, 0 : 2 * G])
-        experts(0, G, 2 * G)
-        experts(1, G, 2 * G, half(1, 2 * G, 3 * G).bitcast(F32))
-        gather_high(2 * G, 3 * G)
-        experts(2, G, 2 * G)
-        experts(3, G, 2 * G, woven0[3 * G][:, 0:G].bitcast(F32))
-        weave0(3 * G, S)
-        quantise(0, 2 * G, 3 * G, woven0[2 * G])
-        for t in range(N_TILES):
-            scatter(t, G, 2 * G)
-            if t == 1:
-                quantise(1, 2 * G, 3 * G, woven1[:, 2 * G : 4 * G])
-        experts(0, 2 * G, 3 * G, half(1, 3 * G, S).bitcast(F32))
+        for g in range(2):
+            s0, s1, s2 = g * G, (g + 1) * G, (g + 2) * G
+            if g > 0:
+                experts(0, s0, s1)
+            experts(1, s0, s1, woven0[s2][:, 0:G].bitcast(F32))
+            experts(2, s0, s1, half(1, s1, s2).bitcast(F32))
+            gather_high(s1, s2)
+            experts(3, s0, s1, half(0, s1, s2).bitcast(F32))
+            weave0(s2, s2 + G)
+            for t in range(N_TILES):
+                scatter(t, s0, s1)
+                if t == 2:
+                    quantise(1, s1, s2, woven1[:, 2 * s0 : 2 * s1])
+            quantise(0, s2, s2 + G, woven0[s2])
+        experts(0, 2 * G, 3 * G)
+        experts(1, 2 * G, 3 * G, half(1, 3 * G, S).bitcast(F32))
         gather_high(3 * G, S)
-        quantise(0, 3 * G, S, woven0[3 * G])
+        experts(2, 2 * G, 3 * G, half(0, 3 * G, S).bitcast(F32))
         for t in range(N_TILES - 1):
-            if t > 0:
-                experts(t, 2 * G, 3 * G)
             scatter(t, 2 * G, 3 * G)
-            if t == 0:
+            if t == 1:
                 quantise(1, 3 * G, S, woven1[:, 4 * G : 6 * G])
         for t in range(N_TILES):
             s0 = 3 * G if t < N_TILES - 1 else 2 * G

@@ -28,7 +28,7 @@ MULT = mybir.AluOpType.mult
 G = 2 * C
 GROUPS = ((0, G), (G, 2 * G), (2 * G, S))
 T_FIRST = 768
-SCALAR_TOKENS = ((256, 256), (640, 128), (768, 128))
+SCALAR_TOKENS = ((256, 256), (640, 128), (768, 512))
 
 
 def tile_moe_two_lin_relu2_kernel(tc, xT, w_words, w_scales, b, gate, offs, dst, out):
@@ -50,21 +50,31 @@ def tile_moe_two_lin_relu2_kernel(tc, xT, w_words, w_scales, b, gate, offs, dst,
             return xT[a * K_PASS : (a + 1) * K_PASS, :].rearrange("(p d) t -> p (d t)", d=PACK)
 
         x_pair = []
-        for u in range(3):
-            a, h = divmod(u, 2)
+        x_row = []
+
+        def load_row(d):
+            x = keep.tile([P, T], F32, name=f"x_row{d}", align_bytes=64)
+            nc.sync.dma_start(out=x[:], in_=rows(1)[:, d * T : (d + 1) * T])
+            x_row.append(x)
+
+        for u in range(2):
             x = keep.tile([P, 2 * T], F32, name=f"x_pair{u}", align_bytes=64)
-            run = rows(a)[:, 2 * h * T : 2 * (h + 1) * T]
+            run = rows(0)[:, 2 * u * T : 2 * (u + 1) * T]
             nc.sync.dma_start(out=x[:, 0 : T + T_FIRST], in_=run[:, 0 : T + T_FIRST])
             nc.sync.dma_start(out=x[:, T + T_FIRST : 2 * T], in_=run[:, T + T_FIRST : 2 * T])
             if u == 0:
                 nc.sync.dma_start(offs_sb[:], offs)
-            x_pair.append(x[:].rearrange("p (e t) -> p t e", e=2))
-            last_pair = x
-        x_row = []
-        for d in (2, 3):
-            x = keep.tile([P, T], F32, name=f"x_row{d}")
-            nc.sync.dma_start(out=x[:], in_=rows(1)[:, d * T : (d + 1) * T])
-            x_row.append(x)
+            both = x[:].rearrange("p (e t) -> p t e", e=2)
+            x_pair.append((both[:, 0:T_FIRST, :], both[:, T_FIRST:T, :]))
+        load_row(2)
+        parts = []
+        for t0 in (0, T_FIRST):
+            last_part = keep.tile([P, 2, T_FIRST], F32, name=f"x_part{t0}", align_bytes=64)
+            run = rows(1)[:, 0 : 2 * T].rearrange("p (e t) -> p e t", e=2)
+            nc.sync.dma_start(out=last_part[:], in_=run[:, :, t0 : t0 + T_FIRST])
+            parts.append(last_part[:].rearrange("p e t -> p t e"))
+        x_pair.append(parts)
+        load_row(3)
 
         nc.gpsimd.memset(w_scale_sb[:].rearrange("p g n -> p (g n)").bitcast(I32), 0)
         for t in (0, 3):
@@ -98,9 +108,10 @@ def tile_moe_two_lin_relu2_kernel(tc, xT, w_words, w_scales, b, gate, offs, dst,
         nc.sync.dma_start(dst_sb[:], dst)
         load_gate(0, G)
         w_first = w_first + load_first_weights(2, N_TILES)
-        load_weight_scales(2, E)
+        load_weight_scales(2, 4)
         load_weights(1)
         load_gate(G, S)
+        load_weight_scales(4, E)
         load_weights(2)
         load_weights(3)
 
@@ -108,64 +119,58 @@ def tile_moe_two_lin_relu2_kernel(tc, xT, w_words, w_scales, b, gate, offs, dst,
 
         def round_pair(u):
             rounded = pair_words[u][:].bitcast(BF16).rearrange("p (t e) -> p t e", e=2)
-            for (t0, t1), scalar_tokens in zip(((0, T_FIRST), (T_FIRST, T)), SCALAR_TOKENS[u]):
-                cut = t0 + scalar_tokens
-                if t0 < cut:
-                    nc.scalar.copy(rounded[:, t0:cut, :], x_pair[u][:, t0:cut, :])
-                if cut < t1:
-                    nc.vector.tensor_copy(rounded[:, cut:t1, :], x_pair[u][:, cut:t1, :])
+            for t0, x, cut in zip((0, T_FIRST), x_pair[u], SCALAR_TOKENS[u]):
+                nc.scalar.copy(rounded[:, t0 : t0 + cut, :], x[:, 0:cut, :])
+                if cut < T_FIRST:
+                    nc.vector.tensor_copy(rounded[:, t0 + cut : t0 + T_FIRST, :], x[:, cut:T_FIRST, :])
 
         def entries(s0, s1):
             return offs_sb[:, s0 // LIST : s1 // LIST]
 
-        codes = [keep.tile([P, S], U32, name=f"codes{a}", align_bytes=64) for a in range(PASSES)]
+        HALF = S // 2
+        LATE = S - G
+        codes0_early = keep.tile([P, HALF], U32, name="codes0_early", align_bytes=64)
+        codes1 = keep.tile([P, S], U32, name="codes1", align_bytes=64)
+        codes = {(0, 0): codes0_early[:], (1, 0): codes1[:, 0:HALF], (1, 1): codes1[:, HALF:S]}
         scales = [keep.tile([P, S], U8, name=f"scales{a}", align_bytes=64) for a in range(PASSES)]
 
+        def slot_codes(a, s0, s1):
+            return codes[a, s0 // HALF][:, s0 % HALF : s0 % HALF + s1 - s0].bitcast(E4M3X4)
+
         def quantise(a, s0, s1, woven):
-            nc.vector.quantize_mx(
-                out=codes[a][:, s0:s1].bitcast(E4M3X4),
-                scales=scales[a][:, s0:s1],
-                in_=woven.bitcast(BF16),
-            )
+            nc.vector.quantize_mx(out=slot_codes(a, s0, s1), scales=scales[a][:, s0:s1], in_=woven.bitcast(BF16))
 
-        halves0 = keep.tile([P, 2, S], U32, name="halves0")
-        for u in range(2):
-            round_pair(u)
-            nc.vector.tensor_copy(halves0[:, u, :], pair_words[u][:].indirect(entries(0, S)))
-            if u == 0:
-                out_sb[2] = keep.tile([P, T], F32, name="x_pair0", align_bytes=64)
-                nc.scalar.activation(out_sb[2][:], out_sb[0][:], ACT.Square)
-        round_pair(2)
-        woven0_late = keep.tile([P, S], U32, name="woven0_late", align_bytes=64)
-        woven0 = {
-            0: last_pair[:, 0 : 2 * G].bitcast(U32),
-            G: last_pair[:, T : T + 2 * G].bitcast(U32),
-            2 * G: woven0_late[:, 0 : 2 * G],
-            3 * G: woven0_late[:, 2 * G : 4 * G],
-        }
-
-        def weave0(s0, s1):
-            woven = woven0[s0].rearrange("p (s h) -> p s h", h=2)
-            nc.scalar.copy(woven, halves0[:, :, s0:s1].rearrange("p h s -> p s h"))
-
-        for s0, s1 in GROUPS[:2]:
-            weave0(s0, s1)
-
-        LATE = S - G
         halves1 = keep.tile([P, 2 * LATE], U32, name="halves1", align_bytes=64)
+        woven1 = keep.tile([P, 2 * LATE], U32, name="woven1", align_bytes=64)
         first = halves1[:, 0 : 2 * G]
         first_values = first.bitcast(BF16).rearrange("p (s d) -> p s d", d=PACK)
-        nc.vector.tensor_copy(first.rearrange("p (s h) -> p s h", h=2)[:, :, 0], pair_words[2][:].indirect(entries(0, G)))
+        rounded_row = [keep.tile([P, T], BF16, name=f"rounded_row{e}") for e in range(2)]
+
+        halves0 = keep.tile([P, 2, S], U32, name="halves0")
+        round_pair(0)
+        nc.vector.tensor_copy(halves0[:, 0, :], pair_words[0][:].indirect(entries(0, S)))
+        out_sb[2] = keep.tile([P, T], F32, name="x_pair0", align_bytes=64)
+        nc.scalar.activation(out_sb[2][:], out_sb[0][:], ACT.Square)
+        round_pair(1)
+        nc.vector.tensor_copy(halves0[:, 1, :], pair_words[1][:].indirect(entries(0, S)))
+        nc.scalar.copy(rounded_row[0][:], x_row[0][:])
         nc.vector.tensor_copy(first_values[:, :, 2], x_row[0][:].indirect(entries(0, G)))
-        quantise(0, 0, G, woven0[0])
+        woven0_early = keep.tile([P, S], U32, name="woven0_early", align_bytes=64)
+        nc.vector.tensor_copy(
+            woven0_early[:].rearrange("p (s h) -> p s h", h=2).bitcast(I32),
+            halves0[:, :, 0:HALF].bitcast(I32).rearrange("p h s -> p s h"),
+        )
+        round_pair(2)
+        woven0_late = keep.tile([P, S], U32, name=f"x_part{T_FIRST}", align_bytes=64)
+        nc.scalar.copy(
+            woven0_late[:].rearrange("p (s h) -> p s h", h=2), halves0[:, :, HALF:S].rearrange("p h s -> p s h")
+        )
+        quantise(0, 0, HALF, woven0_early[:])
+
+        nc.vector.tensor_copy(first.rearrange("p (s h) -> p s h", h=2)[:, :, 0], pair_words[2][:].indirect(entries(0, G)))
         nc.vector.tensor_copy(first_values[:, :, 3], x_row[1][:].indirect(entries(0, G)))
         quantise(1, 0, G, first)
-
-        rounded_row = [keep.tile([P, T], BF16, name=f"rounded_row{e}") for e in range(2)]
-        for e in range(2):
-            nc.scalar.copy(rounded_row[e][:], x_row[e][:])
-
-        woven1 = keep.tile([P, 2 * LATE], U32, name="woven1", align_bytes=64)
+        nc.scalar.copy(rounded_row[1][:], x_row[1][:])
 
         def half(h, s0, s1):
             return halves1[:, h * LATE + s0 - G : h * LATE + s1 - G]
@@ -197,7 +202,7 @@ def tile_moe_two_lin_relu2_kernel(tc, xT, w_words, w_scales, b, gate, offs, dst,
                         out=acc[:, local],
                         lhsT=words[:, PASSES * (e % 2) + a, :].bitcast(E2M1X4),
                         lhsT_scale=w_scale_sb[:, PASSES * e + a, t * P : (t + 1) * P],
-                        rhs=codes[a][:, slots].bitcast(E4M3X4),
+                        rhs=slot_codes(a, e * C, (e + 1) * C),
                         rhs_scale=scales[a][:, slots],
                         start=(a == 0),
                         stop=(a == PASSES - 1),
@@ -210,36 +215,32 @@ def tile_moe_two_lin_relu2_kernel(tc, xT, w_words, w_scales, b, gate, offs, dst,
             window = out_sb[t][:].indirect(dst_sb[:, s0 // LIST : s1 // LIST])
             nc.vector.tensor_tensor(window, y_sb[t][:, s0:s1], gate_sb[:, s0:s1], MULT)
 
-        gather_low(G, 2 * G)
-        gather_low(2 * G, S)
-        quantise(0, G, 2 * G, woven0[G])
+        gather_low(G, S)
+        codes0_late = keep.tile([P, HALF], U32, name="x_row3", align_bytes=64)
+        codes[0, 1] = codes0_late[:]
+        quantise(0, HALF, S, woven0_late[:])
 
-        experts(0, 0, C)
-        experts(0, C, G)
         for g in range(2):
             s0, s1, s2 = g * G, (g + 1) * G, (g + 2) * G
-            if g > 0:
+            if g == 0:
+                experts(0, 0, C)
+                experts(0, C, G)
+            else:
                 experts(0, s0, s1)
-            experts(1, s0, s1, woven0[s2][:, 0:G].bitcast(F32))
-            experts(2, s0, s1, half(1, s1, s2).bitcast(F32))
+            experts(1, s0, s1, half(1, s1, s2).bitcast(F32))
             gather_high(s1, s2)
-            experts(3, s0, s1, half(0, s1, s2).bitcast(F32))
-            weave0(s2, s2 + G)
+            experts(2, s0, s1, half(0, s1, s2).bitcast(F32))
+            experts(3, s0, s1, half(1, 3 * G, S).bitcast(F32) if g == 1 else None)
             for t in range(N_TILES):
                 scatter(t, s0, s1)
-                if t == 2:
+                if t == 1:
                     quantise(1, s1, s2, woven1[:, 2 * s0 : 2 * s1])
-            quantise(0, s2, s2 + G, woven0[s2])
-        experts(0, 2 * G, 3 * G)
-        experts(1, 2 * G, 3 * G, half(1, 3 * G, S).bitcast(F32))
         gather_high(3 * G, S)
-        experts(2, 2 * G, 3 * G, half(0, 3 * G, S).bitcast(F32))
-        for t in range(N_TILES - 1):
-            scatter(t, 2 * G, 3 * G)
-            if t == 1:
-                quantise(1, 3 * G, S, woven1[:, 4 * G : 6 * G])
-        for t in range(N_TILES):
-            s0 = 3 * G if t < N_TILES - 1 else 2 * G
+        experts(0, 2 * G, 3 * G, half(0, 3 * G, S).bitcast(F32))
+        quantise(1, 3 * G, S, woven1[:, 4 * G : 6 * G])
+        scatter(0, 2 * G, 3 * G)
+        for t in (1, 2, 0, 3):
+            s0 = 3 * G if t == 0 else 2 * G
             experts(t, s0, S)
             scatter(t, s0, S)
             nc.sync.dma_start(out=out[t * P : (t + 1) * P, :], in_=out_sb[t][:])

@@ -28,7 +28,7 @@ MULT = mybir.AluOpType.mult
 G = 2 * C
 GROUPS = ((0, G), (G, 2 * G), (2 * G, S))
 T_FIRST = 768
-SCALAR_TOKENS = ((256, 256), (640, 128), (768, 512))
+SCALAR_TOKENS = ((256, 256), (480, 256), (768, 288))
 
 
 def tile_moe_two_lin_relu2_kernel(tc, xT, w_words, w_scales, b, gate, offs, dst, out):
@@ -54,7 +54,9 @@ def tile_moe_two_lin_relu2_kernel(tc, xT, w_words, w_scales, b, gate, offs, dst,
 
         def load_row(d):
             x = keep.tile([P, T], F32, name=f"x_row{d}", align_bytes=64)
-            nc.sync.dma_start(out=x[:], in_=rows(1)[:, d * T : (d + 1) * T])
+            width = T // 2 if d == 2 else T
+            for t0 in range(0, T, width):
+                nc.sync.dma_start(out=x[:, t0 : t0 + width], in_=rows(1)[:, d * T + t0 : d * T + t0 + width])
             x_row.append(x)
 
         for u in range(2):
@@ -129,13 +131,11 @@ def tile_moe_two_lin_relu2_kernel(tc, xT, w_words, w_scales, b, gate, offs, dst,
 
         HALF = S // 2
         LATE = S - G
-        codes0_early = keep.tile([P, HALF], U32, name="codes0_early", align_bytes=64)
-        codes1 = keep.tile([P, S], U32, name="codes1", align_bytes=64)
-        codes = {(0, 0): codes0_early[:], (1, 0): codes1[:, 0:HALF], (1, 1): codes1[:, HALF:S]}
+        codes = [keep.tile([P, S], U32, name=f"codes{a}", align_bytes=64) for a in range(PASSES)]
         scales = [keep.tile([P, S], U8, name=f"scales{a}", align_bytes=64) for a in range(PASSES)]
 
         def slot_codes(a, s0, s1):
-            return codes[a, s0 // HALF][:, s0 % HALF : s0 % HALF + s1 - s0].bitcast(E4M3X4)
+            return codes[a][:, s0:s1].bitcast(E4M3X4)
 
         def quantise(a, s0, s1, woven):
             nc.vector.quantize_mx(out=slot_codes(a, s0, s1), scales=scales[a][:, s0:s1], in_=woven.bitcast(BF16))
@@ -153,19 +153,18 @@ def tile_moe_two_lin_relu2_kernel(tc, xT, w_words, w_scales, b, gate, offs, dst,
         nc.scalar.activation(out_sb[2][:], out_sb[0][:], ACT.Square)
         round_pair(1)
         nc.vector.tensor_copy(halves0[:, 1, :], pair_words[1][:].indirect(entries(0, S)))
-        nc.scalar.copy(rounded_row[0][:], x_row[0][:])
-        nc.vector.tensor_copy(first_values[:, :, 2], x_row[0][:].indirect(entries(0, G)))
-        woven0_early = keep.tile([P, S], U32, name="woven0_early", align_bytes=64)
-        nc.vector.tensor_copy(
-            woven0_early[:].rearrange("p (s h) -> p s h", h=2).bitcast(I32),
-            halves0[:, :, 0:HALF].bitcast(I32).rearrange("p h s -> p s h"),
-        )
+        for t0 in (0, T // 2):
+            nc.scalar.copy(rounded_row[0][:, t0 : t0 + T // 2], x_row[0][:, t0 : t0 + T // 2])
+        nc.scalar.activation(first_values[:, :, 2], rounded_row[0][:].indirect(entries(0, G)), ACT.Copy)
+        woven0 = keep.tile([P, 2 * S], U32, name="woven0", align_bytes=64)
+        for s0 in (0, HALF):
+            nc.vector.tensor_copy(
+                woven0[:, 2 * s0 : 2 * s0 + S].rearrange("p (s h) -> p s h", h=2).bitcast(I32),
+                halves0[:, :, s0 : s0 + HALF].bitcast(I32).rearrange("p h s -> p s h"),
+            )
+        for s0 in (0, HALF):
+            quantise(0, s0, s0 + HALF, woven0[:, 2 * s0 : 2 * s0 + S])
         round_pair(2)
-        woven0_late = keep.tile([P, S], U32, name=f"x_part{T_FIRST}", align_bytes=64)
-        nc.scalar.copy(
-            woven0_late[:].rearrange("p (s h) -> p s h", h=2), halves0[:, :, HALF:S].rearrange("p h s -> p s h")
-        )
-        quantise(0, 0, HALF, woven0_early[:])
 
         nc.vector.tensor_copy(first.rearrange("p (s h) -> p s h", h=2)[:, :, 0], pair_words[2][:].indirect(entries(0, G)))
         nc.vector.tensor_copy(first_values[:, :, 3], x_row[1][:].indirect(entries(0, G)))
@@ -216,9 +215,6 @@ def tile_moe_two_lin_relu2_kernel(tc, xT, w_words, w_scales, b, gate, offs, dst,
             nc.vector.tensor_tensor(window, y_sb[t][:, s0:s1], gate_sb[:, s0:s1], MULT)
 
         gather_low(G, S)
-        codes0_late = keep.tile([P, HALF], U32, name="x_row3", align_bytes=64)
-        codes[0, 1] = codes0_late[:]
-        quantise(0, HALF, S, woven0_late[:])
 
         for g in range(2):
             s0, s1, s2 = g * G, (g + 1) * G, (g + 2) * G

@@ -26,9 +26,11 @@ ACT = mybir.ActivationFunctionType
 MULT = mybir.AluOpType.mult
 
 G = 2 * C
-GROUPS = ((0, G), (G, 2 * G), (2 * G, S))
-T_FIRST = 768
-SCALAR_TOKENS = ((256, 256), (480, 256), (768, 288))
+LATE = S - G
+S_HALF = S // 2
+T_HALF = T // 2
+
+SCALAR_TOKENS = ((256, 256), (480, 256), (T_HALF, 320))
 
 
 def tile_moe_two_lin_relu2_kernel(tc, xT, w_words, w_scales, b, gate, offs, dst, out):
@@ -42,41 +44,40 @@ def tile_moe_two_lin_relu2_kernel(tc, xT, w_words, w_scales, b, gate, offs, dst,
         dst_sb = keep.tile([P, S // LIST], U16, name="dst_sb")
         b_sb = keep.tile([P, N_TILES, E], F32, name="b_sb")
         gate_sb = keep.tile([P, S], F32, name="gate_sb")
-        w_sb = {pair: keep.tile([P, 2 * PASSES, 2 * N], U8, name=f"w_sb{pair}", align_bytes=64) for pair in range(1, E // 2)}
+        w_sb = {g: keep.tile([P, 2 * PASSES, 2 * N], U8, name=f"w_sb{g}", align_bytes=64) for g in range(1, S // G)}
         w_scale_sb = keep.tile([P, E * PASSES, N], U8, name="w_scale_sb", align_bytes=64)
         out_sb = {t: keep.tile([P, T], F32, name=f"out_sb{t}") for t in (0, 1, 3)}
 
-        def rows(a):
+        def pass_rows(a):
             return xT[a * K_PASS : (a + 1) * K_PASS, :].rearrange("(p d) t -> p (d t)", d=PACK)
 
-        x_pair = []
-        x_row = []
-
-        def load_row(d):
+        def load_row(d, width):
             x = keep.tile([P, T], F32, name=f"x_row{d}", align_bytes=64)
-            width = T // 2 if d == 2 else T
             for t0 in range(0, T, width):
-                nc.sync.dma_start(out=x[:, t0 : t0 + width], in_=rows(1)[:, d * T + t0 : d * T + t0 + width])
-            x_row.append(x)
+                nc.sync.dma_start(out=x[:, t0 : t0 + width], in_=pass_rows(1)[:, d * T + t0 : d * T + t0 + width])
+            return x
 
-        for u in range(2):
-            x = keep.tile([P, 2 * T], F32, name=f"x_pair{u}", align_bytes=64)
-            run = rows(0)[:, 2 * u * T : 2 * (u + 1) * T]
-            nc.sync.dma_start(out=x[:, 0 : T + T_FIRST], in_=run[:, 0 : T + T_FIRST])
-            nc.sync.dma_start(out=x[:, T + T_FIRST : 2 * T], in_=run[:, T + T_FIRST : 2 * T])
-            if u == 0:
+        x_pairs = []
+        for h in range(2):
+            x = keep.tile([P, 2 * T], F32, name=f"x_pair{h}", align_bytes=64)
+            run = pass_rows(0)[:, 2 * h * T : 2 * (h + 1) * T]
+            nc.sync.dma_start(out=x[:, 0 : T + T_HALF], in_=run[:, 0 : T + T_HALF])
+            nc.sync.dma_start(out=x[:, T + T_HALF : 2 * T], in_=run[:, T + T_HALF : 2 * T])
+            if h == 0:
                 nc.sync.dma_start(offs_sb[:], offs)
-            both = x[:].rearrange("p (e t) -> p t e", e=2)
-            x_pair.append((both[:, 0:T_FIRST, :], both[:, T_FIRST:T, :]))
-        load_row(2)
-        parts = []
-        for t0 in (0, T_FIRST):
-            last_part = keep.tile([P, 2, T_FIRST], F32, name=f"x_part{t0}", align_bytes=64)
-            run = rows(1)[:, 0 : 2 * T].rearrange("p (e t) -> p e t", e=2)
-            nc.sync.dma_start(out=last_part[:], in_=run[:, :, t0 : t0 + T_FIRST])
-            parts.append(last_part[:].rearrange("p e t -> p t e"))
-        x_pair.append(parts)
-        load_row(3)
+            by_token = x[:].rearrange("p (e t) -> p t e", e=2)
+            x_pairs.append((by_token[:, 0:T_HALF, :], by_token[:, T_HALF:T, :]))
+        x_row2 = load_row(2, T_HALF)
+
+        pairs1 = keep.tile([P, LATE + T], U32, name="pairs1", align_bytes=64)
+        x_low1 = keep.tile([P, T], F32, name="x_low1", align_bytes=64)
+        low1_rows = pass_rows(1)[:, 0 : 2 * T].rearrange("p (e t) -> p e t", e=2)
+        low1_halves = []
+        for t0, landing in ((0, x_low1[:]), (T_HALF, pairs1[:, LATE : LATE + T].bitcast(F32))):
+            nc.sync.dma_start(out=landing.rearrange("p (e t) -> p e t", e=2), in_=low1_rows[:, :, t0 : t0 + T_HALF])
+            low1_halves.append(landing.rearrange("p (e t) -> p t e", e=2))
+        x_pairs.append(low1_halves)
+        x_row3 = load_row(3, T)
 
         nc.gpsimd.memset(w_scale_sb[:].rearrange("p g n -> p (g n)").bitcast(I32), 0)
         for t in (0, 3):
@@ -87,6 +88,12 @@ def tile_moe_two_lin_relu2_kernel(tc, xT, w_words, w_scales, b, gate, offs, dst,
             words = w_words[2 * g : 2 * g + 2].rearrange("e a p c -> p (e a) c")
             nc.sync.dma_start(out=w_sb[g][:].bitcast(I32), in_=words.bitcast(I32))
 
+        def load_first_weights(t0, t1):
+            words = w_words[0:2, :, :, 2 * t0 * P : 2 * t1 * P].rearrange("e a p c -> p (e a) c")
+            w_part = keep.tile([P, 2 * PASSES, 2 * (t1 - t0) * P], U8, name=f"w_first{t0}", align_bytes=64)
+            nc.sync.dma_start(out=w_part[:].bitcast(I32), in_=words.bitcast(I32))
+            return [w_part[:, :, 2 * (t - t0) * P : 2 * (t - t0 + 1) * P] for t in range(t0, t1)]
+
         def load_weight_scales(e0, e1):
             for r in range(4):
                 nc.sync.dma_start(
@@ -96,12 +103,6 @@ def tile_moe_two_lin_relu2_kernel(tc, xT, w_words, w_scales, b, gate, offs, dst,
 
         def load_gate(s0, s1):
             nc.sync.dma_start(gate_sb[:, s0:s1], gate[0:P, s0:s1])
-
-        def load_first_weights(t0, t1):
-            words = w_words[0:2, :, :, 2 * t0 * P : 2 * t1 * P].rearrange("e a p c -> p (e a) c")
-            tile = keep.tile([P, 2 * PASSES, 2 * (t1 - t0) * P], U8, name=f"w_first{t0}", align_bytes=64)
-            nc.sync.dma_start(out=tile[:].bitcast(I32), in_=words.bitcast(I32))
-            return [tile[:, :, 2 * (t - t0) * P : 2 * (t - t0 + 1) * P] for t in range(t0, t1)]
 
         load_weight_scales(0, 2)
         w_first = load_first_weights(0, 1)
@@ -117,81 +118,78 @@ def tile_moe_two_lin_relu2_kernel(tc, xT, w_words, w_scales, b, gate, offs, dst,
         load_weights(2)
         load_weights(3)
 
-        pair_words = [keep.tile([P, T], U32, name=f"pair_words{u}") for u in range(3)]
-
-        def round_pair(u):
-            rounded = pair_words[u][:].bitcast(BF16).rearrange("p (t e) -> p t e", e=2)
-            for t0, x, cut in zip((0, T_FIRST), x_pair[u], SCALAR_TOKENS[u]):
-                nc.scalar.copy(rounded[:, t0 : t0 + cut, :], x[:, 0:cut, :])
-                if cut < T_FIRST:
-                    nc.vector.tensor_copy(rounded[:, t0 + cut : t0 + T_FIRST, :], x[:, cut:T_FIRST, :])
-
-        def entries(s0, s1):
-            return offs_sb[:, s0 // LIST : s1 // LIST]
-
-        HALF = S // 2
-        LATE = S - G
+        token_pairs = [keep.tile([P, T], U32, name=f"token_pairs{u}") for u in range(len(x_pairs))]
         codes = [keep.tile([P, S], U32, name=f"codes{a}", align_bytes=64) for a in range(PASSES)]
         scales = [keep.tile([P, S], U8, name=f"scales{a}", align_bytes=64) for a in range(PASSES)]
+        woven1 = keep.tile([P, 2 * LATE], U32, name="woven1", align_bytes=64)
+        token_rows = [keep.tile([P, T], BF16, name=f"token_rows{e}") for e in range(2)]
+        pairs0 = keep.tile([P, 2, S], U32, name="pairs0")
 
-        def slot_codes(a, s0, s1):
-            return codes[a][:, s0:s1].bitcast(E4M3X4)
+        def round_pair(u):
+            rounded = token_pairs[u][:].bitcast(BF16).rearrange("p (t e) -> p t e", e=2)
+            for t0, x, cut in zip((0, T_HALF), x_pairs[u], SCALAR_TOKENS[u]):
+                nc.scalar.copy(rounded[:, t0 : t0 + cut, :], x[:, 0:cut, :])
+                if cut < T_HALF:
+                    nc.vector.tensor_copy(rounded[:, t0 + cut : t0 + T_HALF, :], x[:, cut:T_HALF, :])
+
+        def gathered(window, s0, s1):
+            return window[:].indirect(offs_sb[:, s0 // LIST : s1 // LIST])
 
         def quantise(a, s0, s1, woven):
-            nc.vector.quantize_mx(out=slot_codes(a, s0, s1), scales=scales[a][:, s0:s1], in_=woven.bitcast(BF16))
+            nc.vector.quantize_mx(
+                out=codes[a][:, s0:s1].bitcast(E4M3X4), scales=scales[a][:, s0:s1], in_=woven.bitcast(BF16)
+            )
 
-        halves1 = keep.tile([P, 2 * LATE], U32, name="halves1", align_bytes=64)
-        woven1 = keep.tile([P, 2 * LATE], U32, name="woven1", align_bytes=64)
-        first = halves1[:, 0 : 2 * G]
-        first_values = first.bitcast(BF16).rearrange("p (s d) -> p s d", d=PACK)
-        rounded_row = [keep.tile([P, T], BF16, name=f"rounded_row{e}") for e in range(2)]
+        first_woven = pairs1[:, 0 : 2 * G]
+        first_values = first_woven.bitcast(BF16).rearrange("p (s d) -> p s d", d=PACK)
 
-        halves0 = keep.tile([P, 2, S], U32, name="halves0")
         round_pair(0)
-        nc.vector.tensor_copy(halves0[:, 0, :], pair_words[0][:].indirect(entries(0, S)))
+        nc.vector.tensor_copy(pairs0[:, 0, :], gathered(token_pairs[0], 0, S))
         out_sb[2] = keep.tile([P, T], F32, name="x_pair0", align_bytes=64)
         nc.scalar.activation(out_sb[2][:], out_sb[0][:], ACT.Square)
         round_pair(1)
-        nc.vector.tensor_copy(halves0[:, 1, :], pair_words[1][:].indirect(entries(0, S)))
-        for t0 in (0, T // 2):
-            nc.scalar.copy(rounded_row[0][:, t0 : t0 + T // 2], x_row[0][:, t0 : t0 + T // 2])
-        nc.scalar.activation(first_values[:, :, 2], rounded_row[0][:].indirect(entries(0, G)), ACT.Copy)
+        for s0 in (0, S_HALF):
+            nc.vector.tensor_copy(pairs0[:, 1, s0 : s0 + S_HALF], gathered(token_pairs[1], s0, s0 + S_HALF))
+        for t0 in (0, T_HALF):
+            nc.scalar.copy(token_rows[0][:, t0 : t0 + T_HALF], x_row2[:, t0 : t0 + T_HALF])
+        nc.scalar.activation(first_values[:, :, 2], gathered(token_rows[0], 0, G), ACT.Copy)
         woven0 = keep.tile([P, 2 * S], U32, name="woven0", align_bytes=64)
-        for s0 in (0, HALF):
+        for s0 in (0, S_HALF):
             nc.vector.tensor_copy(
                 woven0[:, 2 * s0 : 2 * s0 + S].rearrange("p (s h) -> p s h", h=2).bitcast(I32),
-                halves0[:, :, s0 : s0 + HALF].bitcast(I32).rearrange("p h s -> p s h"),
+                pairs0[:, :, s0 : s0 + S_HALF].bitcast(I32).rearrange("p h s -> p s h"),
             )
-        for s0 in (0, HALF):
-            quantise(0, s0, s0 + HALF, woven0[:, 2 * s0 : 2 * s0 + S])
+        for s0 in (0, S_HALF):
+            quantise(0, s0, s0 + S_HALF, woven0[:, 2 * s0 : 2 * s0 + S])
+
         round_pair(2)
+        nc.vector.tensor_copy(first_woven.rearrange("p (s h) -> p s h", h=2)[:, :, 0], gathered(token_pairs[2], 0, G))
+        nc.vector.tensor_copy(first_values[:, :, 3], gathered(x_row3, 0, G))
+        quantise(1, 0, G, first_woven)
 
-        nc.vector.tensor_copy(first.rearrange("p (s h) -> p s h", h=2)[:, :, 0], pair_words[2][:].indirect(entries(0, G)))
-        nc.vector.tensor_copy(first_values[:, :, 3], x_row[1][:].indirect(entries(0, G)))
-        quantise(1, 0, G, first)
-        nc.scalar.copy(rounded_row[1][:], x_row[1][:])
+        def late_pairs(h, s0, s1):
+            return pairs1[:, h * LATE + s0 - G : h * LATE + s1 - G]
 
-        def half(h, s0, s1):
-            return halves1[:, h * LATE + s0 - G : h * LATE + s1 - G]
+        def late_woven(s0, s1):
+            return woven1[:, 2 * (s0 - G) : 2 * (s1 - G)]
 
-        def gather_low(s0, s1):
-            nc.vector.tensor_copy(half(0, s0, s1), pair_words[2][:].indirect(entries(s0, s1)))
+        def gather_row(e, s0, s1):
+            high = late_pairs(1, s0, s1).bitcast(BF16).rearrange("p (s e) -> p s e", e=2)
+            nc.scalar.activation(high[:, :, e], gathered(token_rows[e], s0, s1), ACT.Copy)
 
-        def gather_high(s0, s1):
-            high = half(1, s0, s1).bitcast(BF16).rearrange("p (s e) -> p s e", e=2)
-            for e in range(2):
-                nc.scalar.activation(high[:, :, e], rounded_row[e][:].indirect(entries(s0, s1)), ACT.Copy)
-            both = halves1[:].rearrange("p (h s) -> p s h", h=2)
-            woven = woven1[:, 2 * (s0 - G) : 2 * (s1 - G)].rearrange("p (s h) -> p s h", h=2)
-            nc.scalar.copy(woven, both[:, s0 - G : s1 - G, :])
+        def weave_late(s0, s1):
+            low_high = pairs1[:, 0 : 2 * LATE].rearrange("p (h s) -> p s h", h=2)
+            nc.scalar.copy(late_woven(s0, s1).rearrange("p (s h) -> p s h", h=2), low_high[:, s0 - G : s1 - G, :])
 
         y_sb = [keep.tile([P, S], F32, name=f"y_sb{t}") for t in range(N_TILES)]
 
-        def experts(t, s0, s1, relu=None):
+        def experts(t, s0, s1, relu_bytes=None):
             acc = psum.tile([P, s1 - s0], F32, name="acc")
-            if relu is None:
+            if relu_bytes is None:
                 relu_tile = work.tile([P, s1 - s0], F32, name="relu_tile")
                 relu = relu_tile[:]
+            else:
+                relu = relu_bytes.bitcast(F32)
             columns = {e: slice(e * C - s0, (e + 1) * C - s0) for e in range(s0 // C, s1 // C)}
             for e, local in columns.items():
                 slots = slice(e * C, (e + 1) * C)
@@ -201,7 +199,7 @@ def tile_moe_two_lin_relu2_kernel(tc, xT, w_words, w_scales, b, gate, offs, dst,
                         out=acc[:, local],
                         lhsT=words[:, PASSES * (e % 2) + a, :].bitcast(E2M1X4),
                         lhsT_scale=w_scale_sb[:, PASSES * e + a, t * P : (t + 1) * P],
-                        rhs=slot_codes(a, e * C, (e + 1) * C),
+                        rhs=codes[a][:, slots].bitcast(E4M3X4),
                         rhs_scale=scales[a][:, slots],
                         start=(a == 0),
                         stop=(a == PASSES - 1),
@@ -214,26 +212,35 @@ def tile_moe_two_lin_relu2_kernel(tc, xT, w_words, w_scales, b, gate, offs, dst,
             window = out_sb[t][:].indirect(dst_sb[:, s0 // LIST : s1 // LIST])
             nc.vector.tensor_tensor(window, y_sb[t][:, s0:s1], gate_sb[:, s0:s1], MULT)
 
-        gather_low(G, S)
+        def prepare_group(s0, s1):
+            for e in range(2):
+                gather_row(e, s0, s1)
+            weave_late(s0, s1)
+            quantise(1, s0, s1, late_woven(s0, s1))
 
-        for g in range(2):
-            s0, s1, s2 = g * G, (g + 1) * G, (g + 2) * G
-            if g == 0:
-                experts(0, 0, C)
-                experts(0, C, G)
-            else:
-                experts(0, s0, s1)
-            experts(1, s0, s1, half(1, s1, s2).bitcast(F32))
-            gather_high(s1, s2)
-            experts(2, s0, s1, half(0, s1, s2).bitcast(F32))
-            experts(3, s0, s1, half(1, 3 * G, S).bitcast(F32) if g == 1 else None)
-            for t in range(N_TILES):
-                scatter(t, s0, s1)
-                if t == 1:
-                    quantise(1, s1, s2, woven1[:, 2 * s0 : 2 * s1])
-        gather_high(3 * G, S)
-        experts(0, 2 * G, 3 * G, half(0, 3 * G, S).bitcast(F32))
-        quantise(1, 3 * G, S, woven1[:, 4 * G : 6 * G])
+        gather_row(0, G, 2 * G)
+        nc.scalar.copy(token_rows[1][:], x_row3[:])
+        gather_row(1, G, 2 * G)
+        nc.vector.tensor_copy(late_pairs(0, G, S), gathered(token_pairs[2], G, S))
+
+        experts(0, 0, C)
+        experts(0, C, G)
+        experts(1, 0, G, late_woven(G, 2 * G)[:, 0:G])
+        weave_late(G, 2 * G)
+        experts(2, 0, G, late_pairs(0, G, 2 * G))
+        experts(3, 0, G, late_pairs(1, 2 * G, 3 * G))
+        for t in range(N_TILES):
+            scatter(t, 0, G)
+            if t == 1:
+                quantise(1, G, 2 * G, late_woven(G, 2 * G))
+        prepare_group(2 * G, 3 * G)
+
+        for t in range(N_TILES):
+            experts(t, G, 2 * G, late_pairs(1, 3 * G, S) if t == N_TILES - 1 else None)
+            scatter(t, G, 2 * G)
+        prepare_group(3 * G, S)
+
+        experts(0, 2 * G, 3 * G)
         scatter(0, 2 * G, 3 * G)
         for t in (1, 2, 0, 3):
             s0 = 3 * G if t == 0 else 2 * G

@@ -26,11 +26,11 @@ ACT = mybir.ActivationFunctionType
 MULT = mybir.AluOpType.mult
 
 G = 2 * C
-LATE = S - G
+GROUPS = S // G
 S_HALF = S // 2
 T_HALF = T // 2
 
-SCALAR_TOKENS = ((256, 256), (480, 256), (T_HALF, 320))
+SCALAR_TOKENS = ((256, 256), (480, 256), (T_HALF, 256))
 
 
 def tile_moe_two_lin_relu2_kernel(tc, xT, w_words, w_scales, b, gate, offs, dst, out):
@@ -44,40 +44,30 @@ def tile_moe_two_lin_relu2_kernel(tc, xT, w_words, w_scales, b, gate, offs, dst,
         dst_sb = keep.tile([P, S // LIST], U16, name="dst_sb")
         b_sb = keep.tile([P, N_TILES, E], F32, name="b_sb")
         gate_sb = keep.tile([P, S], F32, name="gate_sb")
-        w_sb = {g: keep.tile([P, 2 * PASSES, 2 * N], U8, name=f"w_sb{g}", align_bytes=64) for g in range(1, S // G)}
+        w_sb = {g: keep.tile([P, 2 * PASSES, 2 * N], U8, name=f"w_sb{g}", align_bytes=64) for g in range(1, GROUPS)}
         w_scale_sb = keep.tile([P, E * PASSES, N], U8, name="w_scale_sb", align_bytes=64)
         out_sb = {t: keep.tile([P, T], F32, name=f"out_sb{t}") for t in (0, 1, 3)}
 
         def pass_rows(a):
             return xT[a * K_PASS : (a + 1) * K_PASS, :].rearrange("(p d) t -> p (d t)", d=PACK)
 
-        def load_row(d, width):
-            x = keep.tile([P, T], F32, name=f"x_row{d}", align_bytes=64)
-            for t0 in range(0, T, width):
-                nc.sync.dma_start(out=x[:, t0 : t0 + width], in_=pass_rows(1)[:, d * T + t0 : d * T + t0 + width])
-            return x
-
-        x_pairs = []
-        for h in range(2):
-            x = keep.tile([P, 2 * T], F32, name=f"x_pair{h}", align_bytes=64)
-            run = pass_rows(0)[:, 2 * h * T : 2 * (h + 1) * T]
+        def load_pair(u):
+            x = keep.tile([P, 2 * T], F32, name=f"x_pair{u}", align_bytes=64)
+            run = pass_rows(u // 2)[:, 2 * (u % 2) * T : 2 * (u % 2 + 1) * T]
             nc.sync.dma_start(out=x[:, 0 : T + T_HALF], in_=run[:, 0 : T + T_HALF])
             nc.sync.dma_start(out=x[:, T + T_HALF : 2 * T], in_=run[:, T + T_HALF : 2 * T])
-            if h == 0:
-                nc.sync.dma_start(offs_sb[:], offs)
-            by_token = x[:].rearrange("p (e t) -> p t e", e=2)
-            x_pairs.append((by_token[:, 0:T_HALF, :], by_token[:, T_HALF:T, :]))
-        x_row2 = load_row(2, T_HALF)
+            return x[:].rearrange("p (e t) -> p t e", e=2)
 
-        pairs1 = keep.tile([P, LATE + T], U32, name="pairs1", align_bytes=64)
-        x_low1 = keep.tile([P, T], F32, name="x_low1", align_bytes=64)
-        low1_rows = pass_rows(1)[:, 0 : 2 * T].rearrange("p (e t) -> p e t", e=2)
-        low1_halves = []
-        for t0, landing in ((0, x_low1[:]), (T_HALF, pairs1[:, LATE : LATE + T].bitcast(F32))):
-            nc.sync.dma_start(out=landing.rearrange("p (e t) -> p e t", e=2), in_=low1_rows[:, :, t0 : t0 + T_HALF])
-            low1_halves.append(landing.rearrange("p (e t) -> p t e", e=2))
-        x_pairs.append(low1_halves)
-        x_row3 = load_row(3, T)
+        def load_row(d):
+            x = keep.tile([P, T], F32, name=f"x_row{d}", align_bytes=64)
+            nc.sync.dma_start(out=x[:], in_=pass_rows(1)[:, d * T : (d + 1) * T])
+            return x
+
+        x_pairs = [load_pair(0)]
+        nc.sync.dma_start(offs_sb[:], offs)
+        nc.sync.dma_start(dst_sb[:], dst)
+        x_pairs = x_pairs + [load_pair(1), load_pair(2)]
+        x_rows = [load_row(2), load_row(3)]
 
         nc.gpsimd.memset(w_scale_sb[:].rearrange("p g n -> p (g n)").bitcast(I32), 0)
         for t in (0, 3):
@@ -105,10 +95,8 @@ def tile_moe_two_lin_relu2_kernel(tc, xT, w_words, w_scales, b, gate, offs, dst,
             nc.sync.dma_start(gate_sb[:, s0:s1], gate[0:P, s0:s1])
 
         load_weight_scales(0, 2)
-        w_first = load_first_weights(0, 1)
+        w_first = load_first_weights(0, 2)
         nc.sync.dma_start(out=b_sb[:], in_=b.rearrange("(t p) e -> p t e", p=P))
-        w_first = w_first + load_first_weights(1, 2)
-        nc.sync.dma_start(dst_sb[:], dst)
         load_gate(0, G)
         w_first = w_first + load_first_weights(2, N_TILES)
         load_weight_scales(2, 4)
@@ -121,16 +109,18 @@ def tile_moe_two_lin_relu2_kernel(tc, xT, w_words, w_scales, b, gate, offs, dst,
         token_pairs = [keep.tile([P, T], U32, name=f"token_pairs{u}") for u in range(len(x_pairs))]
         codes = [keep.tile([P, S], U32, name=f"codes{a}", align_bytes=64) for a in range(PASSES)]
         scales = [keep.tile([P, S], U8, name=f"scales{a}", align_bytes=64) for a in range(PASSES)]
-        woven1 = keep.tile([P, 2 * LATE], U32, name="woven1", align_bytes=64)
         token_rows = [keep.tile([P, T], BF16, name=f"token_rows{e}") for e in range(2)]
         pairs0 = keep.tile([P, 2, S], U32, name="pairs0")
+        woven0 = keep.tile([P, 2 * S], U32, name="woven0", align_bytes=64)
+        pairs1 = keep.tile([P, 2 * (S - G)], U32, name="pairs1", align_bytes=64)
+        woven1 = keep.tile([P, 2 * (S - G)], U32, name="woven1", align_bytes=64)
 
-        def round_pair(u):
+        def round_pair(u, half):
             rounded = token_pairs[u][:].bitcast(BF16).rearrange("p (t e) -> p t e", e=2)
-            for t0, x, cut in zip((0, T_HALF), x_pairs[u], SCALAR_TOKENS[u]):
-                nc.scalar.copy(rounded[:, t0 : t0 + cut, :], x[:, 0:cut, :])
-                if cut < T_HALF:
-                    nc.vector.tensor_copy(rounded[:, t0 + cut : t0 + T_HALF, :], x[:, cut:T_HALF, :])
+            t0, cut, t1 = half * T_HALF, half * T_HALF + SCALAR_TOKENS[u][half], (half + 1) * T_HALF
+            nc.scalar.copy(rounded[:, t0:cut, :], x_pairs[u][:, t0:cut, :])
+            if cut < t1:
+                nc.vector.tensor_copy(rounded[:, cut:t1, :], x_pairs[u][:, cut:t1, :])
 
         def gathered(window, s0, s1):
             return window[:].indirect(offs_sb[:, s0 // LIST : s1 // LIST])
@@ -143,32 +133,33 @@ def tile_moe_two_lin_relu2_kernel(tc, xT, w_words, w_scales, b, gate, offs, dst,
         first_woven = pairs1[:, 0 : 2 * G]
         first_values = first_woven.bitcast(BF16).rearrange("p (s d) -> p s d", d=PACK)
 
-        round_pair(0)
+        round_pair(0, 0)
+        round_pair(0, 1)
         nc.vector.tensor_copy(pairs0[:, 0, :], gathered(token_pairs[0], 0, S))
         out_sb[2] = keep.tile([P, T], F32, name="x_pair0", align_bytes=64)
         nc.scalar.activation(out_sb[2][:], out_sb[0][:], ACT.Square)
-        round_pair(1)
-        for s0 in (0, S_HALF):
-            nc.vector.tensor_copy(pairs0[:, 1, s0 : s0 + S_HALF], gathered(token_pairs[1], s0, s0 + S_HALF))
-        for t0 in (0, T_HALF):
-            nc.scalar.copy(token_rows[0][:, t0 : t0 + T_HALF], x_row2[:, t0 : t0 + T_HALF])
-        nc.scalar.activation(first_values[:, :, 2], gathered(token_rows[0], 0, G), ACT.Copy)
-        woven0 = keep.tile([P, 2 * S], U32, name="woven0", align_bytes=64)
-        for s0 in (0, S_HALF):
-            nc.vector.tensor_copy(
-                woven0[:, 2 * s0 : 2 * s0 + S].rearrange("p (s h) -> p s h", h=2).bitcast(I32),
-                pairs0[:, :, s0 : s0 + S_HALF].bitcast(I32).rearrange("p h s -> p s h"),
-            )
+        round_pair(1, 0)
+        round_pair(1, 1)
+        for s0 in range(0, S, G):
+            nc.vector.tensor_copy(pairs0[:, 1, s0 : s0 + G], gathered(token_pairs[1], s0, s0 + G))
+        woven0_words = woven0[:].rearrange("p (s h) -> p s h", h=2)
+        pairs0_words = pairs0[:].rearrange("p h s -> p s h")
+        for s0 in range(0, S - G, G):
+            nc.scalar.copy(woven0_words[:, s0 : s0 + G, :], pairs0_words[:, s0 : s0 + G, :])
+        nc.vector.tensor_copy(woven0_words[:, S - G : S, :].bitcast(I32), pairs0[:, :, S - G : S].bitcast(I32).rearrange("p h s -> p s h"))
+        round_pair(2, 0)
         for s0 in (0, S_HALF):
             quantise(0, s0, s0 + S_HALF, woven0[:, 2 * s0 : 2 * s0 + S])
 
-        round_pair(2)
+        round_pair(2, 1)
         nc.vector.tensor_copy(first_woven.rearrange("p (s h) -> p s h", h=2)[:, :, 0], gathered(token_pairs[2], 0, G))
-        nc.vector.tensor_copy(first_values[:, :, 3], gathered(x_row3, 0, G))
+        for e in range(2):
+            nc.vector.tensor_copy(first_values[:, :, 2 + e], gathered(x_rows[e], 0, G))
+            nc.scalar.copy(token_rows[e][:], x_rows[e][:])
         quantise(1, 0, G, first_woven)
 
         def late_pairs(h, s0, s1):
-            return pairs1[:, h * LATE + s0 - G : h * LATE + s1 - G]
+            return pairs1[:, h * (S - G) + s0 - G : h * (S - G) + s1 - G]
 
         def late_woven(s0, s1):
             return woven1[:, 2 * (s0 - G) : 2 * (s1 - G)]
@@ -178,12 +169,12 @@ def tile_moe_two_lin_relu2_kernel(tc, xT, w_words, w_scales, b, gate, offs, dst,
             nc.scalar.activation(high[:, :, e], gathered(token_rows[e], s0, s1), ACT.Copy)
 
         def weave_late(s0, s1):
-            low_high = pairs1[:, 0 : 2 * LATE].rearrange("p (h s) -> p s h", h=2)
+            low_high = pairs1[:].rearrange("p (h s) -> p s h", h=2)
             nc.scalar.copy(late_woven(s0, s1).rearrange("p (s h) -> p s h", h=2), low_high[:, s0 - G : s1 - G, :])
 
         y_sb = [keep.tile([P, S], F32, name=f"y_sb{t}") for t in range(N_TILES)]
 
-        def experts(t, s0, s1, relu_bytes=None):
+        def experts(t, s0, s1, relu_bytes=None, y_bytes=None):
             acc = psum.tile([P, s1 - s0], F32, name="acc")
             if relu_bytes is None:
                 relu_tile = work.tile([P, s1 - s0], F32, name="relu_tile")
@@ -206,39 +197,43 @@ def tile_moe_two_lin_relu2_kernel(tc, xT, w_words, w_scales, b, gate, offs, dst,
                     )
             for e, local in columns.items():
                 nc.scalar.activation(relu[:, local], acc[:, local], ACT.Relu, bias=b_sb[:, t, e : e + 1])
-            nc.scalar.activation(y_sb[t][:, s0:s1], relu, ACT.Square)
+            y = y_sb[t][:, s0:s1] if y_bytes is None else y_bytes.bitcast(F32)
+            nc.scalar.activation(y, relu, ACT.Square)
+            return y
 
-        def scatter(t, s0, s1):
+        def scatter(t, s0, s1, y=None):
             window = out_sb[t][:].indirect(dst_sb[:, s0 // LIST : s1 // LIST])
-            nc.vector.tensor_tensor(window, y_sb[t][:, s0:s1], gate_sb[:, s0:s1], MULT)
+            nc.vector.tensor_tensor(window, y_sb[t][:, s0:s1] if y is None else y, gate_sb[:, s0:s1], MULT)
 
-        def prepare_group(s0, s1):
-            for e in range(2):
-                gather_row(e, s0, s1)
-            weave_late(s0, s1)
-            quantise(1, s0, s1, late_woven(s0, s1))
-
-        gather_row(0, G, 2 * G)
-        nc.scalar.copy(token_rows[1][:], x_row3[:])
-        gather_row(1, G, 2 * G)
         nc.vector.tensor_copy(late_pairs(0, G, S), gathered(token_pairs[2], G, S))
 
-        experts(0, 0, C)
-        experts(0, C, G)
-        experts(1, 0, G, late_woven(G, 2 * G)[:, 0:G])
+        experts(0, 0, C, late_pairs(1, G, G + C))
+        experts(0, C, G, late_pairs(1, G + C, 2 * G))
+        experts(1, 0, G, late_pairs(1, G, 2 * G))
+        for e in range(2):
+            gather_row(e, G, 2 * G)
+        experts(2, 0, G, late_woven(G, 2 * G)[:, 0:G])
         weave_late(G, 2 * G)
-        experts(2, 0, G, late_pairs(0, G, 2 * G))
-        experts(3, 0, G, late_pairs(1, 2 * G, 3 * G))
-        for t in range(N_TILES):
+        y_last = experts(3, 0, G, late_pairs(1, 2 * G, 3 * G), late_pairs(0, G, 2 * G))
+        for t in range(N_TILES - 1):
             scatter(t, 0, G)
-            if t == 1:
-                quantise(1, G, 2 * G, late_woven(G, 2 * G))
-        prepare_group(2 * G, 3 * G)
+        quantise(1, G, 2 * G, late_woven(G, 2 * G))
+        scatter(3, 0, G, y_last)
+        for e in range(2):
+            gather_row(e, 2 * G, 3 * G)
 
-        for t in range(N_TILES):
-            experts(t, G, 2 * G, late_pairs(1, 3 * G, S) if t == N_TILES - 1 else None)
-            scatter(t, G, 2 * G)
-        prepare_group(3 * G, S)
+        experts(0, G, 2 * G, late_woven(2 * G, 3 * G)[:, 0:G])
+        scatter(0, G, 2 * G)
+        weave_late(2 * G, 3 * G)
+        quantise(1, 2 * G, 3 * G, late_woven(2 * G, 3 * G))
+        scatter(1, G, 2 * G, experts(1, G, 2 * G, late_pairs(1, 3 * G, S), late_pairs(0, 2 * G, 3 * G)))
+        for e in range(2):
+            gather_row(e, 3 * G, S)
+        experts(2, G, 2 * G, late_woven(3 * G, S)[:, 0:G])
+        scatter(2, G, 2 * G)
+        weave_late(3 * G, S)
+        quantise(1, 3 * G, S, late_woven(3 * G, S))
+        scatter(3, G, 2 * G, experts(3, G, 2 * G, None, late_pairs(0, 3 * G, S)))
 
         experts(0, 2 * G, 3 * G)
         scatter(0, 2 * G, 3 * G)

@@ -84,20 +84,22 @@ def tile_moe_two_lin_relu2_kernel(tc, xT, w_words, w_scales, b, gate, offs, dst,
             nc.sync.dma_start(out=w_part[:].bitcast(I32), in_=words.bitcast(I32))
             return [w_part[:, :, 2 * (t - t0) * P : 2 * (t - t0 + 1) * P] for t in range(t0, t1)]
 
-        def load_weight_scales(e0, e1):
+        def load_weight_scales(e0, e1, n0=0, n1=N):
             for r in range(4):
                 nc.sync.dma_start(
-                    out=w_scale_sb[r:P:32, PASSES * e0 : PASSES * e1, :].bitcast(I32),
-                    in_=w_scales[e0:e1, :, r:16:4, :].rearrange("e a q n -> q (e a) n").bitcast(I32),
+                    out=w_scale_sb[r:P:32, PASSES * e0 : PASSES * e1, n0:n1].bitcast(I32),
+                    in_=w_scales[e0:e1, :, r:16:4, n0:n1].rearrange("e a q n -> q (e a) n").bitcast(I32),
                 )
 
         def load_gate(s0, s1):
             nc.sync.dma_start(gate_sb[:, s0:s1], gate[0:P, s0:s1])
 
-        load_weight_scales(0, 2)
-        w_first = load_first_weights(0, 2)
+        load_weight_scales(0, 2, 0, 2 * P)
+        w_first = load_first_weights(0, 1)
         nc.sync.dma_start(out=b_sb[:], in_=b.rearrange("(t p) e -> p t e", p=P))
+        w_first = w_first + load_first_weights(1, 2)
         load_gate(0, G)
+        load_weight_scales(0, 2, 2 * P, N)
         w_first = w_first + load_first_weights(2, N_TILES)
         load_weight_scales(2, 4)
         load_weights(1)

@@ -30,7 +30,7 @@ GROUPS = S // G
 S_HALF = S // 2
 T_HALF = T // 2
 
-SCALAR_TOKENS = ((256, 256), (480, 256), (T_HALF, 256))
+PIECES = (((768, 320), (T, 320)), ((768, 448), (T, 304)), ((768, 768), (T, 0)))
 
 
 def tile_moe_two_lin_relu2_kernel(tc, xT, w_words, w_scales, b, gate, offs, dst, out):
@@ -54,8 +54,9 @@ def tile_moe_two_lin_relu2_kernel(tc, xT, w_words, w_scales, b, gate, offs, dst,
         def load_pair(u):
             x = keep.tile([P, 2 * T], F32, name=f"x_pair{u}", align_bytes=64)
             run = pass_rows(u // 2)[:, 2 * (u % 2) * T : 2 * (u % 2 + 1) * T]
-            nc.sync.dma_start(out=x[:, 0 : T + T_HALF], in_=run[:, 0 : T + T_HALF])
-            nc.sync.dma_start(out=x[:, T + T_HALF : 2 * T], in_=run[:, T + T_HALF : 2 * T])
+            ends = [T + t1 for t1, share in PIECES[u]]
+            for c0, c1 in zip([0] + ends, ends):
+                nc.sync.dma_start(out=x[:, c0:c1], in_=run[:, c0:c1])
             return x[:].rearrange("p (e t) -> p t e", e=2)
 
         def load_row(d):
@@ -65,7 +66,6 @@ def tile_moe_two_lin_relu2_kernel(tc, xT, w_words, w_scales, b, gate, offs, dst,
 
         x_pairs = [load_pair(0)]
         nc.sync.dma_start(offs_sb[:], offs)
-        nc.sync.dma_start(dst_sb[:], dst)
         x_pairs = x_pairs + [load_pair(1), load_pair(2)]
         x_rows = [load_row(2), load_row(3)]
 
@@ -94,12 +94,11 @@ def tile_moe_two_lin_relu2_kernel(tc, xT, w_words, w_scales, b, gate, offs, dst,
         def load_gate(s0, s1):
             nc.sync.dma_start(gate_sb[:, s0:s1], gate[0:P, s0:s1])
 
-        load_weight_scales(0, 2, 0, 2 * P)
-        w_first = load_first_weights(0, 1)
+        load_weight_scales(0, 2)
+        w_first = load_first_weights(0, 2)
         nc.sync.dma_start(out=b_sb[:], in_=b.rearrange("(t p) e -> p t e", p=P))
-        w_first = w_first + load_first_weights(1, 2)
+        nc.sync.dma_start(dst_sb[:], dst)
         load_gate(0, G)
-        load_weight_scales(0, 2, 2 * P, N)
         w_first = w_first + load_first_weights(2, N_TILES)
         load_weight_scales(2, 4)
         load_weights(1)
@@ -117,10 +116,13 @@ def tile_moe_two_lin_relu2_kernel(tc, xT, w_words, w_scales, b, gate, offs, dst,
         pairs1 = keep.tile([P, 2 * (S - G)], U32, name="pairs1", align_bytes=64)
         woven1 = keep.tile([P, 2 * (S - G)], U32, name="woven1", align_bytes=64)
 
-        def round_pair(u, half):
+        def round_pair(u, piece):
             rounded = token_pairs[u][:].bitcast(BF16).rearrange("p (t e) -> p t e", e=2)
-            t0, cut, t1 = half * T_HALF, half * T_HALF + SCALAR_TOKENS[u][half], (half + 1) * T_HALF
-            nc.scalar.copy(rounded[:, t0:cut, :], x_pairs[u][:, t0:cut, :])
+            t0 = PIECES[u][piece - 1][0] if piece > 0 else 0
+            t1, share = PIECES[u][piece]
+            cut = t0 + share
+            if cut > t0:
+                nc.scalar.copy(rounded[:, t0:cut, :], x_pairs[u][:, t0:cut, :])
             if cut < t1:
                 nc.vector.tensor_copy(rounded[:, cut:t1, :], x_pairs[u][:, cut:t1, :])
 
@@ -135,8 +137,8 @@ def tile_moe_two_lin_relu2_kernel(tc, xT, w_words, w_scales, b, gate, offs, dst,
         first_woven = pairs1[:, 0 : 2 * G]
         first_values = first_woven.bitcast(BF16).rearrange("p (s d) -> p s d", d=PACK)
 
-        round_pair(0, 0)
-        round_pair(0, 1)
+        for piece in range(len(PIECES[0])):
+            round_pair(0, piece)
         nc.vector.tensor_copy(pairs0[:, 0, :], gathered(token_pairs[0], 0, S))
         out_sb[2] = keep.tile([P, T], F32, name="x_pair0", align_bytes=64)
         nc.scalar.activation(out_sb[2][:], out_sb[0][:], ACT.Square)
@@ -148,17 +150,20 @@ def tile_moe_two_lin_relu2_kernel(tc, xT, w_words, w_scales, b, gate, offs, dst,
         pairs0_words = pairs0[:].rearrange("p h s -> p s h")
         for s0 in range(0, S - G, G):
             nc.scalar.copy(woven0_words[:, s0 : s0 + G, :], pairs0_words[:, s0 : s0 + G, :])
-        nc.vector.tensor_copy(woven0_words[:, S - G : S, :].bitcast(I32), pairs0[:, :, S - G : S].bitcast(I32).rearrange("p h s -> p s h"))
         round_pair(2, 0)
-        for s0 in (0, S_HALF):
-            quantise(0, s0, s0 + S_HALF, woven0[:, 2 * s0 : 2 * s0 + S])
+        nc.scalar.copy(woven0_words[:, S - G : S, :], pairs0_words[:, S - G : S, :])
+        for s0, s1 in ((0, S_HALF), (S_HALF, S - G)):
+            quantise(0, s0, s1, woven0[:, 2 * s0 : 2 * s1])
 
         round_pair(2, 1)
         nc.vector.tensor_copy(first_woven.rearrange("p (s h) -> p s h", h=2)[:, :, 0], gathered(token_pairs[2], 0, G))
         for e in range(2):
+            if e == 1:
+                quantise(0, S - G, S, woven0[:, 2 * (S - G) : 2 * S])
             nc.vector.tensor_copy(first_values[:, :, 2 + e], gathered(x_rows[e], 0, G))
             nc.scalar.copy(token_rows[e][:], x_rows[e][:])
-        quantise(1, 0, G, first_woven)
+        for s0 in (0, C):
+            quantise(1, s0, s0 + C, first_woven[:, 2 * s0 : 2 * (s0 + C)])
 
         def late_pairs(h, s0, s1):
             return pairs1[:, h * (S - G) + s0 - G : h * (S - G) + s1 - G]

@@ -30,7 +30,7 @@ GROUPS = S // G
 S_HALF = S // 2
 T_HALF = T // 2
 
-PIECES = (((768, 320), (T, 320)), ((768, 448), (T, 304)), ((768, 768), (T, 0)))
+PIECES = (((768, 320), (T, 320)), ((768, 448), (T, 304)))
 
 
 def tile_moe_two_lin_relu2_kernel(tc, xT, w_words, w_scales, b, gate, offs, dst, out):
@@ -61,13 +61,16 @@ def tile_moe_two_lin_relu2_kernel(tc, xT, w_words, w_scales, b, gate, offs, dst,
 
         def load_row(d):
             x = keep.tile([P, T], F32, name=f"x_row{d}", align_bytes=64)
-            nc.sync.dma_start(out=x[:], in_=pass_rows(1)[:, d * T : (d + 1) * T])
+            width = T_HALF if d == 0 else T
+            for t0 in range(0, T, width):
+                nc.sync.dma_start(out=x[:, t0 : t0 + width], in_=pass_rows(1)[:, d * T + t0 : d * T + t0 + width])
             return x
 
         x_pairs = [load_pair(0)]
         nc.sync.dma_start(offs_sb[:], offs)
-        x_pairs = x_pairs + [load_pair(1), load_pair(2)]
-        x_rows = [load_row(2), load_row(3)]
+        nc.sync.dma_start(dst_sb[:], dst)
+        x_pairs.append(load_pair(1))
+        x_rows = [load_row(d) for d in range(PACK)]
 
         nc.gpsimd.memset(w_scale_sb[:].rearrange("p g n -> p (g n)").bitcast(I32), 0)
         for t in (0, 3):
@@ -97,7 +100,6 @@ def tile_moe_two_lin_relu2_kernel(tc, xT, w_words, w_scales, b, gate, offs, dst,
         load_weight_scales(0, 2)
         w_first = load_first_weights(0, 2)
         nc.sync.dma_start(out=b_sb[:], in_=b.rearrange("(t p) e -> p t e", p=P))
-        nc.sync.dma_start(dst_sb[:], dst)
         load_gate(0, G)
         w_first = w_first + load_first_weights(2, N_TILES)
         load_weight_scales(2, 4)
@@ -108,13 +110,26 @@ def tile_moe_two_lin_relu2_kernel(tc, xT, w_words, w_scales, b, gate, offs, dst,
         load_weights(3)
 
         token_pairs = [keep.tile([P, T], U32, name=f"token_pairs{u}") for u in range(len(x_pairs))]
-        codes = [keep.tile([P, S], U32, name=f"codes{a}", align_bytes=64) for a in range(PASSES)]
+        codes_early = keep.tile([P, S_HALF], U32, name="codes_early", align_bytes=64)
+        codes1 = keep.tile([P, S], U32, name="codes1", align_bytes=64)
         scales = [keep.tile([P, S], U8, name=f"scales{a}", align_bytes=64) for a in range(PASSES)]
-        token_rows = [keep.tile([P, T], BF16, name=f"token_rows{e}") for e in range(2)]
+        late = ctx.enter_context(tc.tile_pool(name="late", bufs=1))
+        first_tile = late.tile([P, 2 * G], U32, name="first_tile", align_bytes=64, offset=2 * T - 4 * G)
+        last_row = late.tile([P, T], BF16, name="last_row", align_bytes=64, offset=0)
+        codes_late = late.tile([P, S_HALF], U32, name="codes_late", align_bytes=64, offset=2 * T)
+        token_rows = [keep.tile([P, T], BF16, name=f"token_rows{d}")[:] for d in range(PACK - 1)]
+        token_rows.append(last_row[:])
         pairs0 = keep.tile([P, 2, S], U32, name="pairs0")
         woven0 = keep.tile([P, 2 * S], U32, name="woven0", align_bytes=64)
         pairs1 = keep.tile([P, 2 * (S - G)], U32, name="pairs1", align_bytes=64)
         woven1 = keep.tile([P, 2 * (S - G)], U32, name="woven1", align_bytes=64)
+
+        def codes(a, s0, s1):
+            if a == 1:
+                return codes1[:, s0:s1]
+            if s0 < S_HALF:
+                return codes_early[:, s0:s1]
+            return codes_late[:, s0 - S_HALF : s1 - S_HALF]
 
         def round_pair(u, piece):
             rounded = token_pairs[u][:].bitcast(BF16).rearrange("p (t e) -> p t e", e=2)
@@ -127,14 +142,14 @@ def tile_moe_two_lin_relu2_kernel(tc, xT, w_words, w_scales, b, gate, offs, dst,
                 nc.vector.tensor_copy(rounded[:, cut:t1, :], x_pairs[u][:, cut:t1, :])
 
         def gathered(window, s0, s1):
-            return window[:].indirect(offs_sb[:, s0 // LIST : s1 // LIST])
+            return window[:, :].indirect(offs_sb[:, s0 // LIST : s1 // LIST])
 
         def quantise(a, s0, s1, woven):
             nc.vector.quantize_mx(
-                out=codes[a][:, s0:s1].bitcast(E4M3X4), scales=scales[a][:, s0:s1], in_=woven.bitcast(BF16)
+                out=codes(a, s0, s1).bitcast(E4M3X4), scales=scales[a][:, s0:s1], in_=woven.bitcast(BF16)
             )
 
-        first_woven = pairs1[:, 0 : 2 * G]
+        first_woven = first_tile[:]
         first_values = first_woven.bitcast(BF16).rearrange("p (s d) -> p s d", d=PACK)
 
         for piece in range(len(PIECES[0])):
@@ -144,26 +159,26 @@ def tile_moe_two_lin_relu2_kernel(tc, xT, w_words, w_scales, b, gate, offs, dst,
         nc.scalar.activation(out_sb[2][:], out_sb[0][:], ACT.Square)
         round_pair(1, 0)
         round_pair(1, 1)
-        for s0 in range(0, S, G):
-            nc.vector.tensor_copy(pairs0[:, 1, s0 : s0 + G], gathered(token_pairs[1], s0, s0 + G))
+        for s0 in (0, S_HALF):
+            nc.vector.tensor_copy(pairs0[:, 1, s0 : s0 + S_HALF], gathered(token_pairs[1], s0, s0 + S_HALF))
         woven0_words = woven0[:].rearrange("p (s h) -> p s h", h=2)
-        pairs0_words = pairs0[:].rearrange("p h s -> p s h")
-        for s0 in range(0, S - G, G):
-            nc.scalar.copy(woven0_words[:, s0 : s0 + G, :], pairs0_words[:, s0 : s0 + G, :])
-        round_pair(2, 0)
-        nc.scalar.copy(woven0_words[:, S - G : S, :], pairs0_words[:, S - G : S, :])
-        for s0, s1 in ((0, S_HALF), (S_HALF, S - G)):
-            quantise(0, s0, s1, woven0[:, 2 * s0 : 2 * s1])
-
-        round_pair(2, 1)
-        nc.vector.tensor_copy(first_woven.rearrange("p (s h) -> p s h", h=2)[:, :, 0], gathered(token_pairs[2], 0, G))
-        for e in range(2):
-            if e == 1:
-                quantise(0, S - G, S, woven0[:, 2 * (S - G) : 2 * S])
-            nc.vector.tensor_copy(first_values[:, :, 2 + e], gathered(x_rows[e], 0, G))
-            nc.scalar.copy(token_rows[e][:], x_rows[e][:])
+        for t0 in (0, T_HALF):
+            nc.scalar.copy(token_rows[0][:, t0 : t0 + T_HALF], x_rows[0][:, t0 : t0 + T_HALF])
+        nc.scalar.copy(woven0_words[:, 0:S_HALF, :], pairs0[:].rearrange("p h s -> p s h")[:, 0:S_HALF, :])
+        nc.vector.tensor_copy(first_values[:, :, 0], gathered(x_rows[0], 0, G))
+        nc.vector.tensor_copy(
+            woven0_words[:, S_HALF:S, :].bitcast(I32), pairs0[:, :, S_HALF:S].bitcast(I32).rearrange("p h s -> p s h")
+        )
+        nc.scalar.copy(token_rows[1], x_rows[1][:])
+        nc.vector.tensor_copy(first_values[:, :, 1], gathered(x_rows[1], 0, G))
+        quantise(0, 0, S_HALF, woven0[:, 0:S])
+        nc.scalar.copy(token_rows[2], x_rows[2][:])
+        for d in (2, 3):
+            nc.vector.tensor_copy(first_values[:, :, d], gathered(x_rows[d], 0, G))
         for s0 in (0, C):
             quantise(1, s0, s0 + C, first_woven[:, 2 * s0 : 2 * (s0 + C)])
+        nc.vector.tensor_copy(token_rows[3], x_rows[3][:])
+        quantise(0, S_HALF, S, woven0[:, S : 2 * S])
 
         def late_pairs(h, s0, s1):
             return pairs1[:, h * (S - G) + s0 - G : h * (S - G) + s1 - G]
@@ -171,9 +186,9 @@ def tile_moe_two_lin_relu2_kernel(tc, xT, w_words, w_scales, b, gate, offs, dst,
         def late_woven(s0, s1):
             return woven1[:, 2 * (s0 - G) : 2 * (s1 - G)]
 
-        def gather_row(e, s0, s1):
-            high = late_pairs(1, s0, s1).bitcast(BF16).rearrange("p (s e) -> p s e", e=2)
-            nc.scalar.activation(high[:, :, e], gathered(token_rows[e], s0, s1), ACT.Copy)
+        def gather_row(d, s0, s1):
+            pairs = late_pairs(d // 2, s0, s1).bitcast(BF16).rearrange("p (s e) -> p s e", e=2)
+            nc.scalar.activation(pairs[:, :, d % 2], gathered(token_rows[d], s0, s1), ACT.Copy)
 
         def weave_late(s0, s1):
             low_high = pairs1[:].rearrange("p (h s) -> p s h", h=2)
@@ -197,7 +212,7 @@ def tile_moe_two_lin_relu2_kernel(tc, xT, w_words, w_scales, b, gate, offs, dst,
                         out=acc[:, local],
                         lhsT=words[:, PASSES * (e % 2) + a, :].bitcast(E2M1X4),
                         lhsT_scale=w_scale_sb[:, PASSES * e + a, t * P : (t + 1) * P],
-                        rhs=codes[a][:, slots].bitcast(E4M3X4),
+                        rhs=codes(a, e * C, (e + 1) * C).bitcast(E4M3X4),
                         rhs_scale=scales[a][:, slots],
                         start=(a == 0),
                         stop=(a == PASSES - 1),
@@ -212,40 +227,42 @@ def tile_moe_two_lin_relu2_kernel(tc, xT, w_words, w_scales, b, gate, offs, dst,
             window = out_sb[t][:].indirect(dst_sb[:, s0 // LIST : s1 // LIST])
             nc.vector.tensor_tensor(window, y_sb[t][:, s0:s1] if y is None else y, gate_sb[:, s0:s1], MULT)
 
-        nc.vector.tensor_copy(late_pairs(0, G, S), gathered(token_pairs[2], G, S))
+        def store(t):
+            nc.sync.dma_start(out=out[t * P : (t + 1) * P, :], in_=out_sb[t][:])
 
+        for d in (0, 1):
+            gather_row(d, G, 2 * G)
         experts(0, 0, C, late_pairs(1, G, G + C))
         experts(0, C, G, late_pairs(1, G + C, 2 * G))
-        experts(1, 0, G, late_pairs(1, G, 2 * G))
-        for e in range(2):
-            gather_row(e, G, 2 * G)
-        experts(2, 0, G, late_woven(G, 2 * G)[:, 0:G])
+        scatter(0, 0, G)
+        scatter(1, 0, G, experts(1, 0, G, late_pairs(1, G, 2 * G)))
+        gather_row(2, G, 2 * G)
+        scatter(2, 0, G, experts(2, 0, G, late_pairs(0, 2 * G, 3 * G)))
+        gather_row(3, G, 2 * G)
         weave_late(G, 2 * G)
-        y_last = experts(3, 0, G, late_pairs(1, 2 * G, 3 * G), late_pairs(0, G, 2 * G))
-        for t in range(N_TILES - 1):
-            scatter(t, 0, G)
         quantise(1, G, 2 * G, late_woven(G, 2 * G))
-        scatter(3, 0, G, y_last)
-        for e in range(2):
-            gather_row(e, 2 * G, 3 * G)
-
-        experts(0, G, 2 * G, late_woven(2 * G, 3 * G)[:, 0:G])
-        scatter(0, G, 2 * G)
-        weave_late(2 * G, 3 * G)
-        quantise(1, 2 * G, 3 * G, late_woven(2 * G, 3 * G))
-        scatter(1, G, 2 * G, experts(1, G, 2 * G, late_pairs(1, 3 * G, S), late_pairs(0, 2 * G, 3 * G)))
-        for e in range(2):
-            gather_row(e, 3 * G, S)
-        experts(2, G, 2 * G, late_woven(3 * G, S)[:, 0:G])
-        scatter(2, G, 2 * G)
-        weave_late(3 * G, S)
-        quantise(1, 3 * G, S, late_woven(3 * G, S))
-        scatter(3, G, 2 * G, experts(3, G, 2 * G, None, late_pairs(0, 3 * G, S)))
-
-        experts(0, 2 * G, 3 * G)
-        scatter(0, 2 * G, 3 * G)
-        for t in (1, 2, 0, 3):
-            s0 = 3 * G if t == 0 else 2 * G
-            experts(t, s0, S)
-            scatter(t, s0, S)
-            nc.sync.dma_start(out=out[t * P : (t + 1) * P, :], in_=out_sb[t][:])
+        scatter(3, 0, G, experts(3, 0, G, late_pairs(0, 2 * G, 3 * G), late_pairs(0, G, 2 * G)))
+        for g in (1, 2):
+            s0, s1, s2 = g * G, (g + 1) * G, (g + 2) * G
+            gather_row(0, s1, s2)
+            experts(0, s0, s0 + C, late_pairs(1, s1, s1 + C))
+            experts(0, s0 + C, s1, late_pairs(1, s1 + C, s2))
+            scatter(0, s0, s1)
+            gather_row(1, s1, s2)
+            scatter(1, s0, s1, experts(1, s0, s1, late_pairs(1, s1, s2)))
+            gather_row(2, s1, s2)
+            scatter(2, s0, s1, experts(2, s0, s1))
+            gather_row(3, s1, s2)
+            weave_late(s1, s2)
+            quantise(1, s1, s2, late_woven(s1, s2))
+            if g == 1:
+                scatter(3, s0, s1, experts(3, s0, s1, late_pairs(0, s2, S), late_pairs(0, s1, s2)))
+            else:
+                scatter(3, s0, s1, experts(3, s0, s1, None, late_pairs(0, s1, s2)))
+        experts(0, 3 * G, 3 * G + C)
+        experts(0, 3 * G + C, S)
+        for t in range(N_TILES):
+            if t > 0:
+                experts(t, 3 * G, S)
+            scatter(t, 3 * G, S)
+            store(t)

@@ -38,6 +38,7 @@ def tile_moe_two_lin_relu2_kernel(tc, xT, w_words, w_scales, b, gate, offs, dst,
     with ExitStack() as ctx:
         keep = ctx.enter_context(tc.tile_pool(name="keep", bufs=1))
         work = ctx.enter_context(tc.tile_pool(name="work", bufs=4))
+        late = ctx.enter_context(tc.tile_pool(name="late", bufs=1))
         psum = ctx.enter_context(tc.psum_pool(name="psum", bufs=8))
 
         offs_sb = keep.tile([P, S // LIST], U16, name="offs_sb")
@@ -60,10 +61,11 @@ def tile_moe_two_lin_relu2_kernel(tc, xT, w_words, w_scales, b, gate, offs, dst,
             return x[:].rearrange("p (e t) -> p t e", e=2)
 
         def load_row(d):
-            x = keep.tile([P, T], F32, name=f"x_row{d}", align_bytes=64)
-            width = T_HALF if d == 0 else T
-            for t0 in range(0, T, width):
-                nc.sync.dma_start(out=x[:, t0 : t0 + width], in_=pass_rows(1)[:, d * T + t0 : d * T + t0 + width])
+            if d == 1:
+                x = late.tile([P, T], F32, name="x_row1", align_bytes=64, offset=8 * S)
+            else:
+                x = keep.tile([P, T], F32, name=f"x_row{d}", align_bytes=64)
+            nc.sync.dma_start(out=x[:], in_=pass_rows(1)[:, d * T : (d + 1) * T])
             return x
 
         x_pairs = [load_pair(0)]
@@ -110,17 +112,17 @@ def tile_moe_two_lin_relu2_kernel(tc, xT, w_words, w_scales, b, gate, offs, dst,
         load_weights(3)
 
         token_pairs = [keep.tile([P, T], U32, name=f"token_pairs{u}") for u in range(len(x_pairs))]
-        codes_early = keep.tile([P, S_HALF], U32, name="codes_early", align_bytes=64)
+        codes_early = late.tile([P, S_HALF], U32, name="codes_early", align_bytes=64, offset=8 * S)
         codes1 = keep.tile([P, S], U32, name="codes1", align_bytes=64)
         scales = [keep.tile([P, S], U8, name=f"scales{a}", align_bytes=64) for a in range(PASSES)]
-        late = ctx.enter_context(tc.tile_pool(name="late", bufs=1))
-        first_tile = late.tile([P, 2 * G], U32, name="first_tile", align_bytes=64, offset=2 * T - 4 * G)
-        last_row = late.tile([P, T], BF16, name="last_row", align_bytes=64, offset=0)
+        woven_early = late.tile([P, S], U32, name="woven_early", align_bytes=64, offset=0)
+        third_row = late.tile([P, T], BF16, name="third_row", align_bytes=64, offset=0)
         codes_late = late.tile([P, S_HALF], U32, name="codes_late", align_bytes=64, offset=2 * T)
-        token_rows = [keep.tile([P, T], BF16, name=f"token_rows{d}")[:] for d in range(PACK - 1)]
-        token_rows.append(last_row[:])
+        first_tile = late.tile([P, 2 * G], U32, name="first_tile", align_bytes=64, offset=4 * S)
+        last_row = late.tile([P, T], BF16, name="last_row", align_bytes=64, offset=2 * T + 2 * S)
+        token_rows = [keep.tile([P, T], BF16, name=f"token_rows{d}")[:] for d in (0, 1)] + [third_row[:], last_row[:]]
         pairs0 = keep.tile([P, 2, S], U32, name="pairs0")
-        woven0 = keep.tile([P, 2 * S], U32, name="woven0", align_bytes=64)
+        woven0 = keep.tile([P, S], U32, name="woven0", align_bytes=64)
         pairs1 = keep.tile([P, 2 * (S - G)], U32, name="pairs1", align_bytes=64)
         woven1 = keep.tile([P, 2 * (S - G)], U32, name="woven1", align_bytes=64)
 
@@ -161,24 +163,22 @@ def tile_moe_two_lin_relu2_kernel(tc, xT, w_words, w_scales, b, gate, offs, dst,
         round_pair(1, 1)
         for s0 in (0, S_HALF):
             nc.vector.tensor_copy(pairs0[:, 1, s0 : s0 + S_HALF], gathered(token_pairs[1], s0, s0 + S_HALF))
-        woven0_words = woven0[:].rearrange("p (s h) -> p s h", h=2)
-        for t0 in (0, T_HALF):
-            nc.scalar.copy(token_rows[0][:, t0 : t0 + T_HALF], x_rows[0][:, t0 : t0 + T_HALF])
-        nc.scalar.copy(woven0_words[:, 0:S_HALF, :], pairs0[:].rearrange("p h s -> p s h")[:, 0:S_HALF, :])
-        nc.vector.tensor_copy(first_values[:, :, 0], gathered(x_rows[0], 0, G))
-        nc.vector.tensor_copy(
-            woven0_words[:, S_HALF:S, :].bitcast(I32), pairs0[:, :, S_HALF:S].bitcast(I32).rearrange("p h s -> p s h")
-        )
-        nc.scalar.copy(token_rows[1], x_rows[1][:])
-        nc.vector.tensor_copy(first_values[:, :, 1], gathered(x_rows[1], 0, G))
-        quantise(0, 0, S_HALF, woven0[:, 0:S])
-        nc.scalar.copy(token_rows[2], x_rows[2][:])
-        for d in (2, 3):
+        pairs0_words = pairs0[:].rearrange("p h s -> p s h")
+        nc.scalar.copy(woven_early[:].rearrange("p (s h) -> p s h", h=2), pairs0_words[:, 0:S_HALF, :])
+        nc.scalar.copy(woven0[:].rearrange("p (s h) -> p s h", h=2), pairs0_words[:, S_HALF:S, :])
+        for d in range(PACK):
+            if d == 2:
+                quantise(0, 0, S_HALF, woven_early[:])
+            if d < PACK - 1:
+                cut = T_HALF if d == 2 else 0
+                if cut:
+                    nc.scalar.copy(token_rows[d][:, 0:cut], x_rows[d][:, 0:cut])
+                nc.gpsimd.tensor_scalar(token_rows[d][:, cut:T], x_rows[d][:, cut:T], 1.0, 0.0, MULT, mybir.AluOpType.add)
             nc.vector.tensor_copy(first_values[:, :, d], gathered(x_rows[d], 0, G))
         for s0 in (0, C):
             quantise(1, s0, s0 + C, first_woven[:, 2 * s0 : 2 * (s0 + C)])
         nc.vector.tensor_copy(token_rows[3], x_rows[3][:])
-        quantise(0, S_HALF, S, woven0[:, S : 2 * S])
+        quantise(0, S_HALF, S, woven0[:])
 
         def late_pairs(h, s0, s1):
             return pairs1[:, h * (S - G) + s0 - G : h * (S - G) + s1 - G]
@@ -231,38 +231,43 @@ def tile_moe_two_lin_relu2_kernel(tc, xT, w_words, w_scales, b, gate, offs, dst,
             nc.sync.dma_start(out=out[t * P : (t + 1) * P, :], in_=out_sb[t][:])
 
         for d in (0, 1):
-            gather_row(d, G, 2 * G)
+            gather_row(d, G, 3 * G)
         experts(0, 0, C, late_pairs(1, G, G + C))
         experts(0, C, G, late_pairs(1, G + C, 2 * G))
         scatter(0, 0, G)
         scatter(1, 0, G, experts(1, 0, G, late_pairs(1, G, 2 * G)))
         gather_row(2, G, 2 * G)
-        scatter(2, 0, G, experts(2, 0, G, late_pairs(0, 2 * G, 3 * G)))
+        scatter(2, 0, G, experts(2, 0, G))
         gather_row(3, G, 2 * G)
         weave_late(G, 2 * G)
         quantise(1, G, 2 * G, late_woven(G, 2 * G))
-        scatter(3, 0, G, experts(3, 0, G, late_pairs(0, 2 * G, 3 * G), late_pairs(0, G, 2 * G)))
-        for g in (1, 2):
-            s0, s1, s2 = g * G, (g + 1) * G, (g + 2) * G
-            gather_row(0, s1, s2)
-            experts(0, s0, s0 + C, late_pairs(1, s1, s1 + C))
-            experts(0, s0 + C, s1, late_pairs(1, s1 + C, s2))
-            scatter(0, s0, s1)
-            gather_row(1, s1, s2)
-            scatter(1, s0, s1, experts(1, s0, s1, late_pairs(1, s1, s2)))
-            gather_row(2, s1, s2)
-            scatter(2, s0, s1, experts(2, s0, s1))
-            gather_row(3, s1, s2)
-            weave_late(s1, s2)
-            quantise(1, s1, s2, late_woven(s1, s2))
-            if g == 1:
-                scatter(3, s0, s1, experts(3, s0, s1, late_pairs(0, s2, S), late_pairs(0, s1, s2)))
-            else:
-                scatter(3, s0, s1, experts(3, s0, s1, None, late_pairs(0, s1, s2)))
+        scatter(3, 0, G, experts(3, 0, G, late_pairs(0, 3 * G, S), late_pairs(0, G, 2 * G)))
+        gather_row(0, 3 * G, S)
+
+        experts(0, G, G + C, late_pairs(1, 2 * G, 2 * G + C))
+        experts(0, G + C, 2 * G, late_pairs(1, 2 * G + C, 3 * G))
+        scatter(0, G, 2 * G)
+        gather_row(2, 2 * G, 3 * G)
+        scatter(1, G, 2 * G, experts(1, G, 2 * G))
+        gather_row(3, 2 * G, 3 * G)
+        weave_late(2 * G, 3 * G)
+        quantise(1, 2 * G, 3 * G, late_woven(2 * G, 3 * G))
+        scatter(2, G, 2 * G, experts(2, G, 2 * G, None, late_pairs(0, 2 * G, 3 * G)))
+        scatter(3, G, 2 * G, experts(3, G, 2 * G))
+        gather_row(1, 3 * G, S)
+
+        scatter(0, 2 * G, 3 * G, experts(0, 2 * G, 3 * G, late_pairs(1, 3 * G, S)))
+        gather_row(2, 3 * G, S)
+        scatter(1, 2 * G, 3 * G, experts(1, 2 * G, 3 * G))
+        gather_row(3, 3 * G, S)
+        weave_late(3 * G, S)
+        quantise(1, 3 * G, S, late_woven(3 * G, S))
+        scatter(2, 2 * G, 3 * G, experts(2, 2 * G, 3 * G, None, late_pairs(0, 3 * G, S)))
         experts(0, 3 * G, 3 * G + C)
         experts(0, 3 * G + C, S)
         for t in range(N_TILES):
+            s0 = 2 * G if t == N_TILES - 1 else 3 * G
             if t > 0:
-                experts(t, 3 * G, S)
-            scatter(t, 3 * G, S)
+                experts(t, s0, S)
+            scatter(t, s0, S)
             store(t)

@@ -65,7 +65,9 @@ def tile_moe_two_lin_relu2_kernel(tc, xT, w_words, w_scales, b, gate, offs, dst,
                 x = late.tile([P, T], F32, name="x_row1", align_bytes=64, offset=8 * S)
             else:
                 x = keep.tile([P, T], F32, name=f"x_row{d}", align_bytes=64)
-            nc.sync.dma_start(out=x[:], in_=pass_rows(1)[:, d * T : (d + 1) * T])
+            width = T_HALF if d == 0 else T
+            for t0 in range(0, T, width):
+                nc.sync.dma_start(out=x[:, t0 : t0 + width], in_=pass_rows(1)[:, d * T + t0 : d * T + t0 + width])
             return x
 
         x_pairs = [load_pair(0)]
@@ -99,10 +101,12 @@ def tile_moe_two_lin_relu2_kernel(tc, xT, w_words, w_scales, b, gate, offs, dst,
         def load_gate(s0, s1):
             nc.sync.dma_start(gate_sb[:, s0:s1], gate[0:P, s0:s1])
 
-        load_weight_scales(0, 2)
-        w_first = load_first_weights(0, 2)
+        load_weight_scales(0, 2, 0, 2 * P)
+        w_first = load_first_weights(0, 1)
         nc.sync.dma_start(out=b_sb[:], in_=b.rearrange("(t p) e -> p t e", p=P))
+        w_first = w_first + load_first_weights(1, 2)
         load_gate(0, G)
+        load_weight_scales(0, 2, 2 * P, N)
         w_first = w_first + load_first_weights(2, N_TILES)
         load_weight_scales(2, 4)
         load_weights(1)
@@ -164,14 +168,15 @@ def tile_moe_two_lin_relu2_kernel(tc, xT, w_words, w_scales, b, gate, offs, dst,
         for s0 in (0, S_HALF):
             nc.vector.tensor_copy(pairs0[:, 1, s0 : s0 + S_HALF], gathered(token_pairs[1], s0, s0 + S_HALF))
         pairs0_words = pairs0[:].rearrange("p h s -> p s h")
+        nc.scalar.copy(token_rows[0][:, 0:T_HALF], x_rows[0][:, 0:T_HALF])
         nc.scalar.copy(woven_early[:].rearrange("p (s h) -> p s h", h=2), pairs0_words[:, 0:S_HALF, :])
         nc.scalar.copy(woven0[:].rearrange("p (s h) -> p s h", h=2), pairs0_words[:, S_HALF:S, :])
         for d in range(PACK):
             if d == 2:
                 quantise(0, 0, S_HALF, woven_early[:])
             if d < PACK - 1:
-                cut = T_HALF if d == 2 else 0
-                if cut:
+                cut = T_HALF if d != 1 else 0
+                if d == 2:
                     nc.scalar.copy(token_rows[d][:, 0:cut], x_rows[d][:, 0:cut])
                 nc.gpsimd.tensor_scalar(token_rows[d][:, cut:T], x_rows[d][:, cut:T], 1.0, 0.0, MULT, mybir.AluOpType.add)
             nc.vector.tensor_copy(first_values[:, :, d], gathered(x_rows[d], 0, G))

@@ -102,12 +102,13 @@ def tile_moe_two_lin_relu2_kernel(tc, xT, w_words, w_scales, b, gate, offs, dst,
             nc.sync.dma_start(gate_sb[:, s0:s1], gate[0:P, s0:s1])
 
         load_weight_scales(0, 2, 0, 2 * P)
-        w_first = load_first_weights(0, 1)
-        nc.sync.dma_start(out=b_sb[:], in_=b.rearrange("(t p) e -> p t e", p=P))
-        w_first = w_first + load_first_weights(1, 2)
+        w_first = load_first_weights(0, 2)
+        b_rows = b.rearrange("(t p) e -> p t e", p=P)
+        nc.sync.dma_start(out=b_sb[:, 0:2, :], in_=b_rows[:, 0:2, :])
         load_gate(0, G)
-        load_weight_scales(0, 2, 2 * P, N)
         w_first = w_first + load_first_weights(2, N_TILES)
+        load_weight_scales(0, 2, 2 * P, N)
+        nc.sync.dma_start(out=b_sb[:, 2:N_TILES, :], in_=b_rows[:, 2:N_TILES, :])
         load_weight_scales(2, 4)
         load_weights(1)
         load_gate(G, S)
@@ -201,6 +202,34 @@ def tile_moe_two_lin_relu2_kernel(tc, xT, w_words, w_scales, b, gate, offs, dst,
 
         y_sb = [keep.tile([P, S], F32, name=f"y_sb{t}") for t in range(N_TILES)]
 
+        def product(acc, t, e, a):
+            words = w_first[t] if e < 2 else w_sb[e // 2][:, :, 2 * t * P : 2 * (t + 1) * P]
+            nc.tensor.matmul_mx(
+                out=acc,
+                lhsT=words[:, PASSES * (e % 2) + a, :].bitcast(E2M1X4),
+                lhsT_scale=w_scale_sb[:, PASSES * e + a, t * P : (t + 1) * P],
+                rhs=codes(a, e * C, (e + 1) * C).bitcast(E4M3X4),
+                rhs_scale=scales[a][:, e * C : (e + 1) * C],
+                start=(a == 0),
+                stop=(a == PASSES - 1),
+            )
+
+        def first_tile_of(g, relu_bytes):
+            pair = (2 * g, 2 * g + 1)
+            accs = [psum.tile([P, C], F32, name="acc") for e in pair]
+            for a in range(PASSES):
+                for acc, e in zip(accs, pair):
+                    product(acc[:], 0, e, a)
+            if relu_bytes is None:
+                relu_tile = work.tile([P, G], F32, name="relu_tile")
+                relu = relu_tile[:]
+            else:
+                relu = relu_bytes.bitcast(F32)
+            for i, e in enumerate(pair):
+                nc.scalar.activation(relu[:, i * C : (i + 1) * C], accs[i][:], ACT.Relu, bias=b_sb[:, 0, e : e + 1])
+            for i, e in enumerate(pair):
+                nc.scalar.activation(y_sb[0][:, e * C : (e + 1) * C], relu[:, i * C : (i + 1) * C], ACT.Square)
+
         def experts(t, s0, s1, relu_bytes=None, y_bytes=None):
             acc = psum.tile([P, s1 - s0], F32, name="acc")
             if relu_bytes is None:
@@ -210,18 +239,8 @@ def tile_moe_two_lin_relu2_kernel(tc, xT, w_words, w_scales, b, gate, offs, dst,
                 relu = relu_bytes.bitcast(F32)
             columns = {e: slice(e * C - s0, (e + 1) * C - s0) for e in range(s0 // C, s1 // C)}
             for e, local in columns.items():
-                slots = slice(e * C, (e + 1) * C)
-                words = w_first[t] if e < 2 else w_sb[e // 2][:, :, 2 * t * P : 2 * (t + 1) * P]
                 for a in range(PASSES):
-                    nc.tensor.matmul_mx(
-                        out=acc[:, local],
-                        lhsT=words[:, PASSES * (e % 2) + a, :].bitcast(E2M1X4),
-                        lhsT_scale=w_scale_sb[:, PASSES * e + a, t * P : (t + 1) * P],
-                        rhs=codes(a, e * C, (e + 1) * C).bitcast(E4M3X4),
-                        rhs_scale=scales[a][:, slots],
-                        start=(a == 0),
-                        stop=(a == PASSES - 1),
-                    )
+                    product(acc[:, local], t, e, a)
             for e, local in columns.items():
                 nc.scalar.activation(relu[:, local], acc[:, local], ACT.Relu, bias=b_sb[:, t, e : e + 1])
             y = y_sb[t][:, s0:s1] if y_bytes is None else y_bytes.bitcast(F32)
@@ -237,8 +256,7 @@ def tile_moe_two_lin_relu2_kernel(tc, xT, w_words, w_scales, b, gate, offs, dst,
 
         for d in (0, 1):
             gather_row(d, G, 3 * G)
-        experts(0, 0, C, late_pairs(1, G, G + C))
-        experts(0, C, G, late_pairs(1, G + C, 2 * G))
+        first_tile_of(0, late_pairs(1, G, 2 * G))
         scatter(0, 0, G)
         scatter(1, 0, G, experts(1, 0, G, late_pairs(1, G, 2 * G)))
         gather_row(2, G, 2 * G)
@@ -249,8 +267,7 @@ def tile_moe_two_lin_relu2_kernel(tc, xT, w_words, w_scales, b, gate, offs, dst,
         scatter(3, 0, G, experts(3, 0, G, late_pairs(0, 3 * G, S), late_pairs(0, G, 2 * G)))
         gather_row(0, 3 * G, S)
 
-        experts(0, G, G + C, late_pairs(1, 2 * G, 2 * G + C))
-        experts(0, G + C, 2 * G, late_pairs(1, 2 * G + C, 3 * G))
+        first_tile_of(1, late_pairs(1, 2 * G, 3 * G))
         scatter(0, G, 2 * G)
         gather_row(2, 2 * G, 3 * G)
         scatter(1, G, 2 * G, experts(1, G, 2 * G))
@@ -268,8 +285,7 @@ def tile_moe_two_lin_relu2_kernel(tc, xT, w_words, w_scales, b, gate, offs, dst,
         weave_late(3 * G, S)
         quantise(1, 3 * G, S, late_woven(3 * G, S))
         scatter(2, 2 * G, 3 * G, experts(2, 2 * G, 3 * G, None, late_pairs(0, 3 * G, S)))
-        experts(0, 3 * G, 3 * G + C)
-        experts(0, 3 * G + C, S)
+        first_tile_of(3, None)
         for t in range(N_TILES):
             s0 = 2 * G if t == N_TILES - 1 else 3 * G
             if t > 0:

@@ -183,7 +183,7 @@ def tile_moe_two_lin_relu2_kernel(tc, xT, w_words, w_scales, b, gate, offs, dst,
             nc.vector.tensor_copy(first_values[:, :, d], gathered(x_rows[d], 0, G))
         for s0 in (0, C):
             quantise(1, s0, s0 + C, first_woven[:, 2 * s0 : 2 * (s0 + C)])
-        nc.vector.tensor_copy(token_rows[3], x_rows[3][:])
+        nc.vector.tensor_copy(token_rows[3][:, 0 : T - G], x_rows[3][:, 0 : T - G])
         quantise(0, S_HALF, S, woven0[:])
 
         def late_pairs(h, s0, s1):
@@ -214,21 +214,16 @@ def tile_moe_two_lin_relu2_kernel(tc, xT, w_words, w_scales, b, gate, offs, dst,
                 stop=(a == PASSES - 1),
             )
 
-        def first_tile_of(g, relu_bytes):
+        def first_tile_of(g, relus):
             pair = (2 * g, 2 * g + 1)
             accs = [psum.tile([P, C], F32, name="acc") for e in pair]
             for a in range(PASSES):
                 for acc, e in zip(accs, pair):
                     product(acc[:], 0, e, a)
-            if relu_bytes is None:
-                relu_tile = work.tile([P, G], F32, name="relu_tile")
-                relu = relu_tile[:]
-            else:
-                relu = relu_bytes.bitcast(F32)
-            for i, e in enumerate(pair):
-                nc.scalar.activation(relu[:, i * C : (i + 1) * C], accs[i][:], ACT.Relu, bias=b_sb[:, 0, e : e + 1])
-            for i, e in enumerate(pair):
-                nc.scalar.activation(y_sb[0][:, e * C : (e + 1) * C], relu[:, i * C : (i + 1) * C], ACT.Square)
+            for relu, acc, e in zip(relus, accs, pair):
+                nc.scalar.activation(relu, acc[:], ACT.Relu, bias=b_sb[:, 0, e : e + 1])
+            for relu, e in zip(relus, pair):
+                nc.scalar.activation(y_sb[0][:, e * C : (e + 1) * C], relu, ACT.Square)
 
         def experts(t, s0, s1, relu_bytes=None, y_bytes=None):
             acc = psum.tile([P, s1 - s0], F32, name="acc")
@@ -254,41 +249,30 @@ def tile_moe_two_lin_relu2_kernel(tc, xT, w_words, w_scales, b, gate, offs, dst,
         def store(t):
             nc.sync.dma_start(out=out[t * P : (t + 1) * P, :], in_=out_sb[t][:])
 
-        for d in (0, 1):
-            gather_row(d, G, 3 * G)
-        first_tile_of(0, late_pairs(1, G, 2 * G))
+        cut = 2 * G + T // 8
+        first_relu = keep.tile([P, G], F32, name="first_relu")
+        for d in range(PACK - 1):
+            gather_row(d, G, 2 * G)
+        first_tile_of(0, (first_relu[:, 0:C], token_rows[3][:, T - G : T].bitcast(F32)))
         scatter(0, 0, G)
-        scatter(1, 0, G, experts(1, 0, G, late_pairs(1, G, 2 * G)))
-        gather_row(2, G, 2 * G)
-        scatter(2, 0, G, experts(2, 0, G))
-        gather_row(3, G, 2 * G)
-        weave_late(G, 2 * G)
-        quantise(1, G, 2 * G, late_woven(G, 2 * G))
-        scatter(3, 0, G, experts(3, 0, G, late_pairs(0, 3 * G, S), late_pairs(0, G, 2 * G)))
-        gather_row(0, 3 * G, S)
-
-        first_tile_of(1, late_pairs(1, 2 * G, 3 * G))
-        scatter(0, G, 2 * G)
-        gather_row(2, 2 * G, 3 * G)
-        scatter(1, G, 2 * G, experts(1, G, 2 * G))
-        gather_row(3, 2 * G, 3 * G)
-        weave_late(2 * G, 3 * G)
-        quantise(1, 2 * G, 3 * G, late_woven(2 * G, 3 * G))
-        scatter(2, G, 2 * G, experts(2, G, 2 * G, None, late_pairs(0, 2 * G, 3 * G)))
-        scatter(3, G, 2 * G, experts(3, G, 2 * G))
-        gather_row(1, 3 * G, S)
-
-        scatter(0, 2 * G, 3 * G, experts(0, 2 * G, 3 * G, late_pairs(1, 3 * G, S)))
-        gather_row(2, 3 * G, S)
-        scatter(1, 2 * G, 3 * G, experts(1, 2 * G, 3 * G))
-        gather_row(3, 3 * G, S)
-        weave_late(3 * G, S)
-        quantise(1, 3 * G, S, late_woven(3 * G, S))
-        scatter(2, 2 * G, 3 * G, experts(2, 2 * G, 3 * G, None, late_pairs(0, 3 * G, S)))
-        first_tile_of(3, None)
+        for g in range(GROUPS - 1):
+            s0, s1, s2 = g * G, (g + 1) * G, (g + 2) * G
+            if g == 0:
+                scatter(1, s0, s1, experts(1, s0, s1, first_relu[:]))
+                nc.scalar.copy(token_rows[3][:, T - G : T], x_rows[3][:, T - G : T])
+            else:
+                for d in (0, 1):
+                    gather_row(d, s1, s2)
+                scatter(0, s0, s1, experts(0, s0, s1, late_pairs(1, s1, s2)))
+                gather_row(2, s1, s2)
+                scatter(1, s0, s1, experts(1, s0, s1))
+            gather_row(3, s1, s2)
+            weave_late(s1, s2)
+            quantise(1, s1, s2, late_woven(s1, s2))
+            scatter(2, s0, s1, experts(2, s0, s1, None, late_pairs(0, s1, s2)))
+            experts(3, s0, s1, late_pairs(0, s2, s2 + G) if s2 < S else None)
+            scatter(3, s0, s1 if s2 < S else cut)
         for t in range(N_TILES):
-            s0 = 2 * G if t == N_TILES - 1 else 3 * G
-            if t > 0:
-                experts(t, s0, S)
-            scatter(t, s0, S)
+            experts(t, S - G, S)
+            scatter(t, cut if t == N_TILES - 1 else S - G, S)
             store(t)

@@ -24,13 +24,19 @@ E4M3X4 = mybir.dt.float8_e4m3fn_x4
 E2M1X4 = mybir.dt.float4_e2m1fn_x4
 ACT = mybir.ActivationFunctionType
 MULT = mybir.AluOpType.mult
+ADD = mybir.AluOpType.add
 
 G = 2 * C
 GROUPS = S // G
+LATE = S - G
 S_HALF = S // 2
 T_HALF = T // 2
 
-PIECES = (((768, 320), (T, 320)), ((768, 448), (T, 304)))
+SCALAR_TOKENS = ((320, 320), (448, 304))
+ROW_CUTS = (G, 576, 800, S)
+ROW2_SCALAR = 960
+HELD = 128
+LAST_CUT = 2 * G + T // 8
 
 
 def tile_moe_two_lin_relu2_kernel(tc, xT, w_words, w_scales, b, gate, offs, dst, out):
@@ -38,8 +44,13 @@ def tile_moe_two_lin_relu2_kernel(tc, xT, w_words, w_scales, b, gate, offs, dst,
     with ExitStack() as ctx:
         keep = ctx.enter_context(tc.tile_pool(name="keep", bufs=1))
         work = ctx.enter_context(tc.tile_pool(name="work", bufs=4))
-        late = ctx.enter_context(tc.tile_pool(name="late", bufs=1))
+        placed = ctx.enter_context(tc.tile_pool(name="placed", bufs=1))
         psum = ctx.enter_context(tc.psum_pool(name="psum", bufs=8))
+
+        codes0_late_at = 0
+        first_woven_at = 4 * G
+        row3_at = 8 * G
+        x_row1_at = row3_at + 4 * S
 
         offs_sb = keep.tile([P, S // LIST], U16, name="offs_sb")
         dst_sb = keep.tile([P, S // LIST], U16, name="dst_sb")
@@ -52,20 +63,14 @@ def tile_moe_two_lin_relu2_kernel(tc, xT, w_words, w_scales, b, gate, offs, dst,
         def pass_rows(a):
             return xT[a * K_PASS : (a + 1) * K_PASS, :].rearrange("(p d) t -> p (d t)", d=PACK)
 
-        def load_pair(u):
-            x = keep.tile([P, 2 * T], F32, name=f"x_pair{u}", align_bytes=64)
-            run = pass_rows(u // 2)[:, 2 * (u % 2) * T : 2 * (u % 2 + 1) * T]
-            ends = [T + t1 for t1, share in PIECES[u]]
-            for c0, c1 in zip([0] + ends, ends):
+        def load_pair(h):
+            x = keep.tile([P, 2 * T], F32, name=f"x_pair{h}", align_bytes=64)
+            run = pass_rows(0)[:, 2 * h * T : 2 * (h + 1) * T]
+            for c0, c1 in ((0, T + T_HALF), (T + T_HALF, 2 * T)):
                 nc.sync.dma_start(out=x[:, c0:c1], in_=run[:, c0:c1])
             return x[:].rearrange("p (e t) -> p t e", e=2)
 
-        def load_row(d):
-            if d == 1:
-                x = late.tile([P, T], F32, name="x_row1", align_bytes=64, offset=8 * S)
-            else:
-                x = keep.tile([P, T], F32, name=f"x_row{d}", align_bytes=64)
-            width = T_HALF if d == 0 else T
+        def load_row(d, x, width):
             for t0 in range(0, T, width):
                 nc.sync.dma_start(out=x[:, t0 : t0 + width], in_=pass_rows(1)[:, d * T + t0 : d * T + t0 + width])
             return x
@@ -74,7 +79,12 @@ def tile_moe_two_lin_relu2_kernel(tc, xT, w_words, w_scales, b, gate, offs, dst,
         nc.sync.dma_start(offs_sb[:], offs)
         nc.sync.dma_start(dst_sb[:], dst)
         x_pairs.append(load_pair(1))
-        x_rows = [load_row(d) for d in range(PACK)]
+        x_rows = [
+            load_row(0, keep.tile([P, T], F32, name="x_row0", align_bytes=64), T_HALF),
+            load_row(1, placed.tile([P, T], F32, name="x_row1", align_bytes=64, offset=x_row1_at), T),
+            load_row(2, keep.tile([P, T], F32, name="x_row2", align_bytes=64), T),
+            load_row(3, keep.tile([P, T], F32, name="x_row3", align_bytes=64), T),
+        ]
 
         nc.gpsimd.memset(w_scale_sb[:].rearrange("p g n -> p (g n)").bitcast(I32), 0)
         for t in (0, 3):
@@ -91,62 +101,67 @@ def tile_moe_two_lin_relu2_kernel(tc, xT, w_words, w_scales, b, gate, offs, dst,
             nc.sync.dma_start(out=w_part[:].bitcast(I32), in_=words.bitcast(I32))
             return [w_part[:, :, 2 * (t - t0) * P : 2 * (t - t0 + 1) * P] for t in range(t0, t1)]
 
-        def load_weight_scales(e0, e1, n0=0, n1=N):
+        def load_weight_scales(e0, e1, t0, t1):
             for r in range(4):
                 nc.sync.dma_start(
-                    out=w_scale_sb[r:P:32, PASSES * e0 : PASSES * e1, n0:n1].bitcast(I32),
-                    in_=w_scales[e0:e1, :, r:16:4, n0:n1].rearrange("e a q n -> q (e a) n").bitcast(I32),
+                    out=w_scale_sb[r:P:32, PASSES * e0 : PASSES * e1, t0 * P : t1 * P].bitcast(I32),
+                    in_=w_scales[e0:e1, :, r:16:4, t0 * P : t1 * P].rearrange("e a q n -> q (e a) n").bitcast(I32),
                 )
+
+        def load_bias(t0, t1):
+            nc.sync.dma_start(out=b_sb[:, t0:t1, :], in_=b.rearrange("(t p) e -> p t e", p=P)[:, t0:t1, :])
 
         def load_gate(s0, s1):
             nc.sync.dma_start(gate_sb[:, s0:s1], gate[0:P, s0:s1])
 
-        load_weight_scales(0, 2, 0, 2 * P)
+        load_weight_scales(0, 2, 0, 2)
         w_first = load_first_weights(0, 2)
-        b_rows = b.rearrange("(t p) e -> p t e", p=P)
-        nc.sync.dma_start(out=b_sb[:, 0:2, :], in_=b_rows[:, 0:2, :])
+        load_bias(0, 2)
         load_gate(0, G)
         w_first = w_first + load_first_weights(2, N_TILES)
-        load_weight_scales(0, 2, 2 * P, N)
-        nc.sync.dma_start(out=b_sb[:, 2:N_TILES, :], in_=b_rows[:, 2:N_TILES, :])
-        load_weight_scales(2, 4)
+        load_weight_scales(0, 2, 2, N_TILES)
+        load_bias(2, N_TILES)
+        load_weight_scales(2, 4, 0, N_TILES)
         load_weights(1)
         load_gate(G, S)
-        load_weight_scales(4, E)
+        load_weight_scales(4, E, 0, N_TILES)
         load_weights(2)
         load_weights(3)
 
-        token_pairs = [keep.tile([P, T], U32, name=f"token_pairs{u}") for u in range(len(x_pairs))]
-        codes_early = late.tile([P, S_HALF], U32, name="codes_early", align_bytes=64, offset=8 * S)
+        token_pairs = [keep.tile([P, T], U32, name=f"token_pairs{h}") for h in range(2)]
+        codes0_early = placed.tile([P, S_HALF], U32, name="codes0_early", align_bytes=64, offset=x_row1_at)
         codes1 = keep.tile([P, S], U32, name="codes1", align_bytes=64)
         scales = [keep.tile([P, S], U8, name=f"scales{a}", align_bytes=64) for a in range(PASSES)]
-        woven_early = late.tile([P, S], U32, name="woven_early", align_bytes=64, offset=0)
-        third_row = late.tile([P, T], BF16, name="third_row", align_bytes=64, offset=0)
-        codes_late = late.tile([P, S_HALF], U32, name="codes_late", align_bytes=64, offset=2 * T)
-        first_tile = late.tile([P, 2 * G], U32, name="first_tile", align_bytes=64, offset=4 * S)
-        last_row = late.tile([P, T], BF16, name="last_row", align_bytes=64, offset=2 * T + 2 * S)
-        token_rows = [keep.tile([P, T], BF16, name=f"token_rows{d}")[:] for d in (0, 1)] + [third_row[:], last_row[:]]
+        row2_and_woven = keep.tile([P, ROW2_SCALAR // 2 + S], U32, name="row2_and_woven", align_bytes=64)
+        woven0_early = row2_and_woven[:, ROW2_SCALAR // 2 : ROW2_SCALAR // 2 + S]
+        codes0_late = placed.tile([P, S_HALF], U32, name="codes0_late", align_bytes=64, offset=codes0_late_at)
+        first_woven = placed.tile([P, 2 * G], U32, name="first_woven", align_bytes=64, offset=first_woven_at)
+        row3 = placed.tile([P, T - HELD + 2 * C], BF16, name="row3", align_bytes=64, offset=row3_at)
+        token_rows = [keep.tile([P, T], BF16, name=f"token_rows{d}")[:] for d in (0, 1)]
+        token_rows = token_rows + [row2_and_woven[:, 0:T_HALF].bitcast(BF16), row3[:, 0:T]]
         pairs0 = keep.tile([P, 2, S], U32, name="pairs0")
-        woven0 = keep.tile([P, S], U32, name="woven0", align_bytes=64)
-        pairs1 = keep.tile([P, 2 * (S - G)], U32, name="pairs1", align_bytes=64)
-        woven1 = keep.tile([P, 2 * (S - G)], U32, name="woven1", align_bytes=64)
+        woven0_late = keep.tile([P, S], U32, name="woven0_late", align_bytes=64)
+        pairs1 = keep.tile([P, LATE + ROW_CUTS[2]], U32, name="pairs1", align_bytes=64)
+        woven1 = keep.tile([P, 2 * LATE], U32, name="woven1", align_bytes=64)
 
         def codes(a, s0, s1):
             if a == 1:
                 return codes1[:, s0:s1]
             if s0 < S_HALF:
-                return codes_early[:, s0:s1]
-            return codes_late[:, s0 - S_HALF : s1 - S_HALF]
+                return codes0_early[:, s0:s1]
+            return codes0_late[:, s0 - S_HALF : s1 - S_HALF]
 
-        def round_pair(u, piece):
-            rounded = token_pairs[u][:].bitcast(BF16).rearrange("p (t e) -> p t e", e=2)
-            t0 = PIECES[u][piece - 1][0] if piece > 0 else 0
-            t1, share = PIECES[u][piece]
-            cut = t0 + share
-            if cut > t0:
-                nc.scalar.copy(rounded[:, t0:cut, :], x_pairs[u][:, t0:cut, :])
-            if cut < t1:
-                nc.vector.tensor_copy(rounded[:, cut:t1, :], x_pairs[u][:, cut:t1, :])
+        def by_slot(woven):
+            return woven.rearrange("p (s h) -> p s h", h=2)
+
+        def round_pair(h):
+            rounded = token_pairs[h][:].bitcast(BF16).rearrange("p (t e) -> p t e", e=2)
+            for t0, share in zip((0, T_HALF), SCALAR_TOKENS[h]):
+                nc.scalar.copy(rounded[:, t0 : t0 + share, :], x_pairs[h][:, t0 : t0 + share, :])
+                nc.vector.tensor_copy(rounded[:, t0 + share : t0 + T_HALF, :], x_pairs[h][:, t0 + share : t0 + T_HALF, :])
+
+        def round_on_gpsimd(d, t0):
+            nc.gpsimd.tensor_scalar(token_rows[d][:, t0:T], x_rows[d][:, t0:T], 1.0, 0.0, MULT, ADD)
 
         def gathered(window, s0, s1):
             return window[:, :].indirect(offs_sb[:, s0 // LIST : s1 // LIST])
@@ -156,38 +171,8 @@ def tile_moe_two_lin_relu2_kernel(tc, xT, w_words, w_scales, b, gate, offs, dst,
                 out=codes(a, s0, s1).bitcast(E4M3X4), scales=scales[a][:, s0:s1], in_=woven.bitcast(BF16)
             )
 
-        first_woven = first_tile[:]
-        first_values = first_woven.bitcast(BF16).rearrange("p (s d) -> p s d", d=PACK)
-
-        for piece in range(len(PIECES[0])):
-            round_pair(0, piece)
-        nc.vector.tensor_copy(pairs0[:, 0, :], gathered(token_pairs[0], 0, S))
-        out_sb[2] = keep.tile([P, T], F32, name="x_pair0", align_bytes=64)
-        nc.scalar.activation(out_sb[2][:], out_sb[0][:], ACT.Square)
-        round_pair(1, 0)
-        round_pair(1, 1)
-        for s0 in (0, S_HALF):
-            nc.vector.tensor_copy(pairs0[:, 1, s0 : s0 + S_HALF], gathered(token_pairs[1], s0, s0 + S_HALF))
-        pairs0_words = pairs0[:].rearrange("p h s -> p s h")
-        nc.scalar.copy(token_rows[0][:, 0:T_HALF], x_rows[0][:, 0:T_HALF])
-        nc.scalar.copy(woven_early[:].rearrange("p (s h) -> p s h", h=2), pairs0_words[:, 0:S_HALF, :])
-        nc.scalar.copy(woven0[:].rearrange("p (s h) -> p s h", h=2), pairs0_words[:, S_HALF:S, :])
-        for d in range(PACK):
-            if d == 2:
-                quantise(0, 0, S_HALF, woven_early[:])
-            if d < PACK - 1:
-                cut = T_HALF if d != 1 else 0
-                if d == 2:
-                    nc.scalar.copy(token_rows[d][:, 0:cut], x_rows[d][:, 0:cut])
-                nc.gpsimd.tensor_scalar(token_rows[d][:, cut:T], x_rows[d][:, cut:T], 1.0, 0.0, MULT, mybir.AluOpType.add)
-            nc.vector.tensor_copy(first_values[:, :, d], gathered(x_rows[d], 0, G))
-        for s0 in (0, C):
-            quantise(1, s0, s0 + C, first_woven[:, 2 * s0 : 2 * (s0 + C)])
-        nc.vector.tensor_copy(token_rows[3][:, 0 : T - G], x_rows[3][:, 0 : T - G])
-        quantise(0, S_HALF, S, woven0[:])
-
         def late_pairs(h, s0, s1):
-            return pairs1[:, h * (S - G) + s0 - G : h * (S - G) + s1 - G]
+            return pairs1[:, h * LATE + s0 - G : h * LATE + s1 - G]
 
         def late_woven(s0, s1):
             return woven1[:, 2 * (s0 - G) : 2 * (s1 - G)]
@@ -197,8 +182,36 @@ def tile_moe_two_lin_relu2_kernel(tc, xT, w_words, w_scales, b, gate, offs, dst,
             nc.scalar.activation(pairs[:, :, d % 2], gathered(token_rows[d], s0, s1), ACT.Copy)
 
         def weave_late(s0, s1):
-            low_high = pairs1[:].rearrange("p (h s) -> p s h", h=2)
-            nc.scalar.copy(late_woven(s0, s1).rearrange("p (s h) -> p s h", h=2), low_high[:, s0 - G : s1 - G, :])
+            low_high = pairs1[:, 0 : 2 * LATE].rearrange("p (h s) -> p s h", h=2)
+            nc.scalar.copy(by_slot(late_woven(s0, s1)), low_high[:, s0 - G : s1 - G, :])
+
+        round_pair(0)
+        nc.vector.tensor_copy(pairs0[:, 0, :], gathered(token_pairs[0], 0, S))
+        out_sb[2] = keep.tile([P, T], F32, name="x_pair0", align_bytes=64)
+        nc.scalar.activation(out_sb[2][:], out_sb[0][:], ACT.Square)
+        round_pair(1)
+        for s0 in range(0, S, G):
+            nc.vector.tensor_copy(pairs0[:, 1, s0 : s0 + G], gathered(token_pairs[1], s0, s0 + G))
+        nc.scalar.copy(token_rows[0][:, 0:T_HALF], x_rows[0][:, 0:T_HALF])
+        round_on_gpsimd(0, T_HALF)
+        round_on_gpsimd(1, 0)
+        for s0 in range(0, S, G):
+            woven = woven0_early if s0 < S_HALF else woven0_late[:]
+            at = s0 % S_HALF
+            nc.scalar.copy(by_slot(woven)[:, at : at + G, :], pairs0[:].rearrange("p h s -> p s h")[:, s0 : s0 + G, :])
+
+        gather_row(0, ROW_CUTS[0], ROW_CUTS[1])
+        nc.scalar.copy(token_rows[2][:, 0:ROW2_SCALAR], x_rows[2][:, 0:ROW2_SCALAR])
+        first_values = first_woven[:].bitcast(BF16).rearrange("p (s d) -> p s d", d=PACK)
+        for d in range(PACK):
+            if d == 2:
+                quantise(0, 0, S_HALF, woven0_early)
+                round_on_gpsimd(2, ROW2_SCALAR)
+            nc.vector.tensor_copy(first_values[:, :, d], gathered(x_rows[d], 0, G))
+        for s0 in (0, C):
+            quantise(1, s0, s0 + C, first_woven[:, 2 * s0 : 2 * (s0 + C)])
+        nc.vector.tensor_copy(token_rows[3][:, 0 : T - HELD], x_rows[3][:, 0 : T - HELD])
+        quantise(0, S_HALF, S, woven0_late[:])
 
         y_sb = [keep.tile([P, S], F32, name=f"y_sb{t}") for t in range(N_TILES)]
 
@@ -214,65 +227,67 @@ def tile_moe_two_lin_relu2_kernel(tc, xT, w_words, w_scales, b, gate, offs, dst,
                 stop=(a == PASSES - 1),
             )
 
-        def first_tile_of(g, relus):
-            pair = (2 * g, 2 * g + 1)
-            accs = [psum.tile([P, C], F32, name="acc") for e in pair]
-            for a in range(PASSES):
-                for acc, e in zip(accs, pair):
-                    product(acc[:], 0, e, a)
-            for relu, acc, e in zip(relus, accs, pair):
-                nc.scalar.activation(relu, acc[:], ACT.Relu, bias=b_sb[:, 0, e : e + 1])
-            for relu, e in zip(relus, pair):
-                nc.scalar.activation(y_sb[0][:, e * C : (e + 1) * C], relu, ACT.Square)
+        def relu_of(relu, acc, t, e):
+            nc.scalar.activation(relu, acc, ACT.Relu, bias=b_sb[:, t, e : e + 1])
 
-        def experts(t, s0, s1, relu_bytes=None, y_bytes=None):
-            acc = psum.tile([P, s1 - s0], F32, name="acc")
+        def experts(t, g, relu_bytes=None, y_bytes=None):
+            acc = psum.tile([P, G], F32, name="acc")
             if relu_bytes is None:
-                relu_tile = work.tile([P, s1 - s0], F32, name="relu_tile")
+                relu_tile = work.tile([P, G], F32, name="relu_tile")
                 relu = relu_tile[:]
             else:
                 relu = relu_bytes.bitcast(F32)
-            columns = {e: slice(e * C - s0, (e + 1) * C - s0) for e in range(s0 // C, s1 // C)}
-            for e, local in columns.items():
+            for i in range(2):
                 for a in range(PASSES):
-                    product(acc[:, local], t, e, a)
-            for e, local in columns.items():
-                nc.scalar.activation(relu[:, local], acc[:, local], ACT.Relu, bias=b_sb[:, t, e : e + 1])
-            y = y_sb[t][:, s0:s1] if y_bytes is None else y_bytes.bitcast(F32)
+                    product(acc[:, i * C : (i + 1) * C], t, 2 * g + i, a)
+            for i in range(2):
+                relu_of(relu[:, i * C : (i + 1) * C], acc[:, i * C : (i + 1) * C], t, 2 * g + i)
+            y = y_sb[t][:, g * G : (g + 1) * G] if y_bytes is None else y_bytes.bitcast(F32)
             nc.scalar.activation(y, relu, ACT.Square)
             return y
 
-        def scatter(t, s0, s1, y=None):
+        def scatter(t, s0, s1, y):
             window = out_sb[t][:].indirect(dst_sb[:, s0 // LIST : s1 // LIST])
-            nc.vector.tensor_tensor(window, y_sb[t][:, s0:s1] if y is None else y, gate_sb[:, s0:s1], MULT)
+            nc.vector.tensor_tensor(window, y, gate_sb[:, s0:s1], MULT)
 
-        def store(t):
-            nc.sync.dma_start(out=out[t * P : (t + 1) * P, :], in_=out_sb[t][:])
-
-        cut = 2 * G + T // 8
         first_relu = keep.tile([P, G], F32, name="first_relu")
-        for d in range(PACK - 1):
-            gather_row(d, G, 2 * G)
-        first_tile_of(0, (first_relu[:, 0:C], token_rows[3][:, T - G : T].bitcast(F32)))
-        scatter(0, 0, G)
+        for d in (1, 2):
+            gather_row(d, ROW_CUTS[0], ROW_CUTS[1])
+        accs = [psum.tile([P, C], F32, name="acc") for e in range(2)]
+        for a in range(PASSES):
+            for e in range(2):
+                product(accs[e][:], 0, e, a)
+        relus = (first_relu[:, 0:C], row3[:, T - HELD : T - HELD + 2 * C].bitcast(F32))
+        for e in range(2):
+            relu_of(relus[e], accs[e][:], 0, e)
+        for e in range(2):
+            nc.scalar.activation(y_sb[0][:, e * C : (e + 1) * C], relus[e], ACT.Square)
+        scatter(0, 0, G, y_sb[0][:, 0:G])
+
         for g in range(GROUPS - 1):
             s0, s1, s2 = g * G, (g + 1) * G, (g + 2) * G
             if g == 0:
-                scatter(1, s0, s1, experts(1, s0, s1, first_relu[:]))
-                nc.scalar.copy(token_rows[3][:, T - G : T], x_rows[3][:, T - G : T])
+                scatter(1, s0, s1, experts(1, g, first_relu[:]))
+                nc.scalar.copy(token_rows[3][:, T - HELD : T], x_rows[3][:, T - HELD : T])
             else:
+                c0, c1 = ROW_CUTS[g], ROW_CUTS[g + 1]
                 for d in (0, 1):
-                    gather_row(d, s1, s2)
-                scatter(0, s0, s1, experts(0, s0, s1, late_pairs(1, s1, s2)))
-                gather_row(2, s1, s2)
-                scatter(1, s0, s1, experts(1, s0, s1))
+                    gather_row(d, c0, c1)
+                scatter(0, s0, s1, experts(0, g, late_pairs(1, c0, c0 + G)))
+                gather_row(2, c0, c1)
+                scatter(1, s0, s1, experts(1, g))
             gather_row(3, s1, s2)
             weave_late(s1, s2)
             quantise(1, s1, s2, late_woven(s1, s2))
-            scatter(2, s0, s1, experts(2, s0, s1, None, late_pairs(0, s1, s2)))
-            experts(3, s0, s1, late_pairs(0, s2, s2 + G) if s2 < S else None)
-            scatter(3, s0, s1 if s2 < S else cut)
+            scatter(2, s0, s1, experts(2, g, None, late_pairs(0, s1, s2)))
+            if s2 < S:
+                scatter(3, s0, s1, experts(3, g, late_pairs(0, ROW_CUTS[g + 1], ROW_CUTS[g + 1] + G)))
+            else:
+                experts(3, g)
+                scatter(3, s0, LAST_CUT, y_sb[3][:, s0:LAST_CUT])
+
         for t in range(N_TILES):
-            experts(t, S - G, S)
-            scatter(t, cut if t == N_TILES - 1 else S - G, S)
-            store(t)
+            experts(t, GROUPS - 1)
+            s0 = LAST_CUT if t == N_TILES - 1 else S - G
+            scatter(t, s0, S, y_sb[t][:, s0:S])
+            nc.sync.dma_start(out=out[t * P : (t + 1) * P, :], in_=out_sb[t][:])

@@ -25,81 +25,75 @@ E2M1X4 = mybir.dt.float4_e2m1fn_x4
 ACT = mybir.ActivationFunctionType
 MULT = mybir.AluOpType.mult
 ADD = mybir.AluOpType.add
+MAX = mybir.AluOpType.max
 
 G = 2 * C
-GROUPS = S // G
 LATE = S - G
 S_HALF = S // 2
 T_HALF = T // 2
+PAIRS = 2 * PASSES
+BIASES = N_TILES * E
 
-SCALAR_TOKENS = ((320, 320), (448, 304))
-ROW_CUTS = (G, 576, 800, S)
-ROW2_SCALAR = 960
-HELD = 128
-LAST_CUT = 2 * G + T // 8
+PIECES = ((T_HALF,), (512, 1024), (512, 1024), (512, 1024))
+SCALAR_TOKENS = (((0, 256), (768, 1024)), ((384, 512), (512, 896)), ((384, 512), (512, 960)), ((320, 512), (512, 960)))
+VECTOR_TOKENS = (((256, 768), (1024, T)), ((896, T),), ((960, T),), ((960, T),))
+GPSIMD_TOKENS = (0, 384, 384, 320)
+STAGES = ((0, G), (G, 2 * G), (2 * G, S))
+SCALAR_TILES = (0, 2)
+VECTOR_TILES = (1, 3)
 
 
 def tile_moe_two_lin_relu2_kernel(tc, xT, w_words, w_scales, b, gate, offs, dst, out):
     nc = tc.nc
     with ExitStack() as ctx:
         keep = ctx.enter_context(tc.tile_pool(name="keep", bufs=1))
-        work = ctx.enter_context(tc.tile_pool(name="work", bufs=4))
         placed = ctx.enter_context(tc.tile_pool(name="placed", bufs=1))
         psum = ctx.enter_context(tc.psum_pool(name="psum", bufs=8))
-
-        codes0_late_at = 0
-        first_woven_at = 4 * G
-        row3_at = 8 * G
-        x_row1_at = row3_at + 4 * S
 
         offs_sb = keep.tile([P, S // LIST], U16, name="offs_sb")
         dst_sb = keep.tile([P, S // LIST], U16, name="dst_sb")
         b_sb = keep.tile([P, N_TILES, E], F32, name="b_sb")
         gate_sb = keep.tile([P, S], F32, name="gate_sb")
-        w_sb = {g: keep.tile([P, 2 * PASSES, 2 * N], U8, name=f"w_sb{g}", align_bytes=64) for g in range(1, GROUPS)}
-        w_scale_sb = keep.tile([P, E * PASSES, N], U8, name="w_scale_sb", align_bytes=64)
-        out_sb = {t: keep.tile([P, T], F32, name=f"out_sb{t}") for t in (0, 1, 3)}
+        pairs1 = keep.tile([P, 2 * S], U32, name="pairs1", align_bytes=64)
 
-        def pass_rows(a):
-            return xT[a * K_PASS : (a + 1) * K_PASS, :].rearrange("(p d) t -> p (d t)", d=PACK)
+        def gate_of(s0, s1):
+            return gate_sb[:, s0:s1]
+
+        w_scale_sb = keep.tile([P, E * PASSES, N], U8, name="w_scale_sb", align_bytes=64)
+        out_sb = {t: keep.tile([P, T + BIASES], F32, name=f"out_sb{t}") for t in (0, 1, 3)}
 
         def load_pair(h):
-            x = keep.tile([P, 2 * T], F32, name=f"x_pair{h}", align_bytes=64)
-            run = pass_rows(0)[:, 2 * h * T : 2 * (h + 1) * T]
-            for c0, c1 in ((0, T + T_HALF), (T + T_HALF, 2 * T)):
+            if h == PAIRS - 1:
+                x = placed.tile([P, 2 * T], F32, name=f"x_pair{h}", align_bytes=64, offset=4 * S_HALF)
+            else:
+                x = keep.tile([P, 2 * T], F32, name=f"x_pair{h}", align_bytes=64)
+            a = h // 2
+            rows = xT[a * K_PASS : (a + 1) * K_PASS, :].rearrange("(p d) t -> p (d t)", d=PACK)
+            run = rows[:, 2 * (h % 2) * T : 2 * (h % 2 + 1) * T]
+            cuts = (0,) + tuple(T + c for c in PIECES[h]) + (2 * T,)
+            for c0, c1 in zip(cuts, cuts[1:]):
                 nc.sync.dma_start(out=x[:, c0:c1], in_=run[:, c0:c1])
             return x[:].rearrange("p (e t) -> p t e", e=2)
-
-        def load_row(d, x, width):
-            for t0 in range(0, T, width):
-                nc.sync.dma_start(out=x[:, t0 : t0 + width], in_=pass_rows(1)[:, d * T + t0 : d * T + t0 + width])
-            return x
 
         x_pairs = [load_pair(0)]
         nc.sync.dma_start(offs_sb[:], offs)
         nc.sync.dma_start(dst_sb[:], dst)
-        x_pairs.append(load_pair(1))
-        x_rows = [
-            load_row(0, keep.tile([P, T], F32, name="x_row0", align_bytes=64), T_HALF),
-            load_row(1, placed.tile([P, T], F32, name="x_row1", align_bytes=64, offset=x_row1_at), T),
-            load_row(2, keep.tile([P, T], F32, name="x_row2", align_bytes=64), T),
-            load_row(3, keep.tile([P, T], F32, name="x_row3", align_bytes=64), T),
-        ]
+        x_pairs = x_pairs + [load_pair(h) for h in range(1, PAIRS)]
 
         nc.gpsimd.memset(w_scale_sb[:].rearrange("p g n -> p (g n)").bitcast(I32), 0)
         for t in (0, 3):
-            nc.vector.memset(out_sb[t][:], 0.0)
-        nc.scalar.activation(out_sb[1][:], out_sb[0][:], ACT.Square)
+            nc.vector.memset(out_sb[t][:, 0:T].bitcast(I32), 0)
+        nc.scalar.activation(out_sb[1][:, 0:T], out_sb[0][:, 0:T], ACT.Square)
 
-        def load_weights(g):
-            words = w_words[2 * g : 2 * g + 2].rearrange("e a p c -> p (e a) c")
-            nc.sync.dma_start(out=w_sb[g][:].bitcast(I32), in_=words.bitcast(I32))
-
-        def load_first_weights(t0, t1):
-            words = w_words[0:2, :, :, 2 * t0 * P : 2 * t1 * P].rearrange("e a p c -> p (e a) c")
-            w_part = keep.tile([P, 2 * PASSES, 2 * (t1 - t0) * P], U8, name=f"w_first{t0}", align_bytes=64)
-            nc.sync.dma_start(out=w_part[:].bitcast(I32), in_=words.bitcast(I32))
-            return [w_part[:, :, 2 * (t - t0) * P : 2 * (t - t0 + 1) * P] for t in range(t0, t1)]
+        def load_weights(e0, e1, t0, t1):
+            words = w_words[e0:e1, :, :, 2 * t0 * P : 2 * t1 * P].rearrange("e a p c -> p (e a) c")
+            w = keep.tile([P, (e1 - e0) * PASSES, 2 * (t1 - t0) * P], U8, name=f"w{e0}_{t0}", align_bytes=64)
+            nc.sync.dma_start(out=w[:].bitcast(I32), in_=words.bitcast(I32))
+            return {
+                (e, t): w[:, PASSES * (e - e0) : PASSES * (e - e0 + 1), 2 * (t - t0) * P : 2 * (t - t0 + 1) * P]
+                for e in range(e0, e1)
+                for t in range(t0, t1)
+            }
 
         def load_weight_scales(e0, e1, t0, t1):
             for r in range(4):
@@ -112,37 +106,52 @@ def tile_moe_two_lin_relu2_kernel(tc, xT, w_words, w_scales, b, gate, offs, dst,
             nc.sync.dma_start(out=b_sb[:, t0:t1, :], in_=b.rearrange("(t p) e -> p t e", p=P)[:, t0:t1, :])
 
         def load_gate(s0, s1):
-            nc.sync.dma_start(gate_sb[:, s0:s1], gate[0:P, s0:s1])
+            nc.sync.dma_start(gate_of(s0, s1), gate[0:P, s0:s1])
 
-        load_weight_scales(0, 2, 0, 2)
-        w_first = load_first_weights(0, 2)
-        load_bias(0, 2)
+        w_sb = {}
+        load_weight_scales(0, 4, 0, N_TILES)
+        w_sb.update(load_weights(0, 2, 0, 2))
+        load_bias(0, N_TILES)
         load_gate(0, G)
-        w_first = w_first + load_first_weights(2, N_TILES)
-        load_weight_scales(0, 2, 2, N_TILES)
-        load_bias(2, N_TILES)
-        load_weight_scales(2, 4, 0, N_TILES)
-        load_weights(1)
+        w_sb.update(load_weights(0, 2, 2, N_TILES))
+        w_sb.update(load_weights(2, 4, 0, N_TILES))
         load_gate(G, S)
         load_weight_scales(4, E, 0, N_TILES)
-        load_weights(2)
-        load_weights(3)
+        w_sb.update(load_weights(4, E, 0, N_TILES))
 
-        token_pairs = [keep.tile([P, T], U32, name=f"token_pairs{h}") for h in range(2)]
-        codes0_early = placed.tile([P, S_HALF], U32, name="codes0_early", align_bytes=64, offset=x_row1_at)
+        token_pairs = [keep.tile([P, T], U32, name=f"token_pairs{h}") for h in range(PAIRS)]
+        pairs0 = keep.tile([P, 2 * S], U32, name="pairs0")
         codes1 = keep.tile([P, S], U32, name="codes1", align_bytes=64)
         scales = [keep.tile([P, S], U8, name=f"scales{a}", align_bytes=64) for a in range(PASSES)]
-        row2_and_woven = keep.tile([P, ROW2_SCALAR // 2 + S], U32, name="row2_and_woven", align_bytes=64)
-        woven0_early = row2_and_woven[:, ROW2_SCALAR // 2 : ROW2_SCALAR // 2 + S]
-        codes0_late = placed.tile([P, S_HALF], U32, name="codes0_late", align_bytes=64, offset=codes0_late_at)
-        first_woven = placed.tile([P, 2 * G], U32, name="first_woven", align_bytes=64, offset=first_woven_at)
-        row3 = placed.tile([P, T - HELD + 2 * C], BF16, name="row3", align_bytes=64, offset=row3_at)
-        token_rows = [keep.tile([P, T], BF16, name=f"token_rows{d}")[:] for d in (0, 1)]
-        token_rows = token_rows + [row2_and_woven[:, 0:T_HALF].bitcast(BF16), row3[:, 0:T]]
-        pairs0 = keep.tile([P, 2, S], U32, name="pairs0")
-        woven0_late = keep.tile([P, S], U32, name="woven0_late", align_bytes=64)
-        pairs1 = keep.tile([P, LATE + ROW_CUTS[2]], U32, name="pairs1", align_bytes=64)
-        woven1 = keep.tile([P, 2 * LATE], U32, name="woven1", align_bytes=64)
+        relu_sb = [keep.tile([P, S], F32, name=f"relu_sb{t}") for t in range(N_TILES)]
+        half_sb = [keep.tile([P, S], F32, name=f"half_sb{t}") for t in range(N_TILES)]
+        y_sb = [keep.tile([P, S], F32, name=f"y_sb{t}") for t in range(N_TILES)]
+        woven1 = keep.tile([P, 2 * S], U32, name="woven1", align_bytes=64)
+        second_woven = placed.tile([P, G], U32, name="second_woven", align_bytes=64, offset=0)
+        codes0_late = placed.tile([P, S_HALF], U32, name="codes0_late", align_bytes=64, offset=0)
+
+        def round_pair(h):
+            rounded = token_pairs[h][:].bitcast(BF16).rearrange("p (t e) -> p t e", e=2)
+            for t0, t1 in SCALAR_TOKENS[h]:
+                nc.scalar.copy(rounded[:, t0:t1, :], x_pairs[h][:, t0:t1, :])
+            if GPSIMD_TOKENS[h] > 0:
+                t1 = GPSIMD_TOKENS[h]
+                nc.gpsimd.tensor_scalar(rounded[:, 0:t1, :], x_pairs[h][:, 0:t1, :], 1.0, 0.0, MULT, ADD)
+            for t0, t1 in VECTOR_TOKENS[h]:
+                nc.vector.tensor_copy(rounded[:, t0:t1, :], x_pairs[h][:, t0:t1, :])
+
+        def gather(h, s0, s1):
+            pairs = (pairs0, pairs1)[h // 2]
+            at = (h % 2) * S
+            window = token_pairs[h][:, :].indirect(offs_sb[:, s0 // LIST : s1 // LIST])
+            nc.vector.tensor_copy(pairs[:, at + s0 : at + s1], window)
+
+        def weave(a, s0, s1, woven, on_vector=False):
+            low_high = (pairs0, pairs1)[a][:, 0 : 2 * S].rearrange("p (h s) -> p s h", h=2)
+            if on_vector:
+                nc.vector.tensor_copy(woven.rearrange("p (s h) -> p s h", h=2).bitcast(I32), low_high[:, s0:s1, :].bitcast(I32))
+            else:
+                nc.scalar.copy(woven.rearrange("p (s h) -> p s h", h=2), low_high[:, s0:s1, :])
 
         def codes(a, s0, s1):
             if a == 1:
@@ -151,143 +160,133 @@ def tile_moe_two_lin_relu2_kernel(tc, xT, w_words, w_scales, b, gate, offs, dst,
                 return codes0_early[:, s0:s1]
             return codes0_late[:, s0 - S_HALF : s1 - S_HALF]
 
-        def by_slot(woven):
-            return woven.rearrange("p (s h) -> p s h", h=2)
-
-        def round_pair(h):
-            rounded = token_pairs[h][:].bitcast(BF16).rearrange("p (t e) -> p t e", e=2)
-            for t0, share in zip((0, T_HALF), SCALAR_TOKENS[h]):
-                nc.scalar.copy(rounded[:, t0 : t0 + share, :], x_pairs[h][:, t0 : t0 + share, :])
-                nc.vector.tensor_copy(rounded[:, t0 + share : t0 + T_HALF, :], x_pairs[h][:, t0 + share : t0 + T_HALF, :])
-
-        def round_on_gpsimd(d, t0):
-            nc.gpsimd.tensor_scalar(token_rows[d][:, t0:T], x_rows[d][:, t0:T], 1.0, 0.0, MULT, ADD)
-
-        def gathered(window, s0, s1):
-            return window[:, :].indirect(offs_sb[:, s0 // LIST : s1 // LIST])
-
         def quantise(a, s0, s1, woven):
             nc.vector.quantize_mx(
                 out=codes(a, s0, s1).bitcast(E4M3X4), scales=scales[a][:, s0:s1], in_=woven.bitcast(BF16)
             )
 
-        def late_pairs(h, s0, s1):
-            return pairs1[:, h * LATE + s0 - G : h * LATE + s1 - G]
-
-        def late_woven(s0, s1):
-            return woven1[:, 2 * (s0 - G) : 2 * (s1 - G)]
-
-        def gather_row(d, s0, s1):
-            pairs = late_pairs(d // 2, s0, s1).bitcast(BF16).rearrange("p (s e) -> p s e", e=2)
-            nc.scalar.activation(pairs[:, :, d % 2], gathered(token_rows[d], s0, s1), ACT.Copy)
-
-        def weave_late(s0, s1):
-            low_high = pairs1[:, 0 : 2 * LATE].rearrange("p (h s) -> p s h", h=2)
-            nc.scalar.copy(by_slot(late_woven(s0, s1)), low_high[:, s0 - G : s1 - G, :])
-
         round_pair(0)
-        nc.vector.tensor_copy(pairs0[:, 0, :], gathered(token_pairs[0], 0, S))
-        out_sb[2] = keep.tile([P, T], F32, name="x_pair0", align_bytes=64)
-        nc.scalar.activation(out_sb[2][:], out_sb[0][:], ACT.Square)
+        gather(0, 0, S)
+        out_sb[2] = keep.tile([P, T + BIASES], F32, name="x_pair0", align_bytes=64)
+        nc.scalar.activation(out_sb[2][:, 0:T], out_sb[0][:, 0:T], ACT.Square)
+
         round_pair(1)
-        for s0 in range(0, S, G):
-            nc.vector.tensor_copy(pairs0[:, 1, s0 : s0 + G], gathered(token_pairs[1], s0, s0 + G))
-        nc.scalar.copy(token_rows[0][:, 0:T_HALF], x_rows[0][:, 0:T_HALF])
-        round_on_gpsimd(0, T_HALF)
-        round_on_gpsimd(1, 0)
-        for s0 in range(0, S, G):
-            woven = woven0_early if s0 < S_HALF else woven0_late[:]
-            at = s0 % S_HALF
-            nc.scalar.copy(by_slot(woven)[:, at : at + G, :], pairs0[:].rearrange("p h s -> p s h")[:, s0 : s0 + G, :])
+        gather(1, 0, S)
+        round_pair(2)
+        gather(2, 0, S)
+        woven0_early = keep.tile([P, S], U32, name="x_pair2", align_bytes=64)
+        weave(0, 0, S_HALF, woven0_early[:])
+        round_pair(3)
+        woven0_late = placed.tile([P, S], U32, name="woven0_late", align_bytes=64, offset=4 * S_HALF)
+        codes0_early = placed.tile([P, S_HALF], U32, name="codes0_early", align_bytes=64, offset=4 * S_HALF + 4 * S)
+        weave(0, S_HALF, S, woven0_late[:])
 
-        gather_row(0, ROW_CUTS[0], ROW_CUTS[1])
-        nc.scalar.copy(token_rows[2][:, 0:ROW2_SCALAR], x_rows[2][:, 0:ROW2_SCALAR])
-        first_values = first_woven[:].bitcast(BF16).rearrange("p (s d) -> p s d", d=PACK)
-        for d in range(PACK):
-            if d == 2:
-                quantise(0, 0, S_HALF, woven0_early)
-                round_on_gpsimd(2, ROW2_SCALAR)
-            nc.vector.tensor_copy(first_values[:, :, d], gathered(x_rows[d], 0, G))
-        for s0 in (0, C):
-            quantise(1, s0, s0 + C, first_woven[:, 2 * s0 : 2 * (s0 + C)])
-        nc.vector.tensor_copy(token_rows[3][:, 0 : T - HELD], x_rows[3][:, 0 : T - HELD])
+        for t in range(N_TILES):
+            nc.gpsimd.tensor_copy(out_sb[t][:, T : T + BIASES], b_sb[:].rearrange("p t e -> p (t e)"))
+
+        def woven_of(s0, s1):
+            if s0 == 0:
+                return pairs1[:, S + S_HALF : S + S_HALF + G]
+            if s0 == C:
+                return second_woven[:]
+            return woven1[:, 2 * s0 : 2 * s1]
+
+        gather(3, 0, G)
+        quantise(0, 0, S_HALF, woven0_early[:])
+        gather(3, G, 2 * G)
+        for s0, s1 in ((0, C), (C, G)):
+            weave(1, s0, s1, woven_of(s0, s1))
+            quantise(1, s0, s1, woven_of(s0, s1))
+        weave(1, G, 2 * G, woven_of(G, 2 * G))
+        gather(3, S_HALF, S)
+        quantise(1, G, 2 * G, woven_of(G, 2 * G))
+        weave(1, S_HALF, S, woven_of(S_HALF, S), True)
         quantise(0, S_HALF, S, woven0_late[:])
+        quantise(1, S_HALF, S, woven_of(S_HALF, S))
 
-        y_sb = [keep.tile([P, S], F32, name=f"y_sb{t}") for t in range(N_TILES)]
-
-        def product(acc, t, e, a):
-            words = w_first[t] if e < 2 else w_sb[e // 2][:, :, 2 * t * P : 2 * (t + 1) * P]
+        def product(acc, t, e, a, start, stop):
             nc.tensor.matmul_mx(
                 out=acc,
-                lhsT=words[:, PASSES * (e % 2) + a, :].bitcast(E2M1X4),
+                lhsT=w_sb[e, t][:, a, :].bitcast(E2M1X4),
                 lhsT_scale=w_scale_sb[:, PASSES * e + a, t * P : (t + 1) * P],
                 rhs=codes(a, e * C, (e + 1) * C).bitcast(E4M3X4),
                 rhs_scale=scales[a][:, e * C : (e + 1) * C],
-                start=(a == 0),
-                stop=(a == PASSES - 1),
+                start=start,
+                stop=stop,
             )
 
-        def relu_of(relu, acc, t, e):
-            nc.scalar.activation(relu, acc, ACT.Relu, bias=b_sb[:, t, e : e + 1])
-
-        def experts(t, g, relu_bytes=None, y_bytes=None):
-            acc = psum.tile([P, G], F32, name="acc")
-            if relu_bytes is None:
-                relu_tile = work.tile([P, G], F32, name="relu_tile")
-                relu = relu_tile[:]
-            else:
-                relu = relu_bytes.bitcast(F32)
-            for i in range(2):
+        def products(t, s0, s1):
+            acc = psum.tile([P, s1 - s0], F32, name="acc")
+            for e in range(s0 // C, s1 // C):
                 for a in range(PASSES):
-                    product(acc[:, i * C : (i + 1) * C], t, 2 * g + i, a)
-            for i in range(2):
-                relu_of(relu[:, i * C : (i + 1) * C], acc[:, i * C : (i + 1) * C], t, 2 * g + i)
-            y = y_sb[t][:, g * G : (g + 1) * G] if y_bytes is None else y_bytes.bitcast(F32)
-            nc.scalar.activation(y, relu, ACT.Square)
-            return y
+                    product(acc[:, e * C - s0 : (e + 1) * C - s0], t, e, a, a == 0, a == PASSES - 1)
+            return acc
 
-        def scatter(t, s0, s1, y):
-            window = out_sb[t][:].indirect(dst_sb[:, s0 // LIST : s1 // LIST])
-            nc.vector.tensor_tensor(window, y, gate_sb[:, s0:s1], MULT)
-
-        first_relu = keep.tile([P, G], F32, name="first_relu")
-        for d in (1, 2):
-            gather_row(d, ROW_CUTS[0], ROW_CUTS[1])
-        accs = [psum.tile([P, C], F32, name="acc") for e in range(2)]
+        first = [psum.tile([P, G], F32, name="acc") for t in range(N_TILES)]
         for a in range(PASSES):
-            for e in range(2):
-                product(accs[e][:], 0, e, a)
-        relus = (first_relu[:, 0:C], row3[:, T - HELD : T - HELD + 2 * C].bitcast(F32))
-        for e in range(2):
-            relu_of(relus[e], accs[e][:], 0, e)
-        for e in range(2):
-            nc.scalar.activation(y_sb[0][:, e * C : (e + 1) * C], relus[e], ACT.Square)
-        scatter(0, 0, G, y_sb[0][:, 0:G])
+            for t in range(N_TILES):
+                for e in range(2):
+                    product(first[t][:, e * C : (e + 1) * C], t, e, a, a == 0 and e == 0, a == 1 and e == 1)
 
-        for g in range(GROUPS - 1):
-            s0, s1, s2 = g * G, (g + 1) * G, (g + 2) * G
-            if g == 0:
-                scatter(1, s0, s1, experts(1, g, first_relu[:]))
-                nc.scalar.copy(token_rows[3][:, T - HELD : T], x_rows[3][:, T - HELD : T])
-            else:
-                c0, c1 = ROW_CUTS[g], ROW_CUTS[g + 1]
-                for d in (0, 1):
-                    gather_row(d, c0, c1)
-                scatter(0, s0, s1, experts(0, g, late_pairs(1, c0, c0 + G)))
-                gather_row(2, c0, c1)
-                scatter(1, s0, s1, experts(1, g))
-            gather_row(3, s1, s2)
-            weave_late(s1, s2)
-            quantise(1, s1, s2, late_woven(s1, s2))
-            scatter(2, s0, s1, experts(2, g, None, late_pairs(0, s1, s2)))
-            if s2 < S:
-                scatter(3, s0, s1, experts(3, g, late_pairs(0, ROW_CUTS[g + 1], ROW_CUTS[g + 1] + G)))
-            else:
-                experts(3, g)
-                scatter(3, s0, LAST_CUT, y_sb[3][:, s0:LAST_CUT])
+        def bias(home, t, e, last):
+            if last:
+                return b_sb[:, t, e : e + 1]
+            return out_sb[home][:, T + t * E + e : T + t * E + e + 1]
 
+        def by_scalar(t, s0, s1, home):
+            acc = first[t] if s0 == 0 else products(t, s0, s1)
+            for e in range(s0 // C, s1 // C):
+                z = acc[:, e * C - s0 : (e + 1) * C - s0]
+                at = bias(home, t, e, e == s1 // C - 1)
+                nc.scalar.activation(relu_sb[t][:, e * C : (e + 1) * C], z, ACT.Relu, bias=at)
+            nc.scalar.activation(half_sb[t][:, s0:s1], relu_sb[t][:, s0:s1], ACT.Square)
+
+        def by_vector(t, s0, s1, home):
+            acc = first[t] if s0 == 0 else products(t, s0, s1)
+            for e in range(s0 // C, s1 // C):
+                z = acc[:, e * C - s0 : (e + 1) * C - s0]
+                cols = slice(e * C, (e + 1) * C)
+                at = bias(home, t, e, False)
+                nc.vector.tensor_scalar(relu_sb[t][:, cols], z, at, 0.0, ADD, MAX)
+                nc.vector.scalar_tensor_tensor(half_sb[t][:, cols], z, at, gate_sb[:, cols], ADD, MULT)
+            nc.vector.tensor_tensor(y_sb[t][:, s0:s1], relu_sb[t][:, s0:s1], half_sb[t][:, s0:s1], MULT)
+
+        def scatter(t, c0, c1):
+            window = out_sb[t][:].indirect(dst_sb[:, c0 // LIST : c1 // LIST])
+            if t in SCALAR_TILES:
+                nc.scalar.activation(window, y_sb[t][:, c0:c1], ACT.Copy)
+            else:
+                nc.vector.tensor_tensor(window, half_sb[t][:, c0:c1], gate_sb[:, c0:c1], MULT)
+
+        def store(t):
+            nc.sync.dma_start(out=out[t * P : (t + 1) * P, :], in_=out_sb[t][:, 0:T])
+
+        by_scalar(0, 0, G, 0)
+        nc.vector.tensor_tensor(y_sb[0][:, 0:G], half_sb[0][:, 0:G], gate_sb[:, 0:G], MULT)
+        by_scalar(1, 0, G, 0)
+        by_scalar(2, 0, G, 0)
+        nc.vector.tensor_tensor(y_sb[2][:, 0:G], half_sb[2][:, 0:G], gate_sb[:, 0:G], MULT)
+        by_scalar(3, 0, G, 0)
+        for t in (0, 1):
+            scatter(t, 0, G)
+        by_vector(0, G, 2 * G, 3)
+        by_scalar(1, G, 2 * G, 2)
+        for t in (2, 3):
+            scatter(t, 0, G)
+        by_vector(2, G, 2 * G, 1)
+        by_scalar(3, G, 2 * G, 0)
+        for t in (0, 1):
+            scatter(t, G, 2 * G)
+        by_vector(0, S_HALF, S, 3)
+        by_scalar(1, S_HALF, S, 2)
+        for t in (2, 3):
+            scatter(t, G, 2 * G)
+        by_vector(2, S_HALF, S, 1)
+        by_scalar(3, S_HALF, S, 0)
         for t in range(N_TILES):
-            experts(t, GROUPS - 1)
-            s0 = LAST_CUT if t == N_TILES - 1 else S - G
-            scatter(t, s0, S, y_sb[t][:, s0:S])
-            nc.sync.dma_start(out=out[t * P : (t + 1) * P, :], in_=out_sb[t][:])
+            if t in SCALAR_TILES:
+                for c0 in (2 * G, 3 * G):
+                    scatter(t, c0, c0 + G)
+            else:
+                scatter(t, S_HALF, S)
+            store(t)

@@ -32,7 +32,7 @@ LATE = S - G
 S_HALF = S // 2
 T_HALF = T // 2
 PAIRS = 2 * PASSES
-BIASES = N_TILES * E
+BIASES = E
 
 PIECES = ((T_HALF,), (512, 1024), (512, 1024), (512, 1024))
 SCALAR_TOKENS = (((0, 256), (768, 1024)), ((384, 512), (512, 896)), ((384, 512), (512, 960)), ((320, 512), (512, 960)))
@@ -124,8 +124,18 @@ def tile_moe_two_lin_relu2_kernel(tc, xT, w_words, w_scales, b, gate, offs, dst,
         codes1 = keep.tile([P, S], U32, name="codes1", align_bytes=64)
         scales = [keep.tile([P, S], U8, name=f"scales{a}", align_bytes=64) for a in range(PASSES)]
         relu_sb = [keep.tile([P, S], F32, name=f"relu_sb{t}") for t in range(N_TILES)]
-        half_sb = [keep.tile([P, S], F32, name=f"half_sb{t}") for t in range(N_TILES)]
-        y_sb = [keep.tile([P, S], F32, name=f"y_sb{t}") for t in range(N_TILES)]
+        late_y = keep.tile([P, LATE], F32, name="late_y")
+        factor = {
+            (t, s0): keep.tile([P, S_HALF], F32, name=f"factor{t}_{s0}")[:]
+            for t in range(N_TILES)
+            for s0, s1 in STAGES
+        }
+        factor[1, G] = late_y[:, 0:G]
+        factor[0, S_HALF] = late_y[:, G:LATE]
+        first_y = keep.tile([P, 2 * G], F32, name="first_y")
+        y_at = {(0, 0): first_y[:, 0:G], (1, 0): first_y[:, G : 2 * G], (2, 0): factor[0, 0], (3, 0): factor[1, 0]}
+        y_at.update({(1, G): factor[2, 0], (0, G): factor[3, 0], (3, G): factor[1, G], (2, G): factor[0, G]})
+        y_at.update({(1, S_HALF): factor[3, G], (0, S_HALF): relu_sb[1][:, S_HALF:S], (3, S_HALF): factor[0, S_HALF]})
         woven1 = keep.tile([P, 2 * S], U32, name="woven1", align_bytes=64)
         second_woven = placed.tile([P, G], U32, name="second_woven", align_bytes=64, offset=0)
         codes0_late = placed.tile([P, S_HALF], U32, name="codes0_late", align_bytes=64, offset=0)
@@ -182,7 +192,7 @@ def tile_moe_two_lin_relu2_kernel(tc, xT, w_words, w_scales, b, gate, offs, dst,
         weave(0, S_HALF, S, woven0_late[:])
 
         for t in range(N_TILES):
-            nc.gpsimd.tensor_copy(out_sb[t][:, T : T + BIASES], b_sb[:].rearrange("p t e -> p (t e)"))
+            nc.gpsimd.tensor_copy(out_sb[t][:, T : T + BIASES], b_sb[:, t, :])
 
         def woven_of(s0, s1):
             if s0 == 0:
@@ -228,65 +238,75 @@ def tile_moe_two_lin_relu2_kernel(tc, xT, w_words, w_scales, b, gate, offs, dst,
                 for e in range(2):
                     product(first[t][:, e * C : (e + 1) * C], t, e, a, a == 0 and e == 0, a == 1 and e == 1)
 
-        def bias(home, t, e, last):
-            if last:
-                return b_sb[:, t, e : e + 1]
-            return out_sb[home][:, T + t * E + e : T + t * E + e + 1]
-
-        def by_scalar(t, s0, s1, home):
-            acc = first[t] if s0 == 0 else products(t, s0, s1)
-            for e in range(s0 // C, s1 // C):
-                z = acc[:, e * C - s0 : (e + 1) * C - s0]
-                at = bias(home, t, e, e == s1 // C - 1)
-                nc.scalar.activation(relu_sb[t][:, e * C : (e + 1) * C], z, ACT.Relu, bias=at)
-            nc.scalar.activation(half_sb[t][:, s0:s1], relu_sb[t][:, s0:s1], ACT.Square)
-
-        def by_vector(t, s0, s1, home):
+        def read_out(t, s0, s1, on_vector, held=False):
             acc = first[t] if s0 == 0 else products(t, s0, s1)
             for e in range(s0 // C, s1 // C):
                 z = acc[:, e * C - s0 : (e + 1) * C - s0]
                 cols = slice(e * C, (e + 1) * C)
-                at = bias(home, t, e, False)
-                nc.vector.tensor_scalar(relu_sb[t][:, cols], z, at, 0.0, ADD, MAX)
-                nc.vector.scalar_tensor_tensor(half_sb[t][:, cols], z, at, gate_sb[:, cols], ADD, MULT)
-            nc.vector.tensor_tensor(y_sb[t][:, s0:s1], relu_sb[t][:, s0:s1], half_sb[t][:, s0:s1], MULT)
+                free = e == s1 // C - 1 and not held
+                bias = b_sb[:, t, e : e + 1] if free else out_sb[t][:, T + e : T + e + 1]
+                if on_vector:
+                    gated = factor[t, s0][:, e * C - s0 : (e + 1) * C - s0]
+                    nc.vector.tensor_scalar(relu_sb[t][:, cols], z, bias, 0.0, ADD, MAX)
+                    nc.vector.scalar_tensor_tensor(gated, z, bias, gate_sb[:, cols], ADD, MULT)
+                else:
+                    nc.scalar.activation(relu_sb[t][:, cols], z, ACT.Relu, bias=bias)
 
-        def scatter(t, c0, c1):
+        def square(t, s0, s1):
+            nc.scalar.activation(factor[t, s0][:, 0 : s1 - s0], relu_sb[t][:, s0:s1], ACT.Square)
+
+        def finish(t, s0, s1, on_vector):
+            other = relu_sb[t][:, s0:s1] if on_vector else gate_sb[:, s0:s1]
+            nc.gpsimd.tensor_tensor(y_at[t, s0][:, 0 : s1 - s0], factor[t, s0][:, 0 : s1 - s0], other, MULT)
+
+        def unit(t, s0, s1, on_vector):
+            read_out(t, s0, s1, on_vector)
+            if not on_vector:
+                square(t, s0, s1)
+            finish(t, s0, s1, on_vector)
+
+        def scatter(t, c0, c1, y):
             window = out_sb[t][:].indirect(dst_sb[:, c0 // LIST : c1 // LIST])
             if t in SCALAR_TILES:
-                nc.scalar.activation(window, y_sb[t][:, c0:c1], ACT.Copy)
+                nc.scalar.activation(window, y, ACT.Copy)
             else:
-                nc.vector.tensor_tensor(window, half_sb[t][:, c0:c1], gate_sb[:, c0:c1], MULT)
+                nc.vector.tensor_copy(window, y)
 
         def store(t):
-            nc.sync.dma_start(out=out[t * P : (t + 1) * P, :], in_=out_sb[t][:, 0:T])
+            queue = nc.scalar if t == 2 else nc.sync
+            queue.dma_start(out=out[t * P : (t + 1) * P, :], in_=out_sb[t][:, 0:T])
 
-        by_scalar(0, 0, G, 0)
-        nc.vector.tensor_tensor(y_sb[0][:, 0:G], half_sb[0][:, 0:G], gate_sb[:, 0:G], MULT)
-        by_scalar(1, 0, G, 0)
-        by_scalar(2, 0, G, 0)
-        nc.vector.tensor_tensor(y_sb[2][:, 0:G], half_sb[2][:, 0:G], gate_sb[:, 0:G], MULT)
-        by_scalar(3, 0, G, 0)
-        for t in (0, 1):
-            scatter(t, 0, G)
-        by_vector(0, G, 2 * G, 3)
-        by_scalar(1, G, 2 * G, 2)
-        for t in (2, 3):
-            scatter(t, 0, G)
-        by_vector(2, G, 2 * G, 1)
-        by_scalar(3, G, 2 * G, 0)
-        for t in (0, 1):
-            scatter(t, G, 2 * G)
-        by_vector(0, S_HALF, S, 3)
-        by_scalar(1, S_HALF, S, 2)
-        for t in (2, 3):
-            scatter(t, G, 2 * G)
-        by_vector(2, S_HALF, S, 1)
-        by_scalar(3, S_HALF, S, 0)
         for t in range(N_TILES):
-            if t in SCALAR_TILES:
-                for c0 in (2 * G, 3 * G):
-                    scatter(t, c0, c0 + G)
-            else:
-                scatter(t, S_HALF, S)
-            store(t)
+            unit(t, 0, G, False)
+        for t in (1, 0, 3):
+            unit(t, G, S_HALF, t == 3)
+            scatter(t, 0, G, y_at[t, 0][:, 0:G])
+        read_out(2, G, S_HALF, False)
+        scatter(2, 0, G, y_at[2, 0][:, 0:G])
+        read_out(0, S_HALF, S, False, True)
+        square(2, G, S_HALF)
+        finish(2, G, S_HALF, False)
+        unit(1, S_HALF, S, True)
+        square(0, S_HALF, S)
+        finish(0, S_HALF, S, False)
+        for t in (1, 0):
+            scatter(t, G, S_HALF, y_at[t, G][:, 0:G])
+        unit(3, S_HALF, S, True)
+        read_out(2, S_HALF, S, False)
+        square(2, S_HALF, S)
+        scatter(2, G, S_HALF, y_at[2, G][:, 0:G])
+        scatter(1, S_HALF, S, y_at[1, S_HALF])
+        store(1)
+        y0 = y_at[0, S_HALF]
+        scatter(0, 2 * G, 3 * G, y0[:, 0:G])
+        y2 = (y0[:, 0:G], factor[1, S_HALF][:, 0:G])
+        for i in range(2):
+            s0 = S_HALF + i * G
+            nc.gpsimd.tensor_tensor(y2[i], factor[2, S_HALF][:, i * G : (i + 1) * G], gate_sb[:, s0 : s0 + G], MULT)
+        scatter(0, 3 * G, S, y0[:, G:S_HALF])
+        store(0)
+        scatter(3, G, S, late_y[:])
+        store(3)
+        for i in range(2):
+            scatter(2, S_HALF + i * G, S_HALF + (i + 1) * G, y2[i])
+        store(2)

@@ -273,8 +273,7 @@ def tile_moe_two_lin_relu2_kernel(tc, xT, w_words, w_scales, b, gate, offs, dst,
                 nc.vector.tensor_copy(window, y)
 
         def store(t):
-            queue = nc.scalar if t == 2 else nc.sync
-            queue.dma_start(out=out[t * P : (t + 1) * P, :], in_=out_sb[t][:, 0:T])
+            nc.sync.dma_start(out=out[t * P : (t + 1) * P, :], in_=out_sb[t][:, 0:T])
 
         for t in range(N_TILES):
             unit(t, 0, G, False)

@@ -109,15 +109,17 @@ def tile_moe_two_lin_relu2_kernel(tc, xT, w_words, w_scales, b, gate, offs, dst,
             nc.sync.dma_start(gate_of(s0, s1), gate[0:P, s0:s1])
 
         w_sb = {}
-        load_weight_scales(0, 4, 0, N_TILES)
+        load_weight_scales(0, 2, 0, N_TILES)
         w_sb.update(load_weights(0, 2, 0, 2))
         load_bias(0, N_TILES)
-        load_gate(0, G)
         w_sb.update(load_weights(0, 2, 2, N_TILES))
+        load_gate(0, S_HALF)
+        load_weight_scales(2, 4, 0, N_TILES)
         w_sb.update(load_weights(2, 4, 0, N_TILES))
-        load_gate(G, S)
         load_weight_scales(4, E, 0, N_TILES)
-        w_sb.update(load_weights(4, E, 0, N_TILES))
+        w_sb.update(load_weights(4, E, 0, 2))
+        load_gate(S_HALF, S)
+        w_sb.update(load_weights(4, E, 2, N_TILES))
 
         token_pairs = [keep.tile([P, T], U32, name=f"token_pairs{h}") for h in range(PAIRS)]
         pairs0 = keep.tile([P, 2 * S], U32, name="pairs0")
@@ -233,10 +235,12 @@ def tile_moe_two_lin_relu2_kernel(tc, xT, w_words, w_scales, b, gate, offs, dst,
             return acc
 
         first = [psum.tile([P, G], F32, name="acc") for t in range(N_TILES)]
-        for a in range(PASSES):
-            for t in range(N_TILES):
-                for e in range(2):
-                    product(first[t][:, e * C : (e + 1) * C], t, e, a, a == 0 and e == 0, a == 1 and e == 1)
+        for tiles, order in (((0, 1), (0, 1)), ((2, 3), (1, 0))):
+            for a in order:
+                for t in tiles:
+                    for e in range(2):
+                        start, stop = (a, e) == (order[0], 0), (a, e) == (order[1], 1)
+                        product(first[t][:, e * C : (e + 1) * C], t, e, a, start, stop)
 
         def read_out(t, s0, s1, on_vector, held=False):
             acc = first[t] if s0 == 0 else products(t, s0, s1)

@@ -257,7 +257,10 @@ def tile_moe_two_lin_relu2_kernel(tc, xT, w_words, w_scales, b, gate, offs, dst,
                     nc.scalar.activation(relu_sb[t][:, cols], z, ACT.Relu, bias=bias)
 
         def square(t, s0, s1):
-            nc.scalar.activation(factor[t, s0][:, 0 : s1 - s0], relu_sb[t][:, s0:s1], ACT.Square)
+            if s0 == G and t in SCALAR_TILES:
+                nc.gpsimd.tensor_tensor(factor[t, s0][:, 0:G], relu_sb[t][:, s0:s1], relu_sb[t][:, s0:s1], MULT)
+            else:
+                nc.scalar.activation(factor[t, s0][:, 0 : s1 - s0], relu_sb[t][:, s0:s1], ACT.Square)
 
         def finish(t, s0, s1, on_vector):
             other = relu_sb[t][:, s0:s1] if on_vector else gate_sb[:, s0:s1]

@@ -34,10 +34,10 @@ T_HALF = T // 2
 PAIRS = 2 * PASSES
 BIASES = E
 
-PIECES = ((T_HALF,), (512, 1024), (512, 1024), (512, 1024))
-SCALAR_TOKENS = (((0, 256), (768, 1024)), ((384, 512), (512, 896)), ((384, 512), (512, 960)), ((320, 512), (512, 960)))
-VECTOR_TOKENS = (((256, 768), (1024, T)), ((896, T),), ((960, T),), ((960, T),))
-GPSIMD_TOKENS = (0, 384, 384, 320)
+PIECES = PAIRS * ((T_HALF,),)
+SCALAR_TOKENS = (((0, 256), (768, 1024)),) + 3 * (((384, 768), (768, 992)),)
+VECTOR_TOKENS = (((256, 768), (1024, T)),) + 3 * (((992, T),),)
+GPSIMD_TOKENS = (0, 384, 384, 384)
 STAGES = ((0, G), (G, 2 * G), (2 * G, S))
 SCALAR_TILES = (0, 2)
 VECTOR_TILES = (1, 3)
@@ -77,7 +77,6 @@ def tile_moe_two_lin_relu2_kernel(tc, xT, w_words, w_scales, b, gate, offs, dst,
 
         x_pairs = [load_pair(0)]
         nc.sync.dma_start(offs_sb[:], offs)
-        nc.sync.dma_start(dst_sb[:], dst)
         x_pairs = x_pairs + [load_pair(h) for h in range(1, PAIRS)]
 
         nc.gpsimd.memset(w_scale_sb[:].rearrange("p g n -> p (g n)").bitcast(I32), 0)
@@ -114,6 +113,7 @@ def tile_moe_two_lin_relu2_kernel(tc, xT, w_words, w_scales, b, gate, offs, dst,
         load_bias(0, N_TILES)
         w_sb.update(load_weights(0, 2, 2, N_TILES))
         load_gate(0, S_HALF)
+        nc.sync.dma_start(dst_sb[:], dst)
         load_weight_scales(2, 4, 0, N_TILES)
         w_sb.update(load_weights(2, 4, 0, N_TILES))
         load_weight_scales(4, E, 0, N_TILES)

@@ -32,7 +32,7 @@ LATE = S - G
 S_HALF = S // 2
 T_HALF = T // 2
 PAIRS = 2 * PASSES
-BIASES = E
+BIASES = N_TILES * E
 
 PIECES = PAIRS * ((T_HALF,),)
 SCALAR_TOKENS = (((0, 256), (768, 1024)),) + 3 * (((384, 768), (768, 992)),)
@@ -194,7 +194,7 @@ def tile_moe_two_lin_relu2_kernel(tc, xT, w_words, w_scales, b, gate, offs, dst,
         weave(0, S_HALF, S, woven0_late[:])
 
         for t in range(N_TILES):
-            nc.gpsimd.tensor_copy(out_sb[t][:, T : T + BIASES], b_sb[:, t, :])
+            nc.gpsimd.tensor_copy(out_sb[t][:, T : T + BIASES], b_sb[:].rearrange("p t e -> p (t e)"))
 
         def woven_of(s0, s1):
             if s0 == 0:
@@ -242,19 +242,26 @@ def tile_moe_two_lin_relu2_kernel(tc, xT, w_words, w_scales, b, gate, offs, dst,
                         start, stop = (a, e) == (order[0], 0), (a, e) == (order[1], 1)
                         product(first[t][:, e * C : (e + 1) * C], t, e, a, start, stop)
 
-        def read_out(t, s0, s1, on_vector, held=False):
-            acc = first[t] if s0 == 0 else products(t, s0, s1)
+        banks = {(t, 0): first[t] for t in range(N_TILES)}
+
+        def read_out(t, s0, s1, on_vector, last_home=None, acc=None):
+            relu_done = acc is not None
+            if acc is None:
+                acc = banks[t, s0] if (t, s0) in banks else products(t, s0, s1)
             for e in range(s0 // C, s1 // C):
                 z = acc[:, e * C - s0 : (e + 1) * C - s0]
                 cols = slice(e * C, (e + 1) * C)
-                free = e == s1 // C - 1 and not held
-                bias = b_sb[:, t, e : e + 1] if free else out_sb[t][:, T + e : T + e + 1]
+                home = last_home if e == s1 // C - 1 else t
+                at = T + t * E + e
+                bias = b_sb[:, t, e : e + 1] if home is None else out_sb[home][:, at : at + 1]
                 if on_vector:
                     gated = factor[t, s0][:, e * C - s0 : (e + 1) * C - s0]
-                    nc.vector.tensor_scalar(relu_sb[t][:, cols], z, bias, 0.0, ADD, MAX)
+                    if not relu_done:
+                        nc.vector.tensor_scalar(relu_sb[t][:, cols], z, bias, 0.0, ADD, MAX)
                     nc.vector.scalar_tensor_tensor(gated, z, bias, gate_sb[:, cols], ADD, MULT)
                 else:
                     nc.scalar.activation(relu_sb[t][:, cols], z, ACT.Relu, bias=bias)
+            return acc
 
         def square(t, s0, s1):
             if s0 == G and t in SCALAR_TILES:
@@ -284,12 +291,18 @@ def tile_moe_two_lin_relu2_kernel(tc, xT, w_words, w_scales, b, gate, offs, dst,
 
         for t in range(N_TILES):
             unit(t, 0, G, False)
-        for t in (1, 0, 3):
-            unit(t, G, S_HALF, t == 3)
-            scatter(t, 0, G, y_at[t, 0][:, 0:G])
+        unit(1, G, S_HALF, False)
+        scatter(1, 0, G, y_at[1, 0][:, 0:G])
+        shared = read_out(3, G, S_HALF, False)
+        unit(0, G, S_HALF, False)
+        scatter(0, 0, G, y_at[0, 0][:, 0:G])
+        read_out(3, G, S_HALF, True, None, shared)
+        finish(3, G, S_HALF, True)
+        scatter(3, 0, G, y_at[3, 0][:, 0:G])
         read_out(2, G, S_HALF, False)
         scatter(2, 0, G, y_at[2, 0][:, 0:G])
-        read_out(0, S_HALF, S, False, True)
+        banks[1, S_HALF] = products(1, S_HALF, S)
+        read_out(0, S_HALF, S, False, 0)
         square(2, G, S_HALF)
         finish(2, G, S_HALF, False)
         unit(1, S_HALF, S, True)
@@ -298,7 +311,7 @@ def tile_moe_two_lin_relu2_kernel(tc, xT, w_words, w_scales, b, gate, offs, dst,
         for t in (1, 0):
             scatter(t, G, S_HALF, y_at[t, G][:, 0:G])
         unit(3, S_HALF, S, True)
-        read_out(2, S_HALF, S, False)
+        read_out(2, S_HALF, S, False, 0)
         square(2, S_HALF, S)
         scatter(2, G, S_HALF, y_at[2, G][:, 0:G])
         scatter(1, S_HALF, S, y_at[1, S_HALF])

@@ -112,13 +112,15 @@ def tile_moe_two_lin_relu2_kernel(tc, xT, w_words, w_scales, b, gate, offs, dst,
         w_sb.update(load_weights(0, 2, 0, 2))
         load_bias(0, N_TILES)
         w_sb.update(load_weights(0, 2, 2, N_TILES))
-        load_gate(0, S_HALF)
+        load_gate(0, G)
         nc.sync.dma_start(dst_sb[:], dst)
         load_weight_scales(2, 4, 0, N_TILES)
         w_sb.update(load_weights(2, 4, 0, N_TILES))
-        load_weight_scales(4, E, 0, N_TILES)
+        load_gate(G, S_HALF)
+        load_weight_scales(4, E, 0, 2)
         w_sb.update(load_weights(4, E, 0, 2))
         load_gate(S_HALF, S)
+        load_weight_scales(4, E, 2, N_TILES)
         w_sb.update(load_weights(4, E, 2, N_TILES))
 
         token_pairs = [keep.tile([P, T], U32, name=f"token_pairs{h}") for h in range(PAIRS)]
@@ -244,7 +246,7 @@ def tile_moe_two_lin_relu2_kernel(tc, xT, w_words, w_scales, b, gate, offs, dst,
 
         banks = {(t, 0): first[t] for t in range(N_TILES)}
 
-        def read_out(t, s0, s1, on_vector, last_home=None, acc=None):
+        def read_out(t, s0, s1, on_vector, last_home=None, acc=None, later_home=None):
             relu_done = acc is not None
             if acc is None:
                 acc = banks[t, s0] if (t, s0) in banks else products(t, s0, s1)
@@ -252,6 +254,8 @@ def tile_moe_two_lin_relu2_kernel(tc, xT, w_words, w_scales, b, gate, offs, dst,
                 z = acc[:, e * C - s0 : (e + 1) * C - s0]
                 cols = slice(e * C, (e + 1) * C)
                 home = last_home if e == s1 // C - 1 else t
+                if later_home is not None and s0 // C < e < s1 // C - 1:
+                    home = later_home
                 at = T + t * E + e
                 bias = b_sb[:, t, e : e + 1] if home is None else out_sb[home][:, at : at + 1]
                 if on_vector:
@@ -310,7 +314,8 @@ def tile_moe_two_lin_relu2_kernel(tc, xT, w_words, w_scales, b, gate, offs, dst,
         finish(0, S_HALF, S, False)
         for t in (1, 0):
             scatter(t, G, S_HALF, y_at[t, G][:, 0:G])
-        unit(3, S_HALF, S, True)
+        read_out(3, S_HALF, S, True, None, None, 1)
+        finish(3, S_HALF, S, True)
         read_out(2, S_HALF, S, False, 0)
         square(2, S_HALF, S)
         scatter(2, G, S_HALF, y_at[2, G][:, 0:G])

@@ -28,65 +28,45 @@ ADD = mybir.AluOpType.add
 MAX = mybir.AluOpType.max
 
 G = 2 * C
-LATE = S - G
-S_HALF = S // 2
-T_HALF = T // 2
-PAIRS = 2 * PASSES
-BIASES = N_TILES * E
-
-PIECES = PAIRS * ((T_HALF,),)
-SCALAR_TOKENS = (((0, 256), (768, 1024)),) + 3 * (((384, 768), (768, 992)),)
-VECTOR_TOKENS = (((256, 768), (1024, T)),) + 3 * (((992, T),),)
-GPSIMD_TOKENS = (0, 384, 384, 384)
-STAGES = ((0, G), (G, 2 * G), (2 * G, S))
-SCALAR_TILES = (0, 2)
-VECTOR_TILES = (1, 3)
+H = S // 2
+DMA_ALIGN = 256
 
 
 def tile_moe_two_lin_relu2_kernel(tc, xT, w_words, w_scales, b, gate, offs, dst, out):
     nc = tc.nc
     with ExitStack() as ctx:
         keep = ctx.enter_context(tc.tile_pool(name="keep", bufs=1))
-        placed = ctx.enter_context(tc.tile_pool(name="placed", bufs=1))
         psum = ctx.enter_context(tc.psum_pool(name="psum", bufs=8))
 
         offs_sb = keep.tile([P, S // LIST], U16, name="offs_sb")
         dst_sb = keep.tile([P, S // LIST], U16, name="dst_sb")
         b_sb = keep.tile([P, N_TILES, E], F32, name="b_sb")
-        gate_sb = keep.tile([P, S], F32, name="gate_sb")
-        pairs1 = keep.tile([P, 2 * S], U32, name="pairs1", align_bytes=64)
+        gate_sb = keep.tile([P, S], F32, name="gate_sb", align_bytes=DMA_ALIGN)
+        w_scale_sb = keep.tile([P, E * PASSES, N], U8, name="w_scale_sb", align_bytes=DMA_ALIGN)
+        out_sb = [keep.tile([P, T + E + 1], F32, name=f"out_sb{t}", align_bytes=DMA_ALIGN) for t in range(N_TILES)]
 
-        def gate_of(s0, s1):
-            return gate_sb[:, s0:s1]
+        def load_row(a, d):
+            x = keep.tile([P, T], F32, name=f"x{a}_{d}", align_bytes=DMA_ALIGN)
+            rows = xT[a * K_PASS : (a + 1) * K_PASS, :].rearrange("(p d) t -> p d t", d=PACK)
+            nc.sync.dma_start(out=x[:], in_=rows[:, d, :])
+            return x
 
-        w_scale_sb = keep.tile([P, E * PASSES, N], U8, name="w_scale_sb", align_bytes=64)
-        out_sb = {t: keep.tile([P, T + BIASES], F32, name=f"out_sb{t}") for t in (0, 1, 3)}
-
-        def load_pair(h):
-            if h == PAIRS - 1:
-                x = placed.tile([P, 2 * T], F32, name=f"x_pair{h}", align_bytes=64, offset=4 * S_HALF)
-            else:
-                x = keep.tile([P, 2 * T], F32, name=f"x_pair{h}", align_bytes=64)
-            a = h // 2
-            rows = xT[a * K_PASS : (a + 1) * K_PASS, :].rearrange("(p d) t -> p (d t)", d=PACK)
-            run = rows[:, 2 * (h % 2) * T : 2 * (h % 2 + 1) * T]
-            cuts = (0,) + tuple(T + c for c in PIECES[h]) + (2 * T,)
-            for c0, c1 in zip(cuts, cuts[1:]):
-                nc.sync.dma_start(out=x[:, c0:c1], in_=run[:, c0:c1])
-            return x[:].rearrange("p (e t) -> p t e", e=2)
-
-        x_pairs = [load_pair(0)]
+        x_row = {(0, 0): load_row(0, 0)}
         nc.sync.dma_start(offs_sb[:], offs)
-        x_pairs = x_pairs + [load_pair(h) for h in range(1, PAIRS)]
+        for a in range(PASSES):
+            for d in range(PACK):
+                if (a, d) not in x_row:
+                    x_row.update({(a, d): load_row(a, d)})
 
-        nc.gpsimd.memset(w_scale_sb[:].rearrange("p g n -> p (g n)").bitcast(I32), 0)
-        for t in (0, 3):
-            nc.vector.memset(out_sb[t][:, 0:T].bitcast(I32), 0)
+        nc.gpsimd.memset(out_sb[0][:, 0:T], 0.0)
         nc.scalar.activation(out_sb[1][:, 0:T], out_sb[0][:, 0:T], ACT.Square)
+        nc.gpsimd.memset(w_scale_sb[:].rearrange("p g n -> p (g n)").bitcast(I32), 0)
+        for t in (2, 3):
+            nc.gpsimd.memset(out_sb[t][:, 0:T], 0.0)
 
         def load_weights(e0, e1, t0, t1):
             words = w_words[e0:e1, :, :, 2 * t0 * P : 2 * t1 * P].rearrange("e a p c -> p (e a) c")
-            w = keep.tile([P, (e1 - e0) * PASSES, 2 * (t1 - t0) * P], U8, name=f"w{e0}_{t0}", align_bytes=64)
+            w = keep.tile([P, (e1 - e0) * PASSES, 2 * (t1 - t0) * P], U8, name=f"w{e0}_{t0}", align_bytes=DMA_ALIGN)
             nc.sync.dma_start(out=w[:].bitcast(I32), in_=words.bitcast(I32))
             return {
                 (e, t): w[:, PASSES * (e - e0) : PASSES * (e - e0 + 1), 2 * (t - t0) * P : 2 * (t - t0 + 1) * P]
@@ -101,236 +81,225 @@ def tile_moe_two_lin_relu2_kernel(tc, xT, w_words, w_scales, b, gate, offs, dst,
                     in_=w_scales[e0:e1, :, r:16:4, t0 * P : t1 * P].rearrange("e a q n -> q (e a) n").bitcast(I32),
                 )
 
-        def load_bias(t0, t1):
-            nc.sync.dma_start(out=b_sb[:, t0:t1, :], in_=b.rearrange("(t p) e -> p t e", p=P)[:, t0:t1, :])
-
         def load_gate(s0, s1):
-            nc.sync.dma_start(gate_of(s0, s1), gate[0:P, s0:s1])
+            nc.sync.dma_start(gate_sb[:, s0:s1], gate[0:P, s0:s1])
 
         w_sb = {}
         load_weight_scales(0, 2, 0, N_TILES)
         w_sb.update(load_weights(0, 2, 0, 2))
-        load_bias(0, N_TILES)
+        nc.sync.dma_start(out=b_sb[:], in_=b.rearrange("(t p) e -> p t e", p=P))
         w_sb.update(load_weights(0, 2, 2, N_TILES))
         load_gate(0, G)
         nc.sync.dma_start(dst_sb[:], dst)
         load_weight_scales(2, 4, 0, N_TILES)
         w_sb.update(load_weights(2, 4, 0, N_TILES))
-        load_gate(G, S_HALF)
+        load_gate(G, H)
         load_weight_scales(4, E, 0, 2)
         w_sb.update(load_weights(4, E, 0, 2))
-        load_gate(S_HALF, S)
+        load_gate(H, S)
         load_weight_scales(4, E, 2, N_TILES)
         w_sb.update(load_weights(4, E, 2, N_TILES))
 
-        token_pairs = [keep.tile([P, T], U32, name=f"token_pairs{h}") for h in range(PAIRS)]
-        pairs0 = keep.tile([P, 2 * S], U32, name="pairs0")
-        codes1 = keep.tile([P, S], U32, name="codes1", align_bytes=64)
+        for t in (0, 1):
+            nc.gpsimd.tensor_copy(out_sb[t][:, T + 2 : T + E], b_sb[:, t, 2:E])
+        for t in (2, 3):
+            nc.gpsimd.tensor_copy(out_sb[t][:, T + 2 : T + E - 1], b_sb[:, t, 2 : E - 1])
+            nc.gpsimd.tensor_copy(out_sb[t - 2][:, T + E : T + E + 1], b_sb[:, t, E - 1 : E])
+
+        codes = [keep.tile([P, S], U32, name=f"codes{a}", align_bytes=64) for a in range(PASSES)]
         scales = [keep.tile([P, S], U8, name=f"scales{a}", align_bytes=64) for a in range(PASSES)]
-        relu_sb = [keep.tile([P, S], F32, name=f"relu_sb{t}") for t in range(N_TILES)]
-        late_y = keep.tile([P, LATE], F32, name="late_y")
-        factor = {
-            (t, s0): keep.tile([P, S_HALF], F32, name=f"factor{t}_{s0}")[:]
-            for t in range(N_TILES)
-            for s0, s1 in STAGES
-        }
-        factor[1, G] = late_y[:, 0:G]
-        factor[0, S_HALF] = late_y[:, G:LATE]
-        first_y = keep.tile([P, 2 * G], F32, name="first_y")
-        y_at = {(0, 0): first_y[:, 0:G], (1, 0): first_y[:, G : 2 * G], (2, 0): factor[0, 0], (3, 0): factor[1, 0]}
-        y_at.update({(1, G): factor[2, 0], (0, G): factor[3, 0], (3, G): factor[1, G], (2, G): factor[0, G]})
-        y_at.update({(1, S_HALF): factor[3, G], (0, S_HALF): relu_sb[1][:, S_HALF:S], (3, S_HALF): factor[0, S_HALF]})
-        woven1 = keep.tile([P, 2 * S], U32, name="woven1", align_bytes=64)
-        second_woven = placed.tile([P, G], U32, name="second_woven", align_bytes=64, offset=0)
-        codes0_late = placed.tile([P, S_HALF], U32, name="codes0_late", align_bytes=64, offset=0)
 
-        def round_pair(h):
-            rounded = token_pairs[h][:].bitcast(BF16).rearrange("p (t e) -> p t e", e=2)
-            for t0, t1 in SCALAR_TOKENS[h]:
-                nc.scalar.copy(rounded[:, t0:t1, :], x_pairs[h][:, t0:t1, :])
-            if GPSIMD_TOKENS[h] > 0:
-                t1 = GPSIMD_TOKENS[h]
-                nc.gpsimd.tensor_scalar(rounded[:, 0:t1, :], x_pairs[h][:, 0:t1, :], 1.0, 0.0, MULT, ADD)
-            for t0, t1 in VECTOR_TOKENS[h]:
-                nc.vector.tensor_copy(rounded[:, t0:t1, :], x_pairs[h][:, t0:t1, :])
-
-        def gather(h, s0, s1):
-            pairs = (pairs0, pairs1)[h // 2]
-            at = (h % 2) * S
-            window = token_pairs[h][:, :].indirect(offs_sb[:, s0 // LIST : s1 // LIST])
-            nc.vector.tensor_copy(pairs[:, at + s0 : at + s1], window)
-
-        def weave(a, s0, s1, woven, on_vector=False):
-            low_high = (pairs0, pairs1)[a][:, 0 : 2 * S].rearrange("p (h s) -> p s h", h=2)
+        def gather(on_vector, a, d, s0, s1, to):
+            window = x_row[a, d][:].indirect(offs_sb[:, s0 // LIST : s1 // LIST])
             if on_vector:
-                nc.vector.tensor_copy(woven.rearrange("p (s h) -> p s h", h=2).bitcast(I32), low_high[:, s0:s1, :].bitcast(I32))
+                nc.vector.tensor_copy(to, window)
             else:
-                nc.scalar.copy(woven.rearrange("p (s h) -> p s h", h=2), low_high[:, s0:s1, :])
+                nc.scalar.activation(to, window, ACT.Copy)
 
-        def codes(a, s0, s1):
-            if a == 1:
-                return codes1[:, s0:s1]
-            if s0 < S_HALF:
-                return codes0_early[:, s0:s1]
-            return codes0_late[:, s0 - S_HALF : s1 - S_HALF]
+        def pair_planes(a, s0, s1):
+            return keep.tile([P, 2, s1 - s0], U32, name=f"pairs{a}_{s0}", align_bytes=64), s0
 
-        def quantise(a, s0, s1, woven):
-            nc.vector.quantize_mx(
-                out=codes(a, s0, s1).bitcast(E4M3X4), scales=scales[a][:, s0:s1], in_=woven.bitcast(BF16)
-            )
+        def into_planes(planes, d, s0, s1):
+            tile, first = planes
+            halves = tile[:].rearrange("p h s -> p (h s)").bitcast(BF16).rearrange("p (h s e) -> p h s e", h=2, e=2)
+            return halves[:, d // 2, s0 - first : s1 - first, d % 2]
 
-        round_pair(0)
-        gather(0, 0, S)
-        out_sb[2] = keep.tile([P, T + BIASES], F32, name="x_pair0", align_bytes=64)
-        nc.scalar.activation(out_sb[2][:, 0:T], out_sb[0][:, 0:T], ACT.Square)
+        def woven_tile(a, s0, s1):
+            return keep.tile([P, 2 * (s1 - s0)], U32, name=f"woven{a}_{s0}", align_bytes=64), s0
 
-        round_pair(1)
-        gather(1, 0, S)
-        round_pair(2)
-        gather(2, 0, S)
-        woven0_early = keep.tile([P, S], U32, name="x_pair2", align_bytes=64)
-        weave(0, 0, S_HALF, woven0_early[:])
-        round_pair(3)
-        woven0_late = placed.tile([P, S], U32, name="woven0_late", align_bytes=64, offset=4 * S_HALF)
-        codes0_early = placed.tile([P, S_HALF], U32, name="codes0_early", align_bytes=64, offset=4 * S_HALF + 4 * S)
-        weave(0, S_HALF, S, woven0_late[:])
+        def weave(on_vector, planes, woven, s0, s1):
+            tile, first = planes
+            low_high = tile[:].rearrange("p h s -> p s h")[:, s0 - first : s1 - first, :]
+            to = woven[0][:, 2 * (s0 - woven[1]) : 2 * (s1 - woven[1])].rearrange("p (s h) -> p s h", h=2)
+            if on_vector:
+                nc.vector.tensor_copy(to.bitcast(I32), low_high.bitcast(I32))
+            else:
+                nc.scalar.copy(to, low_high)
 
-        for t in range(N_TILES):
-            nc.gpsimd.tensor_copy(out_sb[t][:, T : T + BIASES], b_sb[:].rearrange("p t e -> p (t e)"))
+        def quantise(a, woven, s0, s1):
+            values = woven[0][:, 2 * (s0 - woven[1]) : 2 * (s1 - woven[1])].bitcast(BF16)
+            nc.vector.quantize_mx(out=codes[a][:, s0:s1].bitcast(E4M3X4), scales=scales[a][:, s0:s1], in_=values)
 
-        def woven_of(s0, s1):
-            if s0 == 0:
-                return pairs1[:, S + S_HALF : S + S_HALF + G]
-            if s0 == C:
-                return second_woven[:]
-            return woven1[:, 2 * s0 : 2 * s1]
+        vector_planes, scalar_planes = pair_planes(0, 0, H), pair_planes(0, H, S)
+        for d in range(PACK):
+            gather(True, 0, d, 0, H, into_planes(vector_planes, d, 0, H))
+            gather(False, 0, d, H, S, into_planes(scalar_planes, d, H, S))
+        low, high = woven_tile(0, 0, H), woven_tile(0, H, S)
+        weave(True, vector_planes, low, 0, H)
+        weave(False, scalar_planes, high, H + G, S)
+        weave(True, scalar_planes, high, H, H + G)
+        quantise(0, low, 0, H)
 
-        gather(3, 0, G)
-        quantise(0, 0, S_HALF, woven0_early[:])
-        gather(3, G, 2 * G)
-        for s0, s1 in ((0, C), (C, G)):
-            weave(1, s0, s1, woven_of(s0, s1))
-            quantise(1, s0, s1, woven_of(s0, s1))
-        weave(1, G, 2 * G, woven_of(G, 2 * G))
-        gather(3, S_HALF, S)
-        quantise(1, G, 2 * G, woven_of(G, 2 * G))
-        weave(1, S_HALF, S, woven_of(S_HALF, S), True)
-        quantise(0, S_HALF, S, woven0_late[:])
-        quantise(1, S_HALF, S, woven_of(S_HALF, S))
-
-        def product(acc, t, e, a, start, stop):
-            nc.tensor.matmul_mx(
-                out=acc,
-                lhsT=w_sb[e, t][:, a, :].bitcast(E2M1X4),
-                lhsT_scale=w_scale_sb[:, PASSES * e + a, t * P : (t + 1) * P],
-                rhs=codes(a, e * C, (e + 1) * C).bitcast(E4M3X4),
-                rhs_scale=scales[a][:, e * C : (e + 1) * C],
-                start=start,
-                stop=stop,
-            )
+        first = woven_tile(1, 0, G)
+        first_values = first[0][:].bitcast(BF16).rearrange("p (s d) -> p s d", d=PACK)
+        vector_planes, scalar_planes = pair_planes(1, G, H + G), pair_planes(1, H + G, S)
+        for d in range(PACK - 1):
+            gather(True, 1, d, G, H + G, into_planes(vector_planes, d, G, H + G))
+            gather(False, 1, d, 0, G, first_values[:, :, d])
+            gather(False, 1, d, H + G, S, into_planes(scalar_planes, d, H + G, S))
+            if d == 0:
+                quantise(0, high, H, S)
+        d = PACK - 1
+        middle, late = woven_tile(1, G, H + G), woven_tile(1, H + G, S)
+        for s0 in (0, C):
+            gather(False, 1, d, s0, s0 + C, first_values[:, s0 : s0 + C, d])
+        gather(True, 1, d, G, H, into_planes(vector_planes, d, G, H))
+        quantise(1, first, 0, C)
+        gather(True, 1, d, H, H + G, into_planes(vector_planes, d, H, H + G))
+        quantise(1, first, C, G)
+        gather(False, 1, d, H + G, S, into_planes(scalar_planes, d, H + G, S))
+        weave(True, vector_planes, middle, G, H + C)
+        weave(False, scalar_planes, late, H + G, S)
+        weave(False, vector_planes, middle, H + C, H + G)
+        quantise(1, late, H + G, S)
+        quantise(1, middle, G, H + G)
 
         def products(t, s0, s1):
             acc = psum.tile([P, s1 - s0], F32, name="acc")
             for e in range(s0 // C, s1 // C):
                 for a in range(PASSES):
-                    product(acc[:, e * C - s0 : (e + 1) * C - s0], t, e, a, a == 0, a == PASSES - 1)
+                    nc.tensor.matmul_mx(
+                        out=acc[:, e * C - s0 : (e + 1) * C - s0],
+                        lhsT=w_sb[e, t][:, a, :].bitcast(E2M1X4),
+                        lhsT_scale=w_scale_sb[:, PASSES * e + a, t * P : (t + 1) * P],
+                        rhs=codes[a][:, e * C : (e + 1) * C].bitcast(E4M3X4),
+                        rhs_scale=scales[a][:, e * C : (e + 1) * C],
+                        start=a == 0,
+                        stop=a == PASSES - 1,
+                    )
             return acc
 
-        first = [psum.tile([P, G], F32, name="acc") for t in range(N_TILES)]
-        for tiles, order in (((0, 1), (0, 1)), ((2, 3), (1, 0))):
-            for a in order:
-                for t in tiles:
-                    for e in range(2):
-                        start, stop = (a, e) == (order[0], 0), (a, e) == (order[1], 1)
-                        product(first[t][:, e * C : (e + 1) * C], t, e, a, start, stop)
+        stages = {0: G, G: H, H: S}
+        units = [(t, s0) for s0 in stages for t in range(N_TILES)]
+        relu_sb = {(t, s0): keep.tile([P, H], F32, name=f"relu{t}_{s0}") for t, s0 in units}
+        factor = {(t, s0): keep.tile([P, H], F32, name=f"factor{t}_{s0}") for t, s0 in units if (t, s0) not in ((2, G), (0, H), (2, H), (3, H))}
+        y_sb = {(t, 0): keep.tile([P, G], F32, name=f"y{t}") for t in (0, 1)}
+        y_sb.update({(3, 0): factor[1, 0], (2, 0): factor[0, 0], (0, G): factor[3, 0]})
+        factor.update({(2, G): factor[2, 0], (0, H): factor[2, 0], (2, H): factor[2, 0], (3, H): relu_sb[2, H]})
+        y_sb.update({(1, G): factor[0, G], (2, G): relu_sb[2, G], (3, G): factor[1, G]})
+        y_sb.update({(0, H): factor[3, G], (1, H): relu_sb[0, H], (2, H): factor[1, H]})
+        banks = {}
 
-        banks = {(t, 0): first[t] for t in range(N_TILES)}
+        def sums(t, s0):
+            banks.update({(t, s0): products(t, s0, stages[s0])})
 
-        def read_out(t, s0, s1, on_vector, last_home=None, acc=None, later_home=None):
-            relu_done = acc is not None
-            if acc is None:
-                acc = banks[t, s0] if (t, s0) in banks else products(t, s0, s1)
-            for e in range(s0 // C, s1 // C):
-                z = acc[:, e * C - s0 : (e + 1) * C - s0]
-                cols = slice(e * C, (e + 1) * C)
-                home = last_home if e == s1 // C - 1 else t
-                if later_home is not None and s0 // C < e < s1 // C - 1:
-                    home = later_home
-                at = T + t * E + e
-                bias = b_sb[:, t, e : e + 1] if home is None else out_sb[home][:, at : at + 1]
+        def bias_of(t, e):
+            if e < 2:
+                return b_sb[:, t, e : e + 1]
+            if e == E - 1 and t >= 2:
+                return out_sb[t - 2][:, T + E : T + E + 1]
+            return out_sb[t][:, T + e : T + e + 1]
+
+        def experts(t, s0):
+            return [(bias_of(t, e), slice(e * C - s0, (e + 1) * C - s0)) for e in range(s0 // C, stages[s0] // C)]
+
+        def relu(on_vector, t, s0):
+            for bias, cols in experts(t, s0):
                 if on_vector:
-                    gated = factor[t, s0][:, e * C - s0 : (e + 1) * C - s0]
-                    if not relu_done:
-                        nc.vector.tensor_scalar(relu_sb[t][:, cols], z, bias, 0.0, ADD, MAX)
-                    nc.vector.scalar_tensor_tensor(gated, z, bias, gate_sb[:, cols], ADD, MULT)
+                    nc.vector.tensor_scalar(relu_sb[t, s0][:, cols], banks[t, s0][:, cols], bias, 0.0, ADD, MAX)
                 else:
-                    nc.scalar.activation(relu_sb[t][:, cols], z, ACT.Relu, bias=bias)
-            return acc
+                    nc.scalar.activation(relu_sb[t, s0][:, cols], banks[t, s0][:, cols], ACT.Relu, bias=bias)
 
-        def square(t, s0, s1):
-            if s0 == G and t in SCALAR_TILES:
-                nc.gpsimd.tensor_tensor(factor[t, s0][:, 0:G], relu_sb[t][:, s0:s1], relu_sb[t][:, s0:s1], MULT)
+        def gated(t, s0):
+            for bias, cols in experts(t, s0):
+                nc.vector.scalar_tensor_tensor(
+                    factor[t, s0][:, cols], banks[t, s0][:, cols], bias, gate_sb[:, s0:S][:, cols], ADD, MULT
+                )
+
+        def square(on_scalar, t, s0):
+            n = stages[s0] - s0
+            if on_scalar:
+                nc.scalar.activation(factor[t, s0][:, 0:n], relu_sb[t, s0][:, 0:n], ACT.Square)
             else:
-                nc.scalar.activation(factor[t, s0][:, 0 : s1 - s0], relu_sb[t][:, s0:s1], ACT.Square)
+                nc.gpsimd.tensor_tensor(factor[t, s0][:, 0:n], relu_sb[t, s0][:, 0:n], relu_sb[t, s0][:, 0:n], MULT)
 
-        def finish(t, s0, s1, on_vector):
-            other = relu_sb[t][:, s0:s1] if on_vector else gate_sb[:, s0:s1]
-            nc.gpsimd.tensor_tensor(y_at[t, s0][:, 0 : s1 - s0], factor[t, s0][:, 0 : s1 - s0], other, MULT)
+        def finish(t, s0, squared):
+            n = stages[s0] - s0
+            other = gate_sb[:, s0 : s0 + n] if squared else relu_sb[t, s0][:, 0:n]
+            nc.gpsimd.tensor_tensor(y_sb[t, s0][:, 0:n], factor[t, s0][:, 0:n], other, MULT)
 
-        def unit(t, s0, s1, on_vector):
-            read_out(t, s0, s1, on_vector)
-            if not on_vector:
-                square(t, s0, s1)
-            finish(t, s0, s1, on_vector)
-
-        def scatter(t, c0, c1, y):
-            window = out_sb[t][:].indirect(dst_sb[:, c0 // LIST : c1 // LIST])
-            if t in SCALAR_TILES:
-                nc.scalar.activation(window, y, ACT.Copy)
+        def scatter(t, s0):
+            s1 = stages[s0]
+            if t % 2 == 1:
+                window = out_sb[t][:].indirect(dst_sb[:, s0 // LIST : s1 // LIST])
+                nc.vector.tensor_copy(window, y_sb[t, s0][:, 0 : s1 - s0])
             else:
-                nc.vector.tensor_copy(window, y)
+                for c0 in range(s0, s1, G):
+                    window = out_sb[t][:].indirect(dst_sb[:, c0 // LIST : (c0 + G) // LIST])
+                    nc.scalar.activation(window, y_sb[t, s0][:, c0 - s0 : c0 - s0 + G], ACT.Copy)
 
         def store(t):
             nc.sync.dma_start(out=out[t * P : (t + 1) * P, :], in_=out_sb[t][:, 0:T])
 
-        for t in range(N_TILES):
-            unit(t, 0, G, False)
-        unit(1, G, S_HALF, False)
-        scatter(1, 0, G, y_at[1, 0][:, 0:G])
-        shared = read_out(3, G, S_HALF, False)
-        unit(0, G, S_HALF, False)
-        scatter(0, 0, G, y_at[0, 0][:, 0:G])
-        read_out(3, G, S_HALF, True, None, shared)
-        finish(3, G, S_HALF, True)
-        scatter(3, 0, G, y_at[3, 0][:, 0:G])
-        read_out(2, G, S_HALF, False)
-        scatter(2, 0, G, y_at[2, 0][:, 0:G])
-        banks[1, S_HALF] = products(1, S_HALF, S)
-        read_out(0, S_HALF, S, False, 0)
-        square(2, G, S_HALF)
-        finish(2, G, S_HALF, False)
-        unit(1, S_HALF, S, True)
-        square(0, S_HALF, S)
-        finish(0, S_HALF, S, False)
+        for t in (1, 0, 3, 2):
+            sums(t, 0)
+        for t in (0, 1, 3, 2):
+            sums(t, G)
         for t in (1, 0):
-            scatter(t, G, S_HALF, y_at[t, G][:, 0:G])
-        read_out(3, S_HALF, S, True, None, None, 1)
-        finish(3, S_HALF, S, True)
-        read_out(2, S_HALF, S, False, 0)
-        square(2, S_HALF, S)
-        scatter(2, G, S_HALF, y_at[2, G][:, 0:G])
-        scatter(1, S_HALF, S, y_at[1, S_HALF])
-        store(1)
-        y0 = y_at[0, S_HALF]
-        scatter(0, 2 * G, 3 * G, y0[:, 0:G])
-        y2 = (y0[:, 0:G], factor[1, S_HALF][:, 0:G])
-        for i in range(2):
-            s0 = S_HALF + i * G
-            nc.gpsimd.tensor_tensor(y2[i], factor[2, S_HALF][:, i * G : (i + 1) * G], gate_sb[:, s0 : s0 + G], MULT)
-        scatter(0, 3 * G, S, y0[:, G:S_HALF])
-        store(0)
-        scatter(3, G, S, late_y[:])
+            relu(False, t, 0)
+            square(True, t, 0)
+            finish(t, 0, True)
+        relu(True, 3, 0)
+        gated(3, 0)
+        finish(3, 0, False)
+        relu(False, 2, 0)
+        square(True, 2, 0)
+        finish(2, 0, True)
+        for t in (0, 1, 2, 3):
+            sums(t, H)
+        relu(False, 0, G)
+        square(True, 0, G)
+        finish(0, G, True)
+        scatter(1, 0)
+        scatter(0, 0)
+        relu(False, 2, G)
+        square(False, 2, G)
+        for t in (1, 3):
+            relu(True, t, G)
+            gated(t, G)
+        finish(1, G, False)
+        finish(2, G, True)
+        finish(3, G, False)
+        scatter(2, 0)
+        scatter(3, 0)
+        relu(False, 0, H)
+        relu(True, 1, H)
+        gated(1, H)
+        square(False, 0, H)
+        finish(0, H, True)
+        finish(1, H, False)
+        scatter(0, G)
+        scatter(1, G)
+        relu(False, 2, H)
+        relu(True, 3, H)
+        square(False, 2, H)
+        finish(2, H, True)
+        square(False, 3, H)
+        scatter(2, G)
+        scatter(3, G)
+        for t in range(N_TILES - 1):
+            scatter(t, H)
+            store(t)
+        window = out_sb[3][:].indirect(dst_sb[:, H // LIST : S // LIST])
+        nc.vector.tensor_tensor(window, factor[3, H][:], gate_sb[:, H:S], MULT)
         store(3)
-        for i in range(2):
-            scatter(2, S_HALF + i * G, S_HALF + (i + 1) * G, y2[i])
-        store(2)

@@ -29,6 +29,11 @@ MAX = mybir.AluOpType.max
 
 G = 2 * C
 H = S // 2
+DIRECT = C + 192
+LATE = DIRECT + G
+RUNS = ((0, 0, H), (0, H, S), (1, LATE, S))
+BEHIND = (((2, 2, 3),), ((2, 4, 5), (3, 7, E)), ((2, 3, 4),), ((3, 2, 3), (3, 4, 5)))
+SPARE = 8
 DMA_ALIGN = 256
 
 
@@ -43,7 +48,7 @@ def tile_moe_two_lin_relu2_kernel(tc, xT, w_words, w_scales, b, gate, offs, dst,
         b_sb = keep.tile([P, N_TILES, E], F32, name="b_sb")
         gate_sb = keep.tile([P, S], F32, name="gate_sb", align_bytes=DMA_ALIGN)
         w_scale_sb = keep.tile([P, E * PASSES, N], U8, name="w_scale_sb", align_bytes=DMA_ALIGN)
-        out_sb = [keep.tile([P, T + E + 1], F32, name=f"out_sb{t}", align_bytes=DMA_ALIGN) for t in range(N_TILES)]
+        out_sb = [keep.tile([P, T + (SPARE if t % 2 else SPARE + C)], F32, name=f"out_sb{t}", align_bytes=DMA_ALIGN) for t in range(N_TILES)]
 
         def load_row(a, d):
             x = keep.tile([P, T], F32, name=f"x{a}_{d}", align_bytes=DMA_ALIGN)
@@ -58,6 +63,8 @@ def tile_moe_two_lin_relu2_kernel(tc, xT, w_words, w_scales, b, gate, offs, dst,
                 if (a, d) not in x_row:
                     x_row.update({(a, d): load_row(a, d)})
 
+        ones = keep.tile([P, 1], F32, name="ones")
+        nc.vector.memset(ones[:], 1.0)
         nc.gpsimd.memset(out_sb[0][:, 0:T], 0.0)
         nc.scalar.activation(out_sb[1][:, 0:T], out_sb[0][:, 0:T], ACT.Square)
         nc.gpsimd.memset(w_scale_sb[:].rearrange("p g n -> p (g n)").bitcast(I32), 0)
@@ -100,11 +107,13 @@ def tile_moe_two_lin_relu2_kernel(tc, xT, w_words, w_scales, b, gate, offs, dst,
         load_weight_scales(4, E, 2, N_TILES)
         w_sb.update(load_weights(4, E, 2, N_TILES))
 
-        for t in (0, 1):
-            nc.gpsimd.tensor_copy(out_sb[t][:, T + 2 : T + E], b_sb[:, t, 2:E])
-        for t in (2, 3):
-            nc.gpsimd.tensor_copy(out_sb[t][:, T + 2 : T + E - 1], b_sb[:, t, 2 : E - 1])
-            nc.gpsimd.tensor_copy(out_sb[t - 2][:, T + E : T + E + 1], b_sb[:, t, E - 1 : E])
+        bias = {(t, e): b_sb[:, t, e : e + 1] for t in range(N_TILES) for e in range(E)}
+        for home, runs in enumerate(BEHIND):
+            at = T
+            for t, e0, e1 in runs:
+                nc.gpsimd.tensor_copy(out_sb[home][:, at : at + e1 - e0], b_sb[:, t, e0:e1])
+                bias.update({(t, e): out_sb[home][:, at + e - e0 : at + e - e0 + 1] for e in range(e0, e1)})
+                at = at + e1 - e0
 
         codes = [keep.tile([P, S], U32, name=f"codes{a}", align_bytes=64) for a in range(PASSES)]
         scales = [keep.tile([P, S], U8, name=f"scales{a}", align_bytes=64) for a in range(PASSES)]
@@ -116,190 +125,192 @@ def tile_moe_two_lin_relu2_kernel(tc, xT, w_words, w_scales, b, gate, offs, dst,
             else:
                 nc.scalar.activation(to, window, ACT.Copy)
 
-        def pair_planes(a, s0, s1):
-            return keep.tile([P, 2, s1 - s0], U32, name=f"pairs{a}_{s0}", align_bytes=64), s0
+        woven_sb = [keep.tile([P, a * G + 2 * S], U32, name=f"woven{a}", align_bytes=64) for a in range(PASSES)]
+        woven = [woven_sb[a][:, a * G : a * G + 2 * S] for a in range(PASSES)]
+        planes = {run: keep.tile([P, 2 * (run[2] - run[1])], U32, name=f"planes{run[0]}_{run[1]}", align_bytes=64) for run in RUNS}
 
-        def into_planes(planes, d, s0, s1):
-            tile, first = planes
-            halves = tile[:].rearrange("p h s -> p (h s)").bitcast(BF16).rearrange("p (h s e) -> p h s e", h=2, e=2)
-            return halves[:, d // 2, s0 - first : s1 - first, d % 2]
+        def planes_of(a, s0, s1):
+            if (a, s0, s1) == (1, DIRECT, LATE):
+                return woven_sb[1][:, 0 : 3 * G].rearrange("p (h s) -> p h s", s=G)[:, 0:3:2, :]
+            run = [run for run in RUNS if run[0] == a and run[1] <= s0 and s1 <= run[2]][0]
+            return planes[run][:].rearrange("p (h s) -> p h s", h=2)[:, :, s0 - run[1] : s1 - run[1]]
 
-        def woven_tile(a, s0, s1):
-            return keep.tile([P, 2 * (s1 - s0)], U32, name=f"woven{a}_{s0}", align_bytes=64), s0
+        def gather_paired(on_vector, a, d, s0, s1):
+            plane = planes_of(a, s0, s1)[:, d // 2, :].bitcast(BF16)
+            gather(on_vector, a, d, s0, s1, plane.rearrange("p (s e) -> p s e", e=2)[:, :, d % 2])
 
-        def weave(on_vector, planes, woven, s0, s1):
-            tile, first = planes
-            low_high = tile[:].rearrange("p h s -> p s h")[:, s0 - first : s1 - first, :]
-            to = woven[0][:, 2 * (s0 - woven[1]) : 2 * (s1 - woven[1])].rearrange("p (s h) -> p s h", h=2)
+        def gather_woven(on_vector, a, d, s0, s1):
+            values = woven[a][:, 2 * s0 : 2 * s1].bitcast(BF16)
+            gather(on_vector, a, d, s0, s1, values.rearrange("p (s d) -> p s d", d=PACK)[:, :, d])
+
+        def weave(on_vector, a, s0, s1):
+            low_high = planes_of(a, s0, s1).rearrange("p h s -> p s h")
+            to = woven[a][:, 2 * s0 : 2 * s1].rearrange("p (s h) -> p s h", h=2)
             if on_vector:
                 nc.vector.tensor_copy(to.bitcast(I32), low_high.bitcast(I32))
             else:
                 nc.scalar.copy(to, low_high)
 
-        def quantise(a, woven, s0, s1):
-            values = woven[0][:, 2 * (s0 - woven[1]) : 2 * (s1 - woven[1])].bitcast(BF16)
+        def quantise(a, s0, s1):
+            values = woven[a][:, 2 * s0 : 2 * s1].bitcast(BF16)
             nc.vector.quantize_mx(out=codes[a][:, s0:s1].bitcast(E4M3X4), scales=scales[a][:, s0:s1], in_=values)
 
-        vector_planes, scalar_planes = pair_planes(0, 0, H), pair_planes(0, H, S)
         for d in range(PACK):
-            gather(True, 0, d, 0, H, into_planes(vector_planes, d, 0, H))
-            gather(False, 0, d, H, S, into_planes(scalar_planes, d, H, S))
-        low, high = woven_tile(0, 0, H), woven_tile(0, H, S)
-        weave(True, vector_planes, low, 0, H)
-        weave(False, scalar_planes, high, H + G, S)
-        weave(True, scalar_planes, high, H, H + G)
-        quantise(0, low, 0, H)
+            gather_paired(True, 0, d, 0, H)
+            gather_paired(False, 0, d, H, S)
+        weave(True, 0, 0, H)
+        weave(False, 0, S - 192, S)
+        weave(True, 0, H, S - 192)
+        quantise(0, 0, H)
 
-        first = woven_tile(1, 0, G)
-        first_values = first[0][:].bitcast(BF16).rearrange("p (s d) -> p s d", d=PACK)
-        vector_planes, scalar_planes = pair_planes(1, G, H + G), pair_planes(1, H + G, S)
-        for d in range(PACK - 1):
-            gather(True, 1, d, G, H + G, into_planes(vector_planes, d, G, H + G))
-            gather(False, 1, d, 0, G, first_values[:, :, d])
-            gather(False, 1, d, H + G, S, into_planes(scalar_planes, d, H + G, S))
-            if d == 0:
-                quantise(0, high, H, S)
-        d = PACK - 1
-        middle, late = woven_tile(1, G, H + G), woven_tile(1, H + G, S)
-        for s0 in (0, C):
-            gather(False, 1, d, s0, s0 + C, first_values[:, s0 : s0 + C, d])
-        gather(True, 1, d, G, H, into_planes(vector_planes, d, G, H))
-        quantise(1, first, 0, C)
-        gather(True, 1, d, H, H + G, into_planes(vector_planes, d, H, H + G))
-        quantise(1, first, C, G)
-        gather(False, 1, d, H + G, S, into_planes(scalar_planes, d, H + G, S))
-        weave(True, vector_planes, middle, G, H + C)
-        weave(False, scalar_planes, late, H + G, S)
-        weave(False, vector_planes, middle, H + C, H + G)
-        quantise(1, late, H + G, S)
-        quantise(1, middle, G, H + G)
+        for d in (0, 1):
+            gather_woven(False, 1, d, 0, DIRECT)
+            gather_paired(True, 1, d, DIRECT, LATE)
+            gather_paired(True, 1, d, LATE, H + G)
+            gather_paired(False, 1, d, H + G, S)
+        quantise(0, H, S)
+        for d in (2, 3):
+            gather_woven(False, 1, d, 0, C)
+            gather_woven(True, 1, d, C, DIRECT)
+            gather_paired(False, 1, d, LATE, S)
+        quantise(1, 0, C)
+        quantise(1, C, G)
+        for d in (2, 3):
+            gather_paired(True, 1, d, DIRECT, LATE)
+        weave(False, 1, H + G, S)
+        weave(True, 1, DIRECT, LATE)
+        weave(True, 1, LATE, H + G)
+        quantise(1, G, H)
+        quantise(1, H, S)
+
+        def product(acc, t, e, a, start, stop):
+            nc.tensor.matmul_mx(
+                out=acc,
+                lhsT=w_sb[e, t][:, a, :].bitcast(E2M1X4),
+                lhsT_scale=w_scale_sb[:, PASSES * e + a, t * P : (t + 1) * P],
+                rhs=codes[a][:, e * C : (e + 1) * C].bitcast(E4M3X4),
+                rhs_scale=scales[a][:, e * C : (e + 1) * C],
+                start=start,
+                stop=stop,
+            )
 
         def products(t, s0, s1):
             acc = psum.tile([P, s1 - s0], F32, name="acc")
             for e in range(s0 // C, s1 // C):
                 for a in range(PASSES):
-                    nc.tensor.matmul_mx(
-                        out=acc[:, e * C - s0 : (e + 1) * C - s0],
-                        lhsT=w_sb[e, t][:, a, :].bitcast(E2M1X4),
-                        lhsT_scale=w_scale_sb[:, PASSES * e + a, t * P : (t + 1) * P],
-                        rhs=codes[a][:, e * C : (e + 1) * C].bitcast(E4M3X4),
-                        rhs_scale=scales[a][:, e * C : (e + 1) * C],
-                        start=a == 0,
-                        stop=a == PASSES - 1,
-                    )
+                    product(acc[:, e * C - s0 : (e + 1) * C - s0], t, e, a, a == 0, a == PASSES - 1)
             return acc
 
         stages = {0: G, G: H, H: S}
-        units = [(t, s0) for s0 in stages for t in range(N_TILES)]
-        relu_sb = {(t, s0): keep.tile([P, H], F32, name=f"relu{t}_{s0}") for t, s0 in units}
-        factor = {(t, s0): keep.tile([P, H], F32, name=f"factor{t}_{s0}") for t, s0 in units if (t, s0) not in ((2, G), (0, H), (2, H), (3, H))}
-        y_sb = {(t, 0): keep.tile([P, G], F32, name=f"y{t}") for t in (0, 1)}
-        y_sb.update({(3, 0): factor[1, 0], (2, 0): factor[0, 0], (0, G): factor[3, 0]})
-        factor.update({(2, G): factor[2, 0], (0, H): factor[2, 0], (2, H): factor[2, 0], (3, H): relu_sb[2, H]})
-        y_sb.update({(1, G): factor[0, G], (2, G): relu_sb[2, G], (3, G): factor[1, G]})
-        y_sb.update({(0, H): factor[3, G], (1, H): relu_sb[0, H], (2, H): factor[1, H]})
+        spare = {name: keep.tile([P, H], F32, name=name) for name in ("relu02", "relu13", "gated13", "squares02")}
+        relu_sb = {(t, 0): keep.tile([P, G], F32, name=f"relu{t}_first")[:] for t in range(N_TILES)}
+        factor = {(t, 0): keep.tile([P, G], F32, name=f"factor{t}_first")[:] for t in (0, 1, 3)}
+        factor.update({(2, 0): spare["squares02"][:, 0:G]})
+        for t in range(N_TILES):
+            half = slice((t // 2) * G, (t // 2 + 1) * G)
+            relu_sb.update({(t, G): spare["relu13" if t % 2 else "relu02"][:, half]})
+            factor.update({(t, G): spare["gated13" if t % 2 else "squares02"][:, half]})
+            relu_sb.update({(t, H): keep.tile([P, H], F32, name=f"relu{t}_last")[:]})
+        y_sb = {(t, 0): keep.tile([P, G], F32, name=f"y{t}")[:] for t in (0, 1)}
+        y_sb.update({(2, 0): factor[1, 0], (3, 0): factor[0, 0]})
+        y_sb.update({(t, G): factor[t - 1, G] if t % 2 else relu_sb[t, G] for t in range(N_TILES)})
+        factor.update({(t, H): keep.tile([P, H], F32, name=f"factor{t}_last")[:] for t in range(N_TILES - 1)})
+        factor.update({(3, H): factor[2, H]})
+        y_sb.update({(0, H): relu_sb[0, H], (1, H): factor[0, H], (2, H): relu_sb[2, H]})
         banks = {}
 
         def sums(t, s0):
             banks.update({(t, s0): products(t, s0, stages[s0])})
 
-        def bias_of(t, e):
-            if e < 2:
-                return b_sb[:, t, e : e + 1]
-            if e == E - 1 and t >= 2:
-                return out_sb[t - 2][:, T + E : T + E + 1]
-            return out_sb[t][:, T + e : T + e + 1]
+        def experts(s0, e0, e1):
+            return [(e, slice(e * C - s0, (e + 1) * C - s0)) for e in range(max(e0, s0 // C), min(e1, stages[s0] // C))]
 
-        def experts(t, s0):
-            return [(bias_of(t, e), slice(e * C - s0, (e + 1) * C - s0)) for e in range(s0 // C, stages[s0] // C)]
-
-        def relu(on_vector, t, s0):
-            for bias, cols in experts(t, s0):
+        def relu(on_vector, t, s0, e0=0, e1=E):
+            for e, cols in experts(s0, e0, e1):
                 if on_vector:
-                    nc.vector.tensor_scalar(relu_sb[t, s0][:, cols], banks[t, s0][:, cols], bias, 0.0, ADD, MAX)
+                    nc.vector.tensor_scalar(relu_sb[t, s0][:, cols], banks[t, s0][:, cols], bias[t, e], 0.0, ADD, MAX)
                 else:
-                    nc.scalar.activation(relu_sb[t, s0][:, cols], banks[t, s0][:, cols], ACT.Relu, bias=bias)
+                    nc.scalar.activation(relu_sb[t, s0][:, cols], banks[t, s0][:, cols], ACT.Relu, bias=bias[t, e])
 
         def gated(t, s0):
-            for bias, cols in experts(t, s0):
+            for e, cols in experts(s0, 0, E):
                 nc.vector.scalar_tensor_tensor(
-                    factor[t, s0][:, cols], banks[t, s0][:, cols], bias, gate_sb[:, s0:S][:, cols], ADD, MULT
+                    factor[t, s0][:, cols], banks[t, s0][:, cols], bias[t, e], gate_sb[:, s0:S][:, cols], ADD, MULT
                 )
 
-        def square(on_scalar, t, s0):
-            n = stages[s0] - s0
-            if on_scalar:
-                nc.scalar.activation(factor[t, s0][:, 0:n], relu_sb[t, s0][:, 0:n], ACT.Square)
-            else:
-                nc.gpsimd.tensor_tensor(factor[t, s0][:, 0:n], relu_sb[t, s0][:, 0:n], relu_sb[t, s0][:, 0:n], MULT)
+        def multiply(to, left, right):
+            nc.gpsimd.tensor_tensor(to, left, right, MULT)
 
-        def finish(t, s0, squared):
-            n = stages[s0] - s0
-            other = gate_sb[:, s0 : s0 + n] if squared else relu_sb[t, s0][:, 0:n]
-            nc.gpsimd.tensor_tensor(y_sb[t, s0][:, 0:n], factor[t, s0][:, 0:n], other, MULT)
-
-        def scatter(t, s0):
-            s1 = stages[s0]
+        def scatter(t, s0, c0, c1):
+            window = out_sb[t][:].indirect(dst_sb[:, c0 // LIST : c1 // LIST])
             if t % 2 == 1:
-                window = out_sb[t][:].indirect(dst_sb[:, s0 // LIST : s1 // LIST])
-                nc.vector.tensor_copy(window, y_sb[t, s0][:, 0 : s1 - s0])
+                nc.vector.tensor_copy(window, y_sb[t, s0][:, c0 - s0 : c1 - s0])
+            elif s0 < H:
+                nc.scalar.activation(window, y_sb[t, s0][:, c0 - s0 : c1 - s0], ACT.Copy)
             else:
-                for c0 in range(s0, s1, G):
-                    window = out_sb[t][:].indirect(dst_sb[:, c0 // LIST : (c0 + G) // LIST])
-                    nc.scalar.activation(window, y_sb[t, s0][:, c0 - s0 : c0 - s0 + G], ACT.Copy)
+                nc.scalar.activation(window, y_sb[t, s0][:, c0 - s0 : c1 - s0], ACT.Copy, scale=ones[:])
 
         def store(t):
             nc.sync.dma_start(out=out[t * P : (t + 1) * P, :], in_=out_sb[t][:, 0:T])
 
-        for t in (1, 0, 3, 2):
-            sums(t, 0)
-        for t in (0, 1, 3, 2):
-            sums(t, G)
         for t in (1, 0):
+            banks.update({(t, 0): psum.tile([P, G], F32, name="acc")})
+        for a, order in ((0, ((1, 0), (1, 1), (0, 0), (0, 1))), (1, ((1, 0), (0, 0), (1, 1), (0, 1)))):
+            for t, e in order:
+                product(banks[t, 0][:, e * C : (e + 1) * C], t, e, a, (a, e) == (0, 0), (a, e) == (1, 1))
+        for t in (2, 3):
+            sums(t, 0)
+        for t in (0, 2, 1, 3):
+            sums(t, G)
+        for t in (1, 0, 2):
             relu(False, t, 0)
-            square(True, t, 0)
-            finish(t, 0, True)
+            nc.scalar.activation(factor[t, 0], relu_sb[t, 0], ACT.Square)
+            multiply(y_sb[t, 0], factor[t, 0], gate_sb[:, 0:G])
         relu(True, 3, 0)
         gated(3, 0)
-        finish(3, 0, False)
-        relu(False, 2, 0)
-        square(True, 2, 0)
-        finish(2, 0, True)
-        for t in (0, 1, 2, 3):
+        multiply(y_sb[3, 0], factor[3, 0], relu_sb[3, 0])
+        for t in range(N_TILES):
             sums(t, H)
-        relu(False, 0, G)
-        square(True, 0, G)
-        finish(0, G, True)
-        scatter(1, 0)
-        scatter(0, 0)
-        relu(False, 2, G)
-        square(False, 2, G)
+        for t in (0, 2):
+            relu(False, t, G)
+        multiply(spare["squares02"][:], spare["relu02"][:], spare["relu02"][:])
+        both = "p (t s) -> p t s"
+        gate_twice = gate_sb[:, G:H].unsqueeze(1).to_broadcast([P, 2, G])
+        multiply(spare["relu02"][:].rearrange(both, t=2), spare["squares02"][:].rearrange(both, t=2), gate_twice)
+        scatter(1, 0, 0, G)
+        scatter(0, 0, 0, G)
         for t in (1, 3):
             relu(True, t, G)
             gated(t, G)
-        finish(1, G, False)
-        finish(2, G, True)
-        finish(3, G, False)
-        scatter(2, 0)
-        scatter(3, 0)
-        relu(False, 0, H)
+        multiply(spare["squares02"][:], spare["gated13"][:], spare["relu13"][:])
+        scatter(2, 0, 0, G)
+        scatter(3, 0, 0, G)
+        relu(False, 0, H, 4, 6)
+        parked = [(out_sb[t][:, T + SPARE : T + SPARE + C], e, slice(e * C - H, (e + 1) * C - H)) for t, e in ((2, 6), (0, 7))]
+        for at, e, cols in parked:
+            nc.scalar.activation(at, banks[0, H][:, cols], ACT.Relu, bias=bias[0, e])
+        nc.scalar.activation(factor[0, H][:, 0:G], relu_sb[0, H][:, 0:G], ACT.Square)
+        for at, e, cols in parked:
+            nc.scalar.activation(factor[0, H][:, cols], at, ACT.Square)
         relu(True, 1, H)
         gated(1, H)
-        square(False, 0, H)
-        finish(0, H, True)
-        finish(1, H, False)
-        scatter(0, G)
-        scatter(1, G)
-        relu(False, 2, H)
+        multiply(y_sb[0, H], factor[0, H], gate_sb[:, H:S])
+        multiply(y_sb[1, H], factor[1, H], relu_sb[1, H])
+        scatter(0, G, G, H)
+        relu(True, 2, H)
+        scatter(1, G, G, H)
         relu(True, 3, H)
-        square(False, 2, H)
-        finish(2, H, True)
-        square(False, 3, H)
-        scatter(2, G)
-        scatter(3, G)
-        for t in range(N_TILES - 1):
-            scatter(t, H)
-            store(t)
+        multiply(factor[2, H], relu_sb[2, H], relu_sb[2, H])
+        multiply(y_sb[2, H], factor[2, H], gate_sb[:, H:S])
+        multiply(factor[3, H], relu_sb[3, H], relu_sb[3, H])
+        scatter(2, G, G, H)
+        scatter(3, G, G, H)
+        scatter(0, H, H, S)
+        store(0)
+        scatter(1, H, H, S)
+        store(1)
+        scatter(2, H, H, S)
+        store(2)
         window = out_sb[3][:].indirect(dst_sb[:, H // LIST : S // LIST])
-        nc.vector.tensor_tensor(window, factor[3, H][:], gate_sb[:, H:S], MULT)
+        nc.vector.tensor_tensor(window, factor[3, H], gate_sb[:, H:S], MULT)
         store(3)

from contextlib import ExitStack

import concourse.mybir as mybir

K, T, E, C, N = 1024, 1536, 8, 128, 512
S = E * C
P = 128
PACK = 4
K_PASS = P * PACK
PASSES = K // K_PASS
N_TILES = N // P
LIST = 16

FLOPS = 2 * K * S * N
BYTES = 4 * K * T + E * PASSES * (P * 2 * N + 16 * N) + 4 * N * E + 4 * S + 2 * 2 * P * (S // 16) + 4 * N * T

F32 = mybir.dt.float32
BF16 = mybir.dt.bfloat16
I32 = mybir.dt.int32
U32 = mybir.dt.uint32
U16 = mybir.dt.uint16
U8 = mybir.dt.uint8
E4M3X4 = mybir.dt.float8_e4m3fn_x4
E2M1X4 = mybir.dt.float4_e2m1fn_x4
ACT = mybir.ActivationFunctionType
MULT = mybir.AluOpType.mult
ADD = mybir.AluOpType.add
MAX = mybir.AluOpType.max

G = 2 * C
H = S // 2
DIRECT = C + 192
LATE = DIRECT + G
RUNS = ((0, 0, H), (0, H, S), (1, LATE, S))
BEHIND = (((2, 2, 3),), ((2, 4, 5), (3, 7, E)), ((2, 3, 4),), ((3, 2, 3), (3, 4, 5)))
SPARE = 8
DMA_ALIGN = 256


def tile_moe_two_lin_relu2_kernel(tc, xT, w_words, w_scales, b, gate, offs, dst, out):
    nc = tc.nc
    with ExitStack() as ctx:
        keep = ctx.enter_context(tc.tile_pool(name="keep", bufs=1))
        psum = ctx.enter_context(tc.psum_pool(name="psum", bufs=8))

        offs_sb = keep.tile([P, S // LIST], U16, name="offs_sb")
        dst_sb = keep.tile([P, S // LIST], U16, name="dst_sb")
        b_sb = keep.tile([P, N_TILES, E], F32, name="b_sb")
        gate_sb = keep.tile([P, S], F32, name="gate_sb", align_bytes=DMA_ALIGN)
        w_scale_sb = keep.tile([P, E * PASSES, N], U8, name="w_scale_sb", align_bytes=DMA_ALIGN)
        out_sb = [keep.tile([P, T + (SPARE if t % 2 else SPARE + C)], F32, name=f"out_sb{t}", align_bytes=DMA_ALIGN) for t in range(N_TILES)]

        def load_row(a, d):
            x = keep.tile([P, T], F32, name=f"x{a}_{d}", align_bytes=DMA_ALIGN)
            rows = xT[a * K_PASS : (a + 1) * K_PASS, :].rearrange("(p d) t -> p d t", d=PACK)
            nc.sync.dma_start(out=x[:], in_=rows[:, d, :])
            return x

        x_row = {(0, 0): load_row(0, 0)}
        nc.sync.dma_start(offs_sb[:], offs)
        for a in range(PASSES):
            for d in range(PACK):
                if (a, d) not in x_row:
                    x_row.update({(a, d): load_row(a, d)})

        ones = keep.tile([P, 1], F32, name="ones")
        nc.vector.memset(ones[:], 1.0)
        nc.gpsimd.memset(out_sb[0][:, 0:T], 0.0)
        nc.scalar.activation(out_sb[1][:, 0:T], out_sb[0][:, 0:T], ACT.Square)
        nc.gpsimd.memset(w_scale_sb[:].rearrange("p g n -> p (g n)").bitcast(I32), 0)
        for t in (2, 3):
            nc.gpsimd.memset(out_sb[t][:, 0:T], 0.0)

        def load_weights(e0, e1, t0, t1):
            words = w_words[e0:e1, :, :, 2 * t0 * P : 2 * t1 * P].rearrange("e a p c -> p (e a) c")
            w = keep.tile([P, (e1 - e0) * PASSES, 2 * (t1 - t0) * P], U8, name=f"w{e0}_{t0}", align_bytes=DMA_ALIGN)
            nc.sync.dma_start(out=w[:].bitcast(I32), in_=words.bitcast(I32))
            return {
                (e, t): w[:, PASSES * (e - e0) : PASSES * (e - e0 + 1), 2 * (t - t0) * P : 2 * (t - t0 + 1) * P]
                for e in range(e0, e1)
                for t in range(t0, t1)
            }

        def load_weight_scales(e0, e1, t0, t1):
            for r in range(4):
                nc.sync.dma_start(
                    out=w_scale_sb[r:P:32, PASSES * e0 : PASSES * e1, t0 * P : t1 * P].bitcast(I32),
                    in_=w_scales[e0:e1, :, r:16:4, t0 * P : t1 * P].rearrange("e a q n -> q (e a) n").bitcast(I32),
                )

        def load_gate(s0, s1):
            nc.sync.dma_start(gate_sb[:, s0:s1], gate[0:P, s0:s1])

        w_sb = {}
        load_weight_scales(0, 2, 0, N_TILES)
        w_sb.update(load_weights(0, 2, 0, 2))
        nc.sync.dma_start(out=b_sb[:], in_=b.rearrange("(t p) e -> p t e", p=P))
        w_sb.update(load_weights(0, 2, 2, N_TILES))
        load_gate(0, G)
        nc.sync.dma_start(dst_sb[:], dst)
        load_weight_scales(2, 4, 0, N_TILES)
        w_sb.update(load_weights(2, 4, 0, N_TILES))
        load_gate(G, H)
        load_weight_scales(4, E, 0, 2)
        w_sb.update(load_weights(4, E, 0, 2))
        load_gate(H, S)
        load_weight_scales(4, E, 2, N_TILES)
        w_sb.update(load_weights(4, E, 2, N_TILES))

        bias = {(t, e): b_sb[:, t, e : e + 1] for t in range(N_TILES) for e in range(E)}
        for home, runs in enumerate(BEHIND):
            at = T
            for t, e0, e1 in runs:
                nc.gpsimd.tensor_copy(out_sb[home][:, at : at + e1 - e0], b_sb[:, t, e0:e1])
                bias.update({(t, e): out_sb[home][:, at + e - e0 : at + e - e0 + 1] for e in range(e0, e1)})
                at = at + e1 - e0

        codes = [keep.tile([P, S], U32, name=f"codes{a}", align_bytes=64) for a in range(PASSES)]
        scales = [keep.tile([P, S], U8, name=f"scales{a}", align_bytes=64) for a in range(PASSES)]

        def gather(on_vector, a, d, s0, s1, to):
            window = x_row[a, d][:].indirect(offs_sb[:, s0 // LIST : s1 // LIST])
            if on_vector:
                nc.vector.tensor_copy(to, window)
            else:
                nc.scalar.activation(to, window, ACT.Copy)

        woven_sb = [keep.tile([P, a * G + 2 * S], U32, name=f"woven{a}", align_bytes=64) for a in range(PASSES)]
        woven = [woven_sb[a][:, a * G : a * G + 2 * S] for a in range(PASSES)]
        planes = {run: keep.tile([P, 2 * (run[2] - run[1])], U32, name=f"planes{run[0]}_{run[1]}", align_bytes=64) for run in RUNS}

        def planes_of(a, s0, s1):
            if (a, s0, s1) == (1, DIRECT, LATE):
                return woven_sb[1][:, 0 : 3 * G].rearrange("p (h s) -> p h s", s=G)[:, 0:3:2, :]
            run = [run for run in RUNS if run[0] == a and run[1] <= s0 and s1 <= run[2]][0]
            return planes[run][:].rearrange("p (h s) -> p h s", h=2)[:, :, s0 - run[1] : s1 - run[1]]

        def gather_paired(on_vector, a, d, s0, s1):
            plane = planes_of(a, s0, s1)[:, d // 2, :].bitcast(BF16)
            gather(on_vector, a, d, s0, s1, plane.rearrange("p (s e) -> p s e", e=2)[:, :, d % 2])

        def gather_woven(on_vector, a, d, s0, s1):
            values = woven[a][:, 2 * s0 : 2 * s1].bitcast(BF16)
            gather(on_vector, a, d, s0, s1, values.rearrange("p (s d) -> p s d", d=PACK)[:, :, d])

        def weave(on_vector, a, s0, s1):
            low_high = planes_of(a, s0, s1).rearrange("p h s -> p s h")
            to = woven[a][:, 2 * s0 : 2 * s1].rearrange("p (s h) -> p s h", h=2)
            if on_vector:
                nc.vector.tensor_copy(to.bitcast(I32), low_high.bitcast(I32))
            else:
                nc.scalar.copy(to, low_high)

        def quantise(a, s0, s1):
            values = woven[a][:, 2 * s0 : 2 * s1].bitcast(BF16)
            nc.vector.quantize_mx(out=codes[a][:, s0:s1].bitcast(E4M3X4), scales=scales[a][:, s0:s1], in_=values)

        for d in range(PACK):
            gather_paired(True, 0, d, 0, H)
            gather_paired(False, 0, d, H, S)
        weave(True, 0, 0, H)
        weave(False, 0, S - 192, S)
        weave(True, 0, H, S - 192)
        quantise(0, 0, H)

        for d in (0, 1):
            gather_woven(False, 1, d, 0, DIRECT)
            gather_paired(True, 1, d, DIRECT, LATE)
            gather_paired(True, 1, d, LATE, H + G)
            gather_paired(False, 1, d, H + G, S)
        quantise(0, H, S)
        for d in (2, 3):
            gather_woven(False, 1, d, 0, C)
            gather_woven(True, 1, d, C, DIRECT)
            gather_paired(False, 1, d, LATE, S)
        quantise(1, 0, C)
        quantise(1, C, G)
        for d in (2, 3):
            gather_paired(True, 1, d, DIRECT, LATE)
        weave(False, 1, H + G, S)
        weave(True, 1, DIRECT, LATE)
        weave(True, 1, LATE, H + G)
        quantise(1, G, H)
        quantise(1, H, S)

        def product(acc, t, e, a, start, stop):
            nc.tensor.matmul_mx(
                out=acc,
                lhsT=w_sb[e, t][:, a, :].bitcast(E2M1X4),
                lhsT_scale=w_scale_sb[:, PASSES * e + a, t * P : (t + 1) * P],
                rhs=codes[a][:, e * C : (e + 1) * C].bitcast(E4M3X4),
                rhs_scale=scales[a][:, e * C : (e + 1) * C],
                start=start,
                stop=stop,
            )

        def products(t, s0, s1):
            acc = psum.tile([P, s1 - s0], F32, name="acc")
            for e in range(s0 // C, s1 // C):
                for a in range(PASSES):
                    product(acc[:, e * C - s0 : (e + 1) * C - s0], t, e, a, a == 0, a == PASSES - 1)
            return acc

        stages = {0: G, G: H, H: S}
        spare = {name: keep.tile([P, H], F32, name=name) for name in ("relu02", "relu13", "gated13", "squares02")}
        relu_sb = {(t, 0): keep.tile([P, G], F32, name=f"relu{t}_first")[:] for t in range(N_TILES)}
        factor = {(t, 0): keep.tile([P, G], F32, name=f"factor{t}_first")[:] for t in (0, 1, 3)}
        factor.update({(2, 0): spare["squares02"][:, 0:G]})
        for t in range(N_TILES):
            half = slice((t // 2) * G, (t // 2 + 1) * G)
            relu_sb.update({(t, G): spare["relu13" if t % 2 else "relu02"][:, half]})
            factor.update({(t, G): spare["gated13" if t % 2 else "squares02"][:, half]})
            relu_sb.update({(t, H): keep.tile([P, H], F32, name=f"relu{t}_last")[:]})
        y_sb = {(t, 0): keep.tile([P, G], F32, name=f"y{t}")[:] for t in (0, 1)}
        y_sb.update({(2, 0): factor[1, 0], (3, 0): factor[0, 0]})
        y_sb.update({(t, G): factor[t - 1, G] if t % 2 else relu_sb[t, G] for t in range(N_TILES)})
        factor.update({(t, H): keep.tile([P, H], F32, name=f"factor{t}_last")[:] for t in range(N_TILES - 1)})
        factor.update({(3, H): factor[2, H]})
        y_sb.update({(0, H): relu_sb[0, H], (1, H): factor[0, H], (2, H): relu_sb[2, H]})
        banks = {}

        def sums(t, s0):
            banks.update({(t, s0): products(t, s0, stages[s0])})

        def experts(s0, e0, e1):
            return [(e, slice(e * C - s0, (e + 1) * C - s0)) for e in range(max(e0, s0 // C), min(e1, stages[s0] // C))]

        def relu(on_vector, t, s0, e0=0, e1=E):
            for e, cols in experts(s0, e0, e1):
                if on_vector:
                    nc.vector.tensor_scalar(relu_sb[t, s0][:, cols], banks[t, s0][:, cols], bias[t, e], 0.0, ADD, MAX)
                else:
                    nc.scalar.activation(relu_sb[t, s0][:, cols], banks[t, s0][:, cols], ACT.Relu, bias=bias[t, e])

        def gated(t, s0):
            for e, cols in experts(s0, 0, E):
                nc.vector.scalar_tensor_tensor(
                    factor[t, s0][:, cols], banks[t, s0][:, cols], bias[t, e], gate_sb[:, s0:S][:, cols], ADD, MULT
                )

        def multiply(to, left, right):
            nc.gpsimd.tensor_tensor(to, left, right, MULT)

        def scatter(t, s0, c0, c1):
            window = out_sb[t][:].indirect(dst_sb[:, c0 // LIST : c1 // LIST])
            if t % 2 == 1:
                nc.vector.tensor_copy(window, y_sb[t, s0][:, c0 - s0 : c1 - s0])
            elif s0 < H:
                nc.scalar.activation(window, y_sb[t, s0][:, c0 - s0 : c1 - s0], ACT.Copy)
            else:
                nc.scalar.activation(window, y_sb[t, s0][:, c0 - s0 : c1 - s0], ACT.Copy, scale=ones[:])

        def store(t):
            nc.sync.dma_start(out=out[t * P : (t + 1) * P, :], in_=out_sb[t][:, 0:T])

        for t in (1, 0):
            banks.update({(t, 0): psum.tile([P, G], F32, name="acc")})
        for a, order in ((0, ((1, 0), (1, 1), (0, 0), (0, 1))), (1, ((1, 0), (0, 0), (1, 1), (0, 1)))):
            for t, e in order:
                product(banks[t, 0][:, e * C : (e + 1) * C], t, e, a, (a, e) == (0, 0), (a, e) == (1, 1))
        for t in (2, 3):
            sums(t, 0)
        for t in (0, 2, 1, 3):
            sums(t, G)
        for t in (1, 0, 2):
            relu(False, t, 0)
            nc.scalar.activation(factor[t, 0], relu_sb[t, 0], ACT.Square)
            multiply(y_sb[t, 0], factor[t, 0], gate_sb[:, 0:G])
        relu(True, 3, 0)
        gated(3, 0)
        multiply(y_sb[3, 0], factor[3, 0], relu_sb[3, 0])
        for t in range(N_TILES):
            sums(t, H)
        for t in (0, 2):
            relu(False, t, G)
        multiply(spare["squares02"][:], spare["relu02"][:], spare["relu02"][:])
        both = "p (t s) -> p t s"
        gate_twice = gate_sb[:, G:H].unsqueeze(1).to_broadcast([P, 2, G])
        multiply(spare["relu02"][:].rearrange(both, t=2), spare["squares02"][:].rearrange(both, t=2), gate_twice)
        scatter(1, 0, 0, G)
        scatter(0, 0, 0, G)
        for t in (1, 3):
            relu(True, t, G)
            gated(t, G)
        multiply(spare["squares02"][:], spare["gated13"][:], spare["relu13"][:])
        scatter(2, 0, 0, G)
        scatter(3, 0, 0, G)
        relu(False, 0, H, 4, 6)
        parked = [(out_sb[t][:, T + SPARE : T + SPARE + C], e, slice(e * C - H, (e + 1) * C - H)) for t, e in ((2, 6), (0, 7))]
        for at, e, cols in parked:
            nc.scalar.activation(at, banks[0, H][:, cols], ACT.Relu, bias=bias[0, e])
        nc.scalar.activation(factor[0, H][:, 0:G], relu_sb[0, H][:, 0:G], ACT.Square)
        for at, e, cols in parked:
            nc.scalar.activation(factor[0, H][:, cols], at, ACT.Square)
        relu(True, 1, H)
        gated(1, H)
        multiply(y_sb[0, H], factor[0, H], gate_sb[:, H:S])
        multiply(y_sb[1, H], factor[1, H], relu_sb[1, H])
        scatter(0, G, G, H)
        relu(True, 2, H)
        scatter(1, G, G, H)
        relu(True, 3, H)
        multiply(factor[2, H], relu_sb[2, H], relu_sb[2, H])
        multiply(y_sb[2, H], factor[2, H], gate_sb[:, H:S])
        multiply(factor[3, H], relu_sb[3, H], relu_sb[3, H])
        scatter(2, G, G, H)
        scatter(3, G, G, H)
        scatter(0, H, H, S)
        store(0)
        scatter(1, H, H, S)
        store(1)
        scatter(2, H, H, S)
        store(2)
        window = out_sb[3][:].indirect(dst_sb[:, H // LIST : S // LIST])
        nc.vector.tensor_tensor(window, factor[3, H], gate_sb[:, H:S], MULT)
        store(3)
